import numpy as np
import ml_dtypes


def mxq(x, axis, fmt="e4m3"):
    dtype, down = {"e4m3": (ml_dtypes.float8_e4m3fn, 7), "e5m2": (ml_dtypes.float8_e5m2, 14)}[fmt]
    v = np.moveaxis(np.asarray(x, np.float32).astype(ml_dtypes.bfloat16).astype(np.float64), axis, -1)
    blocks = v.reshape(v.shape[:-1] + (-1, 32))
    amax = np.abs(blocks).max(-1, keepdims=True)
    byte = np.maximum(np.where(amax > 0, np.frexp(amax)[1] - 1 + 127, 0) - down, 1)
    scale = np.exp2(byte - 127.0)
    codes = (blocks / scale).astype(np.float32).astype(dtype).astype(np.float64)
    return np.moveaxis((codes * scale).reshape(v.shape), -1, axis)


WIDE = False


def mx_kscale(k):
    if not WIDE:
        return np.ones(k)
    levels = np.array([10, -10, 5, -5, 0])
    if k % 512:
        return np.exp2(np.random.permutation(np.resize(levels, k // 32))).repeat(32)
    a = np.empty((k // 512, 16))
    for p in range(k // 512):
        a[p, :8] = np.random.permutation(np.resize(levels, 8))
        for g in range(8):
            far = levels[np.abs(levels - a[p, g]) >= 10]
            a[p, g + 8] = far[np.random.randint(len(far))]
    return np.exp2(a.ravel()).repeat(32)


def f64(x):
    return np.asarray(x).astype(np.float64)


def striped(idx):
    return np.tile(idx.reshape(-1, 16).T, (8, 1)).astype(np.uint16)


def unstriped(offs):
    return offs[:16].T.reshape(-1).astype(np.int64)


E2M1 = np.array([0.0, 0.5, 1.0, 1.5, 2.0, 3.0, 4.0, 6.0, -0.0, -0.5, -1.0, -1.5, -2.0, -3.0, -4.0, -6.0])


def pack_weight(w, fmt):
    k, n = w.shape
    w = f64(np.asarray(w, np.float32).astype(ml_dtypes.bfloat16)).reshape(k // 32, 32, n)
    amax = np.abs(w).max(1)
    if fmt == "e4m3":
        byte = np.frexp(amax)[1] - 1 + 127 - 7
    else:
        mant, ex = np.frexp(amax / 6.0)
        byte = np.where(mant > 0.5, ex, ex - 1) + 127
    byte = np.clip(np.where(amax > 0, byte, 1), 1, 254)
    scaled = (w * np.exp2(127.0 - byte)[:, None, :]).reshape(k, n).astype(np.float32)
    by_word = np.ascontiguousarray(scaled.reshape(k // 512, 128, 4, n).transpose(0, 1, 3, 2))
    if fmt == "e4m3":
        words = by_word.astype(ml_dtypes.float8_e4m3fn).view(np.uint8)
    else:
        c = by_word.astype(ml_dtypes.float4_e2m1fn).view(np.uint8) & 0xF
        words = (c[..., 0::2] | (c[..., 1::2] << 4)).reshape(k // 512, 128, 2 * n)
    return np.ascontiguousarray(words), np.ascontiguousarray(byte.astype(np.uint8).reshape(k // 512, 16, n))


def unpack_weight(words, scales, fmt):
    g, _, n = scales.shape
    words = np.ascontiguousarray(words).reshape(g, 128, n, -1)
    if fmt == "e4m3":
        vals = words.view(ml_dtypes.float8_e4m3fn).astype(np.float64)
    else:
        nib = np.empty((g, 128, n, 4), np.uint8)
        nib[..., 0::2] = words & 0xF
        nib[..., 1::2] = words >> 4
        vals = E2M1[nib]
    vals = vals * np.repeat(np.exp2(scales.astype(np.float64) - 127.0), 8, axis=1)[..., None]
    return vals.transpose(0, 1, 3, 2).reshape(g * 512, n)


def gelu(v):
    return 0.5 * v * (1.0 + np.tanh(np.sqrt(2.0 / np.pi) * (v + 0.044715 * v**3)))


K, T, S, P, H = 1536, 4096, 1024, 512, 1024

def setup_inputs():
    n = np.random.standard_normal
    s = mx_kscale(K)[:, None]
    u = mx_kscale(H)[:, None]
    tab_words, tab_scales = pack_weight(n((K, T)) * s, "e4m3")
    w4_words, w4_scales = pack_weight(1.5 * n((K, H)) / np.sqrt(K) / s, "e2m1")
    w2 = 1.5 * n((H, H)) / np.sqrt(H) / u
    gain = np.random.uniform(0.5, 2.0, H) * u[:, 0]
    blend = np.random.uniform(0.2, 0.8, H)
    return {
        "tab_words": tab_words, "tab_scales": tab_scales,
        "w4_words": w4_words, "w4_scales": w4_scales,
        "w2": w2.astype(np.float32),
        "gain": gain.astype(np.float32),
        "blend": blend.astype(np.float32),
        "offs": striped(np.random.permutation(T)[:S]),
        "pos1": striped(np.random.permutation(S)[:P]),
        "pos2": striped(np.random.permutation(S)[:P]),
    }

def reference(tab_words, tab_scales, w4_words, w4_scales, w2, gain, blend, offs, pos1, pos2):
    v = unpack_weight(tab_words, tab_scales, "e4m3")[:, unstriped(offs)]
    w4 = unpack_weight(w4_words, w4_scales, "e2m1")
    h = w4.T @ v
    up = h[:, unstriped(pos1)]
    x = f64(gain)[:, None] * (1.0 / (1.0 + np.exp(-up)))
    y = mxq(f64(w2), 0, "e4m3").T @ mxq(x, 0, "e4m3")
    b = h[:, unstriped(pos2)]
    return b + f64(blend)[:, None] * (y - b)

@@ -1,0 +1,217 @@
+from contextlib import ExitStack
+
+import concourse.mybir as mybir
+
+K, T, S, E, H = 1536, 4096, 1024, 512, 1024
+FLOPS = 2 * K * H * S + 2 * H * H * E
+
+F32 = mybir.dt.float32
+BF16 = mybir.dt.bfloat16
+I32 = mybir.dt.int32
+U32 = mybir.dt.uint32
+U16 = mybir.dt.uint16
+U8 = mybir.dt.uint8
+FP8X4 = mybir.dt.float8_e4m3fn_x4
+FP4X4 = mybir.dt.float4_e2m1fn_x4
+MULT = mybir.AluOpType.mult
+ADD = mybir.AluOpType.add
+COPY = mybir.ActivationFunctionType.Copy
+SIGMOID = mybir.ActivationFunctionType.Sigmoid
+
+P = 128
+PACK = 4
+KP = P * PACK
+PASSES1 = K // KP
+GROUPS = H // KP
+BANK = 512
+HALVES = S // BANK
+SHIFT_ROWS = 112
+
+
+def tile_list_ring_leak_blend_kernel(
+    tc, tab_words, tab_scales, w4_words, w4_scales, w2, gain, blend, offs, pos1, pos2, out
+):
+    nc = tc.nc
+    with ExitStack() as ctx:
+        lists = ctx.enter_context(tc.tile_pool(name="lists", bufs=1))
+        keep = ctx.enter_context(tc.tile_pool(name="keep", bufs=1))
+        psum = ctx.enter_context(tc.psum_pool(name="psum", bufs=8))
+
+        def held(name, shape, dtype, tag=None):
+            return keep.tile(shape, dtype, name=name, tag=tag or name, align_bytes=64)
+
+        offs_t = lists.tile([P, S // 16], U16, name="offs_t")
+        pos1_t = lists.tile([P, E // 16], U16, name="pos1_t")
+        pos2_t = lists.tile([P, E // 16], U16, name="pos2_t")
+
+        tab_sc = held("tab_sc", [P, T // 4], I32)
+        w4_sc_raw = held("w4_sc_raw", [P, PASSES1, H // 4], I32)
+        v_sc = [held(f"v_sc{a}", [P, S // 4], I32) for a in range(PASSES1)]
+        nc.vector.memset(tab_sc[:], 0)
+        nc.vector.memset(w4_sc_raw[:], 0)
+        for a in range(1, PASSES1):
+            nc.vector.memset(v_sc[a][:], 0)
+
+        tab_w = [held(f"tab_w{a}", [P, T], I32) for a in range(PASSES1)]
+        w4_raw = held("w4_raw", [P, PASSES1, H // 2], I32)
+        gain_t = held("gain_t", [P, GROUPS, PACK], F32)
+        blend_t = held("blend_t", [P, GROUPS, PACK], F32)
+        w2_raw = [[held(f"w2_raw{b}{c}", [P, PACK, KP], F32) for c in range(GROUPS)] for b in range(GROUPS)]
+
+        def load_table(a):
+            nc.sync.dma_start(tab_w[a][:], tab_words[a].rearrange("p t i -> p (t i)").bitcast(I32))
+
+        nc.sync.dma_start(offs_t[:], offs)
+        load_table(0)
+        nc.sync.dma_start(w4_raw[:], w4_words.bitcast(I32).rearrange("a p c -> p a c"))
+        load_table(1)
+        load_table(2)
+        nc.sync.dma_start(pos1_t[:], pos1)
+        nc.sync.dma_start(pos2_t[:], pos2)
+        for c in range(GROUPS):
+            for b in range(GROUPS):
+                nc.sync.dma_start(
+                    w2_raw[b][c][:],
+                    w2[b * KP : (b + 1) * KP, c * KP : (c + 1) * KP].rearrange("(p j) n -> p j n", j=PACK),
+                )
+        nc.scalar.dma_start(gain_t[:], gain.rearrange("(b p t) -> p b t", p=P, t=PACK))
+        nc.scalar.dma_start(blend_t[:], blend.rearrange("(b p t) -> p b t", p=P, t=PACK))
+        for q in range(4):
+            nc.gpsimd.dma_start(
+                tab_sc[32 * q : 32 * q + 4 * PASSES1, :], tab_scales.bitcast(I32)[:, 4 * q : 4 * q + 4, :]
+            )
+        for q in range(4):
+            nc.gpsimd.dma_start(
+                w4_sc_raw[32 * q : 32 * q + 4, :, :],
+                w4_scales.bitcast(I32)[:, 4 * q : 4 * q + 4, :].rearrange("a r c -> r a c"),
+            )
+
+        warm = held("warm", [P, 1], F32)
+        nc.scalar.activation(warm[:], gain_t[:, 0, 0:1], SIGMOID)
+        keep_t = held("keep_t", [P, GROUPS, PACK], F32)
+        nc.vector.tensor_scalar(keep_t[:], blend_t[:], -1.0, 1.0, MULT, ADD)
+
+        nc.vector.tensor_copy(v_sc[0][:].bitcast(U8), tab_sc[:].bitcast(U8).indirect(offs_t[:]))
+        for a in range(1, PASSES1):
+            nc.gpsimd.dma_start(v_sc[a][0:SHIFT_ROWS, :], v_sc[0][4 * a : 4 * a + SHIFT_ROWS, :])
+
+        v_w = [[held(f"v_w{a}{s}", [P, BANK], U32) for s in range(HALVES)] for a in range(PASSES1)]
+
+        def gather_words(a):
+            for s in range(HALVES):
+                cols = slice(s * BANK // 16, (s + 1) * BANK // 16)
+                nc.vector.tensor_copy(v_w[a][s][:], tab_w[a][:].bitcast(U32).indirect(offs_t[:, cols]))
+
+        w4_w = [held(f"w4_w{a}", [P, 2 * H], U8) for a in range(PASSES1)]
+        w4_sc = [held(f"w4_sc{a}", [P, H], U8) for a in range(PASSES1)]
+
+        def order_w4(a):
+            nc.vector.tensor_copy(
+                w4_w[a][:].bitcast(U16).rearrange("p (b t m) -> p b t m", b=GROUPS, t=PACK),
+                w4_raw[:, a, :].bitcast(U16).rearrange("p (b m t) -> p b t m", b=GROUPS, t=PACK),
+            )
+            nc.vector.tensor_copy(
+                w4_sc[a][:].rearrange("p (b t m) -> p b t m", b=GROUPS, t=PACK),
+                w4_sc_raw[:, a, :].bitcast(U8).rearrange("p (b m t) -> p b t m", b=GROUPS, t=PACK),
+            )
+
+        gather_words(0)
+        for a in range(PASSES1):
+            order_w4(a)
+        gather_words(1)
+        gather_words(2)
+
+        def pass1(bank, i, s, a):
+            nc.tensor.matmul_mx(
+                out=bank[:],
+                lhsT=w4_w[a][:, 2 * P * i : 2 * P * (i + 1)].bitcast(FP4X4),
+                lhsT_scale=w4_sc[a][:, P * i : P * (i + 1)],
+                rhs=v_w[a][s][:].bitcast(FP8X4),
+                rhs_scale=v_sc[a][:].bitcast(U8)[:, s * BANK : (s + 1) * BANK],
+                start=(a == 0),
+                stop=(a == PASSES1 - 1),
+            )
+
+        h = [held(f"h{i}", [P, S], F32) for i in range(GROUPS * PACK)]
+
+        def empty(bank, i, s):
+            nc.scalar.copy(h[i][:, s * BANK : (s + 1) * BANK], bank[:])
+
+        first = [[psum.tile([P, BANK], F32, name="bank") for s in range(HALVES)] for i in range(PACK)]
+        for a in range(PASSES1 - 1):
+            for s in range(HALVES):
+                for i in range(PACK):
+                    pass1(first[i][s], i, s, a)
+        for s in range(HALVES):
+            for i in range(PACK):
+                pass1(first[i][s], i, s, PASSES1 - 1)
+        for i in range(PACK):
+            for s in range(HALVES):
+                empty(first[i][s], i, s)
+        for i in range(PACK, GROUPS * PACK):
+            for s in range(HALVES):
+                bank = psum.tile([P, BANK], F32, name="bank")
+                for a in range(PASSES1):
+                    pass1(bank, i, s, a)
+                empty(bank, i, s)
+
+        w2_w = [[held(f"w2_w{b}{c}", [P, KP], U32) for c in range(GROUPS)] for b in range(GROUPS)]
+        w2_sc = [[held(f"w2_sc{b}{c}", [P, KP], U8) for c in range(GROUPS)] for b in range(GROUPS)]
+
+        def quantise_w2(copy, b, c, tag):
+            rounded = held(f"w2_bf{b}{c}", [P, PACK * KP], BF16, tag=tag)
+            copy(
+                rounded[:].rearrange("p (t m j) -> p m j t", t=PACK, j=PACK),
+                w2_raw[b][c][:].rearrange("p j (m t) -> p m j t", t=PACK),
+            )
+            nc.vector.quantize_mx(out=w2_w[b][c][:].bitcast(FP8X4), scales=w2_sc[b][c][:], in_=rounded[:])
+
+        up = [held(f"up{b}", [P, PACK, E], F32) for b in range(GROUPS)]
+        for i in range(GROUPS * PACK):
+            nc.vector.tensor_copy(up[i // PACK][:, i % PACK, :], h[i][:].indirect(pos1_t[:]))
+        quantise_w2(nc.vector.tensor_copy, 0, 0, "tab_w2")
+
+        sig = [held(f"sig{b}", [P, E, PACK], F32) for b in range(GROUPS)]
+        x_bf = [held(f"x_bf{b}", [P, E, PACK], BF16) for b in range(GROUPS)]
+        x_w = [held(f"x_w{b}", [P, E], U32) for b in range(GROUPS)]
+        x_sc = [held(f"x_sc{b}", [P, E], U8) for b in range(GROUPS)]
+        for b in range(GROUPS):
+            nc.scalar.activation(
+                sig[b][:].rearrange("p (c i) t -> p c t i", i=4),
+                up[b][:].rearrange("p t (c i) -> p c t i", i=4),
+                SIGMOID,
+            )
+            nc.vector.tensor_tensor(
+                x_bf[b][:], sig[b][:], gain_t[:, b : b + 1, :].to_broadcast([P, E, PACK]), MULT
+            )
+            nc.vector.quantize_mx(
+                out=x_w[b][:].bitcast(FP8X4), scales=x_sc[b][:], in_=x_bf[b][:].rearrange("p m t -> p (m t)")
+            )
+        quantise_w2(nc.scalar.copy, 1, 0, "up1")
+        quantise_w2(nc.scalar.copy, 0, 1, "w2_raw10")
+        quantise_w2(nc.scalar.copy, 1, 1, "w2_raw01")
+
+        for c in range(GROUPS):
+            own = held(f"own{c}", [P, PACK, E], F32, tag=f"up{c}")
+            kept = held(f"kept{c}", [P, PACK, E], F32, tag=f"tab_w{c}")
+            res = held(f"res{c}", [P, PACK, E], F32)
+            rows = out[c * KP : (c + 1) * KP, :].rearrange("(p t) m -> p t m", t=PACK)
+            for t in range(PACK):
+                nc.vector.tensor_copy(own[:, t, :], h[c * PACK + t][:].indirect(pos2_t[:]))
+                nc.scalar.activation(kept[:, t, :], own[:, t, :], COPY, scale=keep_t[:, c, t : t + 1])
+            for t in range(PACK):
+                bank = psum.tile([P, BANK], F32, name="bank")
+                for b in range(GROUPS):
+                    nc.tensor.matmul_mx(
+                        out=bank[:],
+                        lhsT=w2_w[b][c][:, P * t : P * (t + 1)].bitcast(FP8X4),
+                        lhsT_scale=w2_sc[b][c][:, P * t : P * (t + 1)],
+                        rhs=x_w[b][:].bitcast(FP8X4),
+                        rhs_scale=x_sc[b][:],
+                        start=(b == 0),
+                        stop=(b == GROUPS - 1),
+                    )
+                nc.vector.scalar_tensor_tensor(
+                    res[:, t, :], bank[:], blend_t[:, c, t : t + 1], kept[:, t, :], MULT, ADD
+                )
+                nc.sync.dma_start(rows[:, t, :], res[:, t, :])

@@ -35,6 +35,7 @@ def tile_list_ring_leak_blend_kernel(
     with ExitStack() as ctx:
         lists = ctx.enter_context(tc.tile_pool(name="lists", bufs=1))
         keep = ctx.enter_context(tc.tile_pool(name="keep", bufs=1))
+        early = ctx.enter_context(tc.tile_pool(name="early", bufs=1))
         psum = ctx.enter_context(tc.psum_pool(name="psum", bufs=8))
 
         def held(name, shape, dtype, tag=None):
@@ -44,82 +45,97 @@ def tile_list_ring_leak_blend_kernel(
         pos1_t = lists.tile([P, E // 16], U16, name="pos1_t")
         pos2_t = lists.tile([P, E // 16], U16, name="pos2_t")
 
-        tab_sc = held("tab_sc", [P, T // 4], I32)
+        tab_sc = early.tile([P, T // 4], I32, name="tab_sc", offset=0, align_bytes=64)
         w4_sc_raw = held("w4_sc_raw", [P, PASSES1, H // 4], I32)
-        v_sc = [held(f"v_sc{a}", [P, S // 4], I32) for a in range(PASSES1)]
+        moved_sc = [held(f"v_sc{a}", [P, S // 4], I32) for a in range(1, PASSES1)]
         nc.vector.memset(tab_sc[:], 0)
         nc.vector.memset(w4_sc_raw[:], 0)
-        for a in range(1, PASSES1):
-            nc.vector.memset(v_sc[a][:], 0)
+        for plane in moved_sc:
+            nc.vector.memset(plane[:], 0)
 
-        tab_w = [held(f"tab_w{a}", [P, T], I32) for a in range(PASSES1)]
+        warm = held("warm", [P, 2], F32)
+        nc.vector.memset(warm[:, 0:1], 0.0)
+        nc.scalar.activation(warm[:, 1:2], warm[:, 0:1], SIGMOID)
+
+        tab_w = [held(f"tab_w{a}", [P, T], I32) for a in range(PASSES1 - 1)]
         w4_raw = held("w4_raw", [P, PASSES1, H // 2], I32)
         gain_t = held("gain_t", [P, GROUPS, PACK], F32)
         blend_t = held("blend_t", [P, GROUPS, PACK], F32)
-        w2_raw = [[held(f"w2_raw{b}{c}", [P, PACK, KP], F32) for c in range(GROUPS)] for b in range(GROUPS)]
 
-        def load_table(a):
-            nc.sync.dma_start(tab_w[a][:], tab_words[a].rearrange("p t i -> p (t i)").bitcast(I32))
+        def load_table(a, cols=slice(0, T)):
+            nc.sync.dma_start(tab_w[a][:, cols], tab_words[a].rearrange("p t i -> p (t i)").bitcast(I32)[:, cols])
 
         nc.sync.dma_start(offs_t[:], offs)
-        load_table(0)
-        nc.sync.dma_start(w4_raw[:], w4_words.bitcast(I32).rearrange("a p c -> p a c"))
-        load_table(1)
-        load_table(2)
         nc.sync.dma_start(pos1_t[:], pos1)
-        nc.sync.dma_start(pos2_t[:], pos2)
-        for c in range(GROUPS):
-            for b in range(GROUPS):
-                nc.sync.dma_start(
-                    w2_raw[b][c][:],
-                    w2[b * KP : (b + 1) * KP, c * KP : (c + 1) * KP].rearrange("(p j) n -> p j n", j=PACK),
-                )
-        nc.scalar.dma_start(gain_t[:], gain.rearrange("(b p t) -> p b t", p=P, t=PACK))
-        nc.scalar.dma_start(blend_t[:], blend.rearrange("(b p t) -> p b t", p=P, t=PACK))
+        nc.sync.dma_start(w4_raw[:], w4_words.bitcast(I32).rearrange("a p c -> p a c"))
+        load_table(0, slice(0, T // 2))
         for q in range(4):
-            nc.gpsimd.dma_start(
+            nc.sync.dma_start(
                 tab_sc[32 * q : 32 * q + 4 * PASSES1, :], tab_scales.bitcast(I32)[:, 4 * q : 4 * q + 4, :]
             )
+        load_table(0, slice(T // 2, T))
         for q in range(4):
-            nc.gpsimd.dma_start(
+            nc.sync.dma_start(
                 w4_sc_raw[32 * q : 32 * q + 4, :, :],
                 w4_scales.bitcast(I32)[:, 4 * q : 4 * q + 4, :].rearrange("a r c -> r a c"),
             )
-
-        warm = held("warm", [P, 1], F32)
-        nc.scalar.activation(warm[:], gain_t[:, 0, 0:1], SIGMOID)
-        keep_t = held("keep_t", [P, GROUPS, PACK], F32)
-        nc.vector.tensor_scalar(keep_t[:], blend_t[:], -1.0, 1.0, MULT, ADD)
-
-        nc.vector.tensor_copy(v_sc[0][:].bitcast(U8), tab_sc[:].bitcast(U8).indirect(offs_t[:]))
-        for a in range(1, PASSES1):
-            nc.gpsimd.dma_start(v_sc[a][0:SHIFT_ROWS, :], v_sc[0][4 * a : 4 * a + SHIFT_ROWS, :])
-
-        v_w = [[held(f"v_w{a}{s}", [P, BANK], U32) for s in range(HALVES)] for a in range(PASSES1)]
-
-        def gather_words(a):
-            for s in range(HALVES):
-                cols = slice(s * BANK // 16, (s + 1) * BANK // 16)
-                nc.vector.tensor_copy(v_w[a][s][:], tab_w[a][:].bitcast(U32).indirect(offs_t[:, cols]))
+        load_table(1)
 
         w4_w = [held(f"w4_w{a}", [P, 2 * H], U8) for a in range(PASSES1)]
-        w4_sc = [held(f"w4_sc{a}", [P, H], U8) for a in range(PASSES1)]
-
-        def order_w4(a):
+        for a in range(PASSES1):
             nc.vector.tensor_copy(
                 w4_w[a][:].bitcast(U16).rearrange("p (b t m) -> p b t m", b=GROUPS, t=PACK),
                 w4_raw[:, a, :].bitcast(U16).rearrange("p (b m t) -> p b t m", b=GROUPS, t=PACK),
             )
+
+        picked_sc = held("picked_sc", [P, S // 4], I32)
+        nc.vector.tensor_copy(picked_sc[:].bitcast(U8), tab_sc[:].bitcast(U8).indirect(offs_t[:]))
+        v_sc = [picked_sc] + moved_sc
+        for a in range(1, PASSES1):
+            nc.sync.dma_start(v_sc[a][0:SHIFT_ROWS, :], picked_sc[4 * a : 4 * a + SHIFT_ROWS, :])
+        tab_w.append(early.tile([P, T], I32, name="tab_w2", offset=3072, align_bytes=64))
+        load_table(2)
+        nc.sync.dma_start(pos2_t[:], pos2)
+        nc.sync.dma_start(gain_t[:], gain.rearrange("(b p t) -> p b t", p=P, t=PACK))
+        nc.sync.dma_start(blend_t[:], blend.rearrange("(b p t) -> p b t", p=P, t=PACK))
+
+        v_w = [[None] * HALVES for a in range(PASSES1)]
+
+        def gather_words(a, s, picked):
+            cols = slice(s * BANK // 16, (s + 1) * BANK // 16)
+            nc.vector.tensor_copy(picked[:], tab_w[a][:].bitcast(U32).indirect(offs_t[:, cols]))
+            v_w[a][s] = picked
+
+        w4_sc = [early.tile([P, H], U8, name="w4_sc0", offset=0, align_bytes=64)]
+        w4_sc.extend(held(f"w4_sc{a}", [P, H], U8) for a in range(1, PASSES1))
+
+        def order_w4_scales(a):
             nc.vector.tensor_copy(
                 w4_sc[a][:].rearrange("p (b t m) -> p b t m", b=GROUPS, t=PACK),
                 w4_sc_raw[:, a, :].bitcast(U8).rearrange("p (b m t) -> p b t m", b=GROUPS, t=PACK),
             )
 
-        gather_words(0)
-        for a in range(PASSES1):
-            order_w4(a)
-        gather_words(1)
-        gather_words(2)
+        order_w4_scales(0)
+        gather_words(0, 0, early.tile([P, BANK], U32, name="v_w00", offset=1024, align_bytes=64))
+        gather_words(0, 1, held("v_w01", [P, BANK], U32, tag="w4_raw"))
+        order_w4_scales(1)
+        order_w4_scales(2)
+        gather_words(1, 0, held("v_w10", [P, BANK], U32, tag="w4_sc_raw"))
+        gather_words(1, 1, held("v_w11", [P, BANK], U32))
+        gather_words(2, 0, held("v_w20", [P, BANK], U32))
+        gather_words(2, 1, held("v_w21", [P, BANK], U32))
+
+        w2_cols = [held(f"w2_cols{c}", [P, GROUPS * PACK * KP], F32, tag=f"tab_w{c}") for c in range(GROUPS)]
+        w2_raw = [
+            [w2_cols[c][:, b * PACK * KP : (b + 1) * PACK * KP].rearrange("p (j n) -> p j n", j=PACK) for c in range(GROUPS)]
+            for b in range(GROUPS)
+        ]
+        for c in range(GROUPS):
+            for b in range(GROUPS):
+                nc.sync.dma_start(
+                    w2_raw[b][c],
+                    w2[b * KP : (b + 1) * KP, c * KP : (c + 1) * KP].rearrange("(p j) n -> p j n", j=PACK),
+                )
 
         def pass1(bank, i, s, a):
             nc.tensor.matmul_mx(
@@ -142,11 +158,11 @@ def tile_list_ring_leak_blend_kernel(
             for s in range(HALVES):
                 for i in range(PACK):
                     pass1(first[i][s], i, s, a)
-        for s in range(HALVES):
-            for i in range(PACK):
-                pass1(first[i][s], i, s, PASSES1 - 1)
-        for i in range(PACK):
-            for s in range(HALVES):
+        for i, s in [(0, 0), (1, 0), (0, 1), (1, 1), (2, 0), (2, 1), (3, 0), (3, 1)]:
+            pass1(first[i][s], i, s, PASSES1 - 1)
+            if (i, s) == (0, 1):
+                nc.vector.tensor_copy(h[i][:, s * BANK : (s + 1) * BANK], first[i][s][:])
+            else:
                 empty(first[i][s], i, s)
         for i in range(PACK, GROUPS * PACK):
             for s in range(HALVES):
@@ -155,63 +171,83 @@ def tile_list_ring_leak_blend_kernel(
                     pass1(bank, i, s, a)
                 empty(bank, i, s)
 
-        w2_w = [[held(f"w2_w{b}{c}", [P, KP], U32) for c in range(GROUPS)] for b in range(GROUPS)]
-        w2_sc = [[held(f"w2_sc{b}{c}", [P, KP], U8) for c in range(GROUPS)] for b in range(GROUPS)]
-
-        def quantise_w2(copy, b, c, tag):
-            rounded = held(f"w2_bf{b}{c}", [P, PACK * KP], BF16, tag=tag)
-            copy(
-                rounded[:].rearrange("p (t m j) -> p m j t", t=PACK, j=PACK),
-                w2_raw[b][c][:].rearrange("p j (m t) -> p m j t", t=PACK),
-            )
-            nc.vector.quantize_mx(out=w2_w[b][c][:].bitcast(FP8X4), scales=w2_sc[b][c][:], in_=rounded[:])
+        keep_t = held("keep_t", [P, GROUPS, PACK], F32)
+        nc.gpsimd.tensor_scalar(keep_t[:], blend_t[:], -1.0, 1.0, MULT, ADD)
+        w2_bf = [[held(f"w2_bf{b}{c}", [P, PACK * KP], BF16) for c in range(GROUPS)] for b in range(GROUPS)]
+        for c in range(GROUPS):
+            for b in range(GROUPS):
+                nc.gpsimd.tensor_scalar(
+                    w2_bf[b][c][:].rearrange("p (t m j) -> p m t j", t=PACK, j=PACK),
+                    w2_raw[b][c].rearrange("p j (m t) -> p m t j", t=PACK),
+                    1.0,
+                    0.0,
+                    MULT,
+                    ADD,
+                )
+        w2_codes = held("w2_codes", [P, GROUPS * GROUPS * KP], U32, tag="tab_w1")
+        w2_w = [[w2_codes[:, (c * GROUPS + b) * KP : (c * GROUPS + b + 1) * KP] for c in range(GROUPS)] for b in range(GROUPS)]
 
         up = [held(f"up{b}", [P, PACK, E], F32) for b in range(GROUPS)]
         for i in range(GROUPS * PACK):
             nc.vector.tensor_copy(up[i // PACK][:, i % PACK, :], h[i][:].indirect(pos1_t[:]))
-        quantise_w2(nc.vector.tensor_copy, 0, 0, "tab_w2")
 
-        sig = [held(f"sig{b}", [P, E, PACK], F32) for b in range(GROUPS)]
+        sig = [held(f"sig{b}", [P, PACK, E], F32, tag=("v_w21", "sig1")[b]) for b in range(GROUPS)]
+        x_rows = [held(f"x_rows{b}", [P, PACK, E], BF16) for b in range(GROUPS)]
         x_bf = [held(f"x_bf{b}", [P, E, PACK], BF16) for b in range(GROUPS)]
-        x_w = [held(f"x_w{b}", [P, E], U32) for b in range(GROUPS)]
         x_sc = [held(f"x_sc{b}", [P, E], U8) for b in range(GROUPS)]
         for b in range(GROUPS):
-            nc.scalar.activation(
-                sig[b][:].rearrange("p (c i) t -> p c t i", i=4),
-                up[b][:].rearrange("p t (c i) -> p c t i", i=4),
-                SIGMOID,
+            nc.scalar.activation(sig[b][:], up[b][:], SIGMOID)
+            for t in range(PACK):
+                nc.scalar.activation(x_rows[b][:, t, :], sig[b][:, t, :], COPY, scale=gain_t[:, b, t : t + 1])
+            nc.scalar.copy(
+                x_bf[b][:].rearrange("p (c i) t -> p c t i", i=4),
+                x_rows[b][:].rearrange("p t (c i) -> p c t i", i=4),
             )
-            nc.vector.tensor_tensor(
-                x_bf[b][:], sig[b][:], gain_t[:, b : b + 1, :].to_broadcast([P, E, PACK]), MULT
-            )
-            nc.vector.quantize_mx(
-                out=x_w[b][:].bitcast(FP8X4), scales=x_sc[b][:], in_=x_bf[b][:].rearrange("p m t -> p (m t)")
-            )
-        quantise_w2(nc.scalar.copy, 1, 0, "up1")
-        quantise_w2(nc.scalar.copy, 0, 1, "w2_raw10")
-        quantise_w2(nc.scalar.copy, 1, 1, "w2_raw01")
 
-        for c in range(GROUPS):
-            own = held(f"own{c}", [P, PACK, E], F32, tag=f"up{c}")
-            kept = held(f"kept{c}", [P, PACK, E], F32, tag=f"tab_w{c}")
-            res = held(f"res{c}", [P, PACK, E], F32)
-            rows = out[c * KP : (c + 1) * KP, :].rearrange("(p t) m -> p t m", t=PACK)
+        def pick_own(c, tag):
+            own = held(f"own{c}", [P, PACK, E], F32, tag=tag)
             for t in range(PACK):
                 nc.vector.tensor_copy(own[:, t, :], h[c * PACK + t][:].indirect(pos2_t[:]))
-                nc.scalar.activation(kept[:, t, :], own[:, t, :], COPY, scale=keep_t[:, c, t : t + 1])
-            for t in range(PACK):
-                bank = psum.tile([P, BANK], F32, name="bank")
-                for b in range(GROUPS):
-                    nc.tensor.matmul_mx(
-                        out=bank[:],
-                        lhsT=w2_w[b][c][:, P * t : P * (t + 1)].bitcast(FP8X4),
-                        lhsT_scale=w2_sc[b][c][:, P * t : P * (t + 1)],
-                        rhs=x_w[b][:].bitcast(FP8X4),
-                        rhs_scale=x_sc[b][:],
-                        start=(b == 0),
-                        stop=(b == GROUPS - 1),
-                    )
-                nc.vector.scalar_tensor_tensor(
-                    res[:, t, :], bank[:], blend_t[:, c, t : t + 1], kept[:, t, :], MULT, ADD
+            return own
+
+        def quantise_x(b, tag):
+            codes = held(f"x_w{b}", [P, E], U32, tag=tag)
+            nc.vector.quantize_mx(
+                out=codes[:].bitcast(FP8X4), scales=x_sc[b][:], in_=x_bf[b][:].rearrange("p m t -> p (m t)")
+            )
+            return codes
+
+        own = [pick_own(0, "up0")]
+        w2_planes = held("w2_planes", [P, GROUPS * GROUPS * KP], U8, tag="h3")
+        w2_sc = [[w2_planes[:, (c * GROUPS + b) * KP : (c * GROUPS + b + 1) * KP] for c in range(GROUPS)] for b in range(GROUPS)]
+        for c in range(GROUPS):
+            for b in range(GROUPS):
+                nc.vector.quantize_mx(out=w2_w[b][c].bitcast(FP8X4), scales=w2_sc[b][c], in_=w2_bf[b][c][:])
+        x_w = [quantise_x(0, "w2_bf10")]
+        own.append(pick_own(1, "x_bf0"))
+        kept = held("kept", [P, GROUPS * PACK, E], F32, tag="x_rows1")
+        res = held("res", [P, GROUPS * PACK, E], F32)
+        rows = out.rearrange("(c p t) m -> p c t m", p=P, t=PACK)
+        for i in range(GROUPS * PACK):
+            c, t = divmod(i, PACK)
+            nc.scalar.activation(kept[:, i, :], own[c][:, t, :], COPY, scale=keep_t[:, c, t : t + 1])
+        x_w.append(quantise_x(1, "h7"))
+
+        banks = [psum.tile([P, BANK], F32, name="bank") for i in range(GROUPS * PACK)]
+        for b in range(GROUPS):
+            for i in range(GROUPS * PACK):
+                c, t = divmod(i, PACK)
+                nc.tensor.matmul_mx(
+                    out=banks[i][:],
+                    lhsT=w2_w[b][c][:, P * t : P * (t + 1)].bitcast(FP8X4),
+                    lhsT_scale=w2_sc[b][c][:, P * t : P * (t + 1)],
+                    rhs=x_w[b][:].bitcast(FP8X4),
+                    rhs_scale=x_sc[b][:],
+                    start=(b == 0),
+                    stop=(b == GROUPS - 1),
                 )
-                nc.sync.dma_start(rows[:, t, :], res[:, t, :])
+
+        for i in range(GROUPS * PACK):
+            c, t = divmod(i, PACK)
+            nc.vector.scalar_tensor_tensor(res[:, i, :], banks[i][:], blend_t[:, c, t : t + 1], kept[:, i, :], MULT, ADD)
+            nc.sync.dma_start(rows[:, c, t, :], res[:, i, :])

@@ -23,9 +23,12 @@ PACK = 4
 KP = P * PACK
 PASSES1 = K // KP
 GROUPS = H // KP
+TILES = GROUPS * PACK
 BANK = 512
 HALVES = S // BANK
-SHIFT_ROWS = 112
+QUADS = 4
+KB = 1024
+EARLY_OWN = 2
 
 
 def tile_list_ring_leak_blend_kernel(
@@ -35,31 +38,28 @@ def tile_list_ring_leak_blend_kernel(
     with ExitStack() as ctx:
         lists = ctx.enter_context(tc.tile_pool(name="lists", bufs=1))
         keep = ctx.enter_context(tc.tile_pool(name="keep", bufs=1))
-        early = ctx.enter_context(tc.tile_pool(name="early", bufs=1))
+        laid = ctx.enter_context(tc.tile_pool(name="laid", bufs=1))
         psum = ctx.enter_context(tc.psum_pool(name="psum", bufs=8))
 
-        def held(name, shape, dtype, tag=None):
-            return keep.tile(shape, dtype, name=name, tag=tag or name, align_bytes=64)
+        def held(name, shape, dtype):
+            return keep.tile(shape, dtype, name=name, align_bytes=64)
+
+        def at(kb, name, shape, dtype):
+            return laid.tile(shape, dtype, name=name, offset=kb * KB, align_bytes=64)
 
         offs_t = lists.tile([P, S // 16], U16, name="offs_t")
         pos1_t = lists.tile([P, E // 16], U16, name="pos1_t")
         pos2_t = lists.tile([P, E // 16], U16, name="pos2_t")
 
-        tab_sc = early.tile([P, T // 4], I32, name="tab_sc", offset=0, align_bytes=64)
-        w4_sc_raw = held("w4_sc_raw", [P, PASSES1, H // 4], I32)
-        moved_sc = [held(f"v_sc{a}", [P, S // 4], I32) for a in range(1, PASSES1)]
+        tab_sc = held("tab_sc", [P, T // 4], I32)
+        w4_sc_raw = held("w4_sc_raw", [P, H // 4], I32)
+        planes = held("planes", [P, PASSES1 * (S + H) // 4], I32)
         nc.vector.memset(tab_sc[:], 0)
         nc.vector.memset(w4_sc_raw[:], 0)
-        for plane in moved_sc:
-            nc.vector.memset(plane[:], 0)
+        nc.vector.memset(planes[:], 0)
 
-        warm = held("warm", [P, 2], F32)
-        nc.vector.memset(warm[:, 0:1], 0.0)
-        nc.scalar.activation(warm[:, 1:2], warm[:, 0:1], SIGMOID)
-
-        tab_w = [held(f"tab_w{a}", [P, T], I32) for a in range(PASSES1 - 1)]
-        w4_raw = held("w4_raw", [P, PASSES1, H // 2], I32)
-        gain_t = held("gain_t", [P, GROUPS, PACK], F32)
+        tab_w = [at(16 * a, f"tab_w{a}", [P, T], I32) for a in range(PASSES1 - 1)]
+        w4_raw = at(104, "w4_raw", [P, PASSES1 * H // 2], I32)
         blend_t = held("blend_t", [P, GROUPS, PACK], F32)
 
         def load_table(a, cols=slice(0, T)):
@@ -67,91 +67,81 @@ def tile_list_ring_leak_blend_kernel(
 
         nc.sync.dma_start(offs_t[:], offs)
         nc.sync.dma_start(pos1_t[:], pos1)
-        nc.sync.dma_start(w4_raw[:], w4_words.bitcast(I32).rearrange("a p c -> p a c"))
         load_table(0, slice(0, T // 2))
-        for q in range(4):
-            nc.sync.dma_start(
-                tab_sc[32 * q : 32 * q + 4 * PASSES1, :], tab_scales.bitcast(I32)[:, 4 * q : 4 * q + 4, :]
-            )
+        nc.sync.dma_start(pos2_t[:], pos2)
+        nc.sync.dma_start(blend_t[:], blend.rearrange("(b p t) -> p b t", p=P, t=PACK))
+        nc.sync.dma_start(tab_sc[0 : 6 * 16 : 2, :], tab_scales.bitcast(I32).rearrange("a j c -> j a c"))
+        nc.sync.dma_start(w4_sc_raw[0 : 6 * 16 : 2, :], w4_scales.bitcast(I32).rearrange("a j c -> j a c"))
         load_table(0, slice(T // 2, T))
-        for q in range(4):
-            nc.sync.dma_start(
-                w4_sc_raw[32 * q : 32 * q + 4, :, :],
-                w4_scales.bitcast(I32)[:, 4 * q : 4 * q + 4, :].rearrange("a r c -> r a c"),
-            )
+        nc.sync.dma_start(
+            w4_raw[:].rearrange("p (a c) -> p a c", a=PASSES1), w4_words.bitcast(I32).rearrange("a p c -> p a c")
+        )
         load_table(1)
-
-        w4_w = [held(f"w4_w{a}", [P, 2 * H], U8) for a in range(PASSES1)]
-        for a in range(PASSES1):
-            nc.vector.tensor_copy(
-                w4_w[a][:].bitcast(U16).rearrange("p (b t m) -> p b t m", b=GROUPS, t=PACK),
-                w4_raw[:, a, :].bitcast(U16).rearrange("p (b m t) -> p b t m", b=GROUPS, t=PACK),
-            )
 
         picked_sc = held("picked_sc", [P, S // 4], I32)
         nc.vector.tensor_copy(picked_sc[:].bitcast(U8), tab_sc[:].bitcast(U8).indirect(offs_t[:]))
-        v_sc = [picked_sc] + moved_sc
-        for a in range(1, PASSES1):
-            nc.sync.dma_start(v_sc[a][0:SHIFT_ROWS, :], picked_sc[4 * a : 4 * a + SHIFT_ROWS, :])
-        tab_w.append(early.tile([P, T], I32, name="tab_w2", offset=3072, align_bytes=64))
-        load_table(2)
-        nc.sync.dma_start(pos2_t[:], pos2)
-        nc.sync.dma_start(gain_t[:], gain.rearrange("(b p t) -> p b t", p=P, t=PACK))
-        nc.sync.dma_start(blend_t[:], blend.rearrange("(b p t) -> p b t", p=P, t=PACK))
-
-        v_w = [[None] * HALVES for a in range(PASSES1)]
-
-        def gather_words(a, s, picked):
-            cols = slice(s * BANK // 16, (s + 1) * BANK // 16)
-            nc.vector.tensor_copy(picked[:], tab_w[a][:].bitcast(U32).indirect(offs_t[:, cols]))
-            v_w[a][s] = picked
-
-        w4_sc = [early.tile([P, H], U8, name="w4_sc0", offset=0, align_bytes=64)]
-        w4_sc.extend(held(f"w4_sc{a}", [P, H], U8) for a in range(1, PASSES1))
-
-        def order_w4_scales(a):
-            nc.vector.tensor_copy(
-                w4_sc[a][:].rearrange("p (b t m) -> p b t m", b=GROUPS, t=PACK),
-                w4_sc_raw[:, a, :].bitcast(U8).rearrange("p (b m t) -> p b t m", b=GROUPS, t=PACK),
+        both_sc = held("both_sc", [P, (S + H) // 4], I32)
+        nc.vector.tensor_copy(
+            both_sc[:, S // 4 :].bitcast(U8).rearrange("p (g t m) -> p g t m", t=PACK, m=P),
+            w4_sc_raw[:].bitcast(U8).rearrange("p (g m t) -> p g t m", t=PACK, m=P),
+        )
+        nc.vector.tensor_copy(both_sc[:, 0 : S // 4], picked_sc[:])
+        for q in range(QUADS):
+            (nc.scalar, nc.sync)[q % 2].dma_start(
+                planes[32 * q : 32 * q + 4, :].rearrange("r (a c) -> r a c", a=PASSES1),
+                both_sc[24 * q : 24 * q + 24 : 2, :],
             )
 
-        order_w4_scales(0)
-        gather_words(0, 0, early.tile([P, BANK], U32, name="v_w00", offset=1024, align_bytes=64))
-        gather_words(0, 1, held("v_w01", [P, BANK], U32, tag="w4_raw"))
-        order_w4_scales(1)
-        order_w4_scales(2)
-        gather_words(1, 0, held("v_w10", [P, BANK], U32, tag="w4_sc_raw"))
-        gather_words(1, 1, held("v_w11", [P, BANK], U32))
-        gather_words(2, 0, held("v_w20", [P, BANK], U32))
-        gather_words(2, 1, held("v_w21", [P, BANK], U32))
+        v_w = [[at(48 + 2 * (HALVES * a + s), f"v_w{a}{s}", [P, BANK], U32) for s in range(HALVES)] for a in range(PASSES1)]
 
-        w2_cols = [held(f"w2_cols{c}", [P, GROUPS * PACK * KP], F32, tag=f"tab_w{c}") for c in range(GROUPS)]
-        w2_raw = [
-            [w2_cols[c][:, b * PACK * KP : (b + 1) * PACK * KP].rearrange("p (j n) -> p j n", j=PACK) for c in range(GROUPS)]
-            for b in range(GROUPS)
-        ]
-        for c in range(GROUPS):
-            for b in range(GROUPS):
+        def gather_words(a):
+            for s in range(HALVES):
+                cols = slice(s * BANK // 16, (s + 1) * BANK // 16)
+                nc.vector.tensor_copy(v_w[a][s][:], tab_w[a][:].bitcast(U32).indirect(offs_t[:, cols]))
+
+        gather_words(0)
+        tab_w.append(at(0, "tab_w2", [P, T], I32))
+        load_table(2)
+
+        w4_w = held("w4_w", [P, PASSES1 * 2 * H], U8)
+        nc.vector.tensor_copy(
+            w4_w[:].bitcast(U16).rearrange("p (g t m) -> p g t m", t=PACK, m=P),
+            w4_raw[:].bitcast(U16).rearrange("p (g m t) -> p g t m", t=PACK, m=P),
+        )
+
+        keep_t = held("keep_t", [P, TILES], F32)
+        undo_t = held("undo_t", [P, TILES], F32)
+        nc.scalar.activation(keep_t[:], blend_t[:].rearrange("p b t -> p (b t)"), COPY, scale=-1.0, bias=1.0)
+        nc.vector.reciprocal(undo_t[:], keep_t[:])
+
+        gain_t = at(104, "gain_t", [P, GROUPS, PACK], F32)
+        nc.sync.dma_start(gain_t[:], gain.rearrange("(b p t) -> p b t", p=P, t=PACK))
+        gather_words(1)
+        gather_words(2)
+
+        w2_raw = [[at(16 * (1 - b) + 8 * c, f"w2_raw{b}{c}", [P, PACK, KP], F32) for c in range(GROUPS)] for b in range(GROUPS)]
+        for b in range(GROUPS):
+            for c in range(GROUPS):
                 nc.sync.dma_start(
-                    w2_raw[b][c],
+                    w2_raw[b][c][:],
                     w2[b * KP : (b + 1) * KP, c * KP : (c + 1) * KP].rearrange("(p j) n -> p j n", j=PACK),
                 )
 
         def pass1(bank, i, s, a):
             nc.tensor.matmul_mx(
                 out=bank[:],
-                lhsT=w4_w[a][:, 2 * P * i : 2 * P * (i + 1)].bitcast(FP4X4),
-                lhsT_scale=w4_sc[a][:, P * i : P * (i + 1)],
+                lhsT=w4_w[:, 2 * (a * H + P * i) : 2 * (a * H + P * (i + 1))].bitcast(FP4X4),
+                lhsT_scale=planes[:].bitcast(U8)[:, a * (S + H) + S + P * i : a * (S + H) + S + P * (i + 1)],
                 rhs=v_w[a][s][:].bitcast(FP8X4),
-                rhs_scale=v_sc[a][:].bitcast(U8)[:, s * BANK : (s + 1) * BANK],
+                rhs_scale=planes[:].bitcast(U8)[:, a * (S + H) + s * BANK : a * (S + H) + (s + 1) * BANK],
                 start=(a == 0),
                 stop=(a == PASSES1 - 1),
             )
 
-        h = [held(f"h{i}", [P, S], F32) for i in range(GROUPS * PACK)]
+        h = [held(f"h{i}", [P, S], F32) for i in range(TILES)]
 
         def empty(bank, i, s):
-            nc.scalar.copy(h[i][:, s * BANK : (s + 1) * BANK], bank[:])
+            nc.scalar.activation(h[i][:, s * BANK : (s + 1) * BANK], bank[:], COPY, scale=keep_t[:, i : i + 1])
 
         first = [[psum.tile([P, BANK], F32, name="bank") for s in range(HALVES)] for i in range(PACK)]
         for a in range(PASSES1 - 1):
@@ -160,82 +150,67 @@ def tile_list_ring_leak_blend_kernel(
                     pass1(first[i][s], i, s, a)
         for i, s in [(0, 0), (1, 0), (0, 1), (1, 1), (2, 0), (2, 1), (3, 0), (3, 1)]:
             pass1(first[i][s], i, s, PASSES1 - 1)
-            if (i, s) == (0, 1):
-                nc.vector.tensor_copy(h[i][:, s * BANK : (s + 1) * BANK], first[i][s][:])
-            else:
-                empty(first[i][s], i, s)
-        for i in range(PACK, GROUPS * PACK):
+            empty(first[i][s], i, s)
+        for i in range(PACK, TILES):
             for s in range(HALVES):
                 bank = psum.tile([P, BANK], F32, name="bank")
                 for a in range(PASSES1):
                     pass1(bank, i, s, a)
                 empty(bank, i, s)
 
-        keep_t = held("keep_t", [P, GROUPS, PACK], F32)
-        nc.gpsimd.tensor_scalar(keep_t[:], blend_t[:], -1.0, 1.0, MULT, ADD)
-        w2_bf = [[held(f"w2_bf{b}{c}", [P, PACK * KP], BF16) for c in range(GROUPS)] for b in range(GROUPS)]
-        for c in range(GROUPS):
-            for b in range(GROUPS):
+        w2_bf = [[at(32 + 4 * (GROUPS * b + c), f"w2_bf{b}{c}", [P, PACK * KP], BF16) for c in range(GROUPS)] for b in range(GROUPS)]
+        for b in range(GROUPS):
+            for c in range(GROUPS):
                 nc.gpsimd.tensor_scalar(
                     w2_bf[b][c][:].rearrange("p (t m j) -> p m t j", t=PACK, j=PACK),
-                    w2_raw[b][c].rearrange("p j (m t) -> p m t j", t=PACK),
+                    w2_raw[b][c][:].rearrange("p j (m t) -> p m t j", t=PACK),
                     1.0,
                     0.0,
                     MULT,
                     ADD,
                 )
-        w2_codes = held("w2_codes", [P, GROUPS * GROUPS * KP], U32, tag="tab_w1")
-        w2_w = [[w2_codes[:, (c * GROUPS + b) * KP : (c * GROUPS + b + 1) * KP] for c in range(GROUPS)] for b in range(GROUPS)]
 
-        up = [held(f"up{b}", [P, PACK, E], F32) for b in range(GROUPS)]
-        for i in range(GROUPS * PACK):
-            nc.vector.tensor_copy(up[i // PACK][:, i % PACK, :], h[i][:].indirect(pos1_t[:]))
+        up = [at(80 + 2 * i, f"up{i}", [P, E], F32) for i in range(TILES)]
+        for i in range(TILES):
+            nc.vector.tensor_copy(up[i][:], h[i][:].indirect(pos1_t[:]))
 
-        sig = [held(f"sig{b}", [P, PACK, E], F32, tag=("v_w21", "sig1")[b]) for b in range(GROUPS)]
-        x_rows = [held(f"x_rows{b}", [P, PACK, E], BF16) for b in range(GROUPS)]
-        x_bf = [held(f"x_bf{b}", [P, E, PACK], BF16) for b in range(GROUPS)]
+        sig = at(58, "sig", [P, TILES * E], F32)
+        x_rows = [held(f"x_rows{b}", [P, PACK * E], BF16) for b in range(GROUPS)]
+        x_bf = [at(96 + 4 * b, f"x_bf{b}", [P, E * PACK], BF16) for b in range(GROUPS)]
+        x_w = [held(f"x_w{b}", [P, E], U32) for b in range(GROUPS)]
         x_sc = [held(f"x_sc{b}", [P, E], U8) for b in range(GROUPS)]
-        for b in range(GROUPS):
-            nc.scalar.activation(sig[b][:], up[b][:], SIGMOID)
+
+        def message(b):
             for t in range(PACK):
-                nc.scalar.activation(x_rows[b][:, t, :], sig[b][:, t, :], COPY, scale=gain_t[:, b, t : t + 1])
+                i = b * PACK + t
+                nc.scalar.activation(sig[:, i * E : (i + 1) * E], up[i][:], SIGMOID, scale=undo_t[:, i : i + 1])
+                nc.vector.tensor_scalar_mul(x_rows[b][:, t * E : (t + 1) * E], sig[:, i * E : (i + 1) * E], gain_t[:, b, t : t + 1])
             nc.scalar.copy(
-                x_bf[b][:].rearrange("p (c i) t -> p c t i", i=4),
-                x_rows[b][:].rearrange("p t (c i) -> p c t i", i=4),
+                x_bf[b][:].rearrange("p (c i t) -> p c t i", i=4, t=PACK),
+                x_rows[b][:].rearrange("p (t c i) -> p c t i", i=4, t=PACK),
             )
 
-        def pick_own(c, tag):
-            own = held(f"own{c}", [P, PACK, E], F32, tag=tag)
-            for t in range(PACK):
-                nc.vector.tensor_copy(own[:, t, :], h[c * PACK + t][:].indirect(pos2_t[:]))
-            return own
+        def quantise_x(b):
+            nc.vector.quantize_mx(out=x_w[b][:].bitcast(FP8X4), scales=x_sc[b][:], in_=x_bf[b][:])
 
-        def quantise_x(b, tag):
-            codes = held(f"x_w{b}", [P, E], U32, tag=tag)
-            nc.vector.quantize_mx(
-                out=codes[:].bitcast(FP8X4), scales=x_sc[b][:], in_=x_bf[b][:].rearrange("p m t -> p (m t)")
-            )
-            return codes
-
-        own = [pick_own(0, "up0")]
-        w2_planes = held("w2_planes", [P, GROUPS * GROUPS * KP], U8, tag="h3")
-        w2_sc = [[w2_planes[:, (c * GROUPS + b) * KP : (c * GROUPS + b + 1) * KP] for c in range(GROUPS)] for b in range(GROUPS)]
-        for c in range(GROUPS):
-            for b in range(GROUPS):
-                nc.vector.quantize_mx(out=w2_w[b][c].bitcast(FP8X4), scales=w2_sc[b][c], in_=w2_bf[b][c][:])
-        x_w = [quantise_x(0, "w2_bf10")]
-        own.append(pick_own(1, "x_bf0"))
-        kept = held("kept", [P, GROUPS * PACK, E], F32, tag="x_rows1")
-        res = held("res", [P, GROUPS * PACK, E], F32)
-        rows = out.rearrange("(c p t) m -> p c t m", p=P, t=PACK)
-        for i in range(GROUPS * PACK):
-            c, t = divmod(i, PACK)
-            nc.scalar.activation(kept[:, i, :], own[c][:, t, :], COPY, scale=keep_t[:, c, t : t + 1])
-        x_w.append(quantise_x(1, "h7"))
-
-        banks = [psum.tile([P, BANK], F32, name="bank") for i in range(GROUPS * PACK)]
+        message(0)
+        message(1)
+        w2_codes = at(80, "w2_codes", [P, GROUPS * GROUPS * KP], U32)
+        w2_planes = held("w2_planes", [P, GROUPS * GROUPS * KP], U8)
+        w2_w = [[w2_codes[:, (b * GROUPS + c) * KP : (b * GROUPS + c + 1) * KP] for c in range(GROUPS)] for b in range(GROUPS)]
+        w2_sc = [[w2_planes[:, (b * GROUPS + c) * KP : (b * GROUPS + c + 1) * KP] for c in range(GROUPS)] for b in range(GROUPS)]
         for b in range(GROUPS):
-            for i in range(GROUPS * PACK):
+            for c in range(GROUPS):
+                nc.vector.quantize_mx(out=w2_w[b][c].bitcast(FP8X4), scales=w2_sc[b][c], in_=w2_bf[b][c][:])
+        quantise_x(0)
+        own = [at(58 + 2 * i, f"own{i}", [P, E], F32) for i in range(EARLY_OWN)]
+        for i in range(EARLY_OWN):
+            nc.vector.tensor_copy(own[i][:], h[i][:].indirect(pos2_t[:]))
+        quantise_x(1)
+
+        banks = [psum.tile([P, BANK], F32, name="bank") for i in range(TILES)]
+        for b in range(GROUPS):
+            for i in range(TILES):
                 c, t = divmod(i, PACK)
                 nc.tensor.matmul_mx(
                     out=banks[i][:],
@@ -247,7 +222,14 @@ def tile_list_ring_leak_blend_kernel(
                     stop=(b == GROUPS - 1),
                 )
 
-        for i in range(GROUPS * PACK):
+        rows = out.rearrange("(c p t) m -> p c t m", p=P, t=PACK)
+        for i in range(TILES):
             c, t = divmod(i, PACK)
-            nc.vector.scalar_tensor_tensor(res[:, i, :], banks[i][:], blend_t[:, c, t : t + 1], kept[:, i, :], MULT, ADD)
-            nc.sync.dma_start(rows[:, c, t, :], res[:, i, :])
+            res = held(f"res{i}", [P, E], F32)
+            if i < EARLY_OWN:
+                nc.vector.scalar_tensor_tensor(res[:], banks[i][:], blend_t[:, c, t : t + 1], own[i][:], MULT, ADD)
+            else:
+                share = held(f"share{i}", [P, E], F32)
+                nc.scalar.activation(share[:], banks[i][:], COPY, scale=blend_t[:, c, t : t + 1])
+                nc.vector.tensor_tensor(res[:], h[i][:].indirect(pos2_t[:]), share[:], ADD)
+            nc.sync.dma_start(rows[:, c, t, :], res[:])

@@ -28,6 +28,7 @@ BANK = 512
 HALVES = S // BANK
 QUADS = 4
 KB = 1024
+EARLY_SIG = 3
 EARLY_OWN = 2
 
 
@@ -78,7 +79,7 @@ def tile_list_ring_leak_blend_kernel(
         )
         load_table(1)
 
-        picked_sc = held("picked_sc", [P, S // 4], I32)
+        picked_sc = at(32, "picked_sc", [P, S // 4], I32)
         nc.vector.tensor_copy(picked_sc[:].bitcast(U8), tab_sc[:].bitcast(U8).indirect(offs_t[:]))
         both_sc = held("both_sc", [P, (S + H) // 4], I32)
         nc.vector.tensor_copy(
@@ -99,9 +100,9 @@ def tile_list_ring_leak_blend_kernel(
                 cols = slice(s * BANK // 16, (s + 1) * BANK // 16)
                 nc.vector.tensor_copy(v_w[a][s][:], tab_w[a][:].bitcast(U32).indirect(offs_t[:, cols]))
 
-        gather_words(0)
-        tab_w.append(at(0, "tab_w2", [P, T], I32))
+        tab_w.append(at(32, "tab_w2", [P, T], I32))
         load_table(2)
+        gather_words(0)
 
         w4_w = held("w4_w", [P, PASSES1 * 2 * H], U8)
         nc.vector.tensor_copy(
@@ -109,17 +110,21 @@ def tile_list_ring_leak_blend_kernel(
             w4_raw[:].bitcast(U16).rearrange("p (g m t) -> p g t m", t=PACK, m=P),
         )
 
-        keep_t = held("keep_t", [P, TILES], F32)
+        blend_cols = blend_t[:].rearrange("p b t -> p (b t)")
+        keep_t = [at(60 + 2 * (i - PACK), f"keep{i}", [P, 1], F32) if i >= PACK else held(f"keep{i}", [P, 1], F32) for i in range(TILES)]
+        for i in range(TILES):
+            nc.scalar.activation(keep_t[i][:], blend_cols[:, i : i + 1], COPY, scale=-1.0, bias=1.0)
+        keep_all = held("keep_all", [P, TILES], F32)
         undo_t = held("undo_t", [P, TILES], F32)
-        nc.scalar.activation(keep_t[:], blend_t[:].rearrange("p b t -> p (b t)"), COPY, scale=-1.0, bias=1.0)
-        nc.vector.reciprocal(undo_t[:], keep_t[:])
+        nc.vector.tensor_scalar(keep_all[:], blend_cols, -1.0, 1.0, MULT, ADD)
+        nc.vector.reciprocal(undo_t[:], keep_all[:])
 
         gain_t = at(104, "gain_t", [P, GROUPS, PACK], F32)
         nc.sync.dma_start(gain_t[:], gain.rearrange("(b p t) -> p b t", p=P, t=PACK))
         gather_words(1)
         gather_words(2)
 
-        w2_raw = [[at(16 * (1 - b) + 8 * c, f"w2_raw{b}{c}", [P, PACK, KP], F32) for c in range(GROUPS)] for b in range(GROUPS)]
+        w2_raw = [[at(16 * b + 8 * c, f"w2_raw{b}{c}", [P, PACK, KP], F32) for c in range(GROUPS)] for b in range(GROUPS)]
         for b in range(GROUPS):
             for c in range(GROUPS):
                 nc.sync.dma_start(
@@ -141,7 +146,7 @@ def tile_list_ring_leak_blend_kernel(
         h = [held(f"h{i}", [P, S], F32) for i in range(TILES)]
 
         def empty(bank, i, s):
-            nc.scalar.activation(h[i][:, s * BANK : (s + 1) * BANK], bank[:], COPY, scale=keep_t[:, i : i + 1])
+            nc.scalar.activation(h[i][:, s * BANK : (s + 1) * BANK], bank[:], COPY, scale=keep_t[i][:])
 
         first = [[psum.tile([P, BANK], F32, name="bank") for s in range(HALVES)] for i in range(PACK)]
         for a in range(PASSES1 - 1):
@@ -150,7 +155,10 @@ def tile_list_ring_leak_blend_kernel(
                     pass1(first[i][s], i, s, a)
         for i, s in [(0, 0), (1, 0), (0, 1), (1, 1), (2, 0), (2, 1), (3, 0), (3, 1)]:
             pass1(first[i][s], i, s, PASSES1 - 1)
-            empty(first[i][s], i, s)
+            if (i, s) == (0, 1):
+                nc.vector.tensor_scalar_mul(h[i][:, s * BANK : (s + 1) * BANK], first[i][s][:], keep_t[i][:])
+            else:
+                empty(first[i][s], i, s)
         for i in range(PACK, TILES):
             for s in range(HALVES):
                 bank = psum.tile([P, BANK], F32, name="bank")
@@ -174,20 +182,24 @@ def tile_list_ring_leak_blend_kernel(
         for i in range(TILES):
             nc.vector.tensor_copy(up[i][:], h[i][:].indirect(pos1_t[:]))
 
-        sig = at(58, "sig", [P, TILES * E], F32)
-        x_rows = [held(f"x_rows{b}", [P, PACK * E], BF16) for b in range(GROUPS)]
-        x_bf = [at(96 + 4 * b, f"x_bf{b}", [P, E * PACK], BF16) for b in range(GROUPS)]
+        own = [at(58, "own0", [P, E], F32)]
+        nc.vector.tensor_copy(own[0][:], h[0][:].indirect(pos2_t[:]))
+        sig = [at(60 + 2 * i, f"sig{i}", [P, E], F32) for i in range(EARLY_SIG)]
+        late_sig = at(66, "late_sig", [P, (TILES - EARLY_SIG) * E], F32)
+        sig = [tile[:] for tile in sig] + [late_sig[:, i * E : (i + 1) * E] for i in range(TILES - EARLY_SIG)]
+        x_rows = [at(24 + 4 * b, f"x_rows{b}", [P, PACK * E], BF16) for b in range(GROUPS)]
+        x_bf = [at(94 + 6 * b, f"x_bf{b}", [P, E * PACK], BF16) for b in range(GROUPS)]
         x_w = [held(f"x_w{b}", [P, E], U32) for b in range(GROUPS)]
         x_sc = [held(f"x_sc{b}", [P, E], U8) for b in range(GROUPS)]
 
         def message(b):
             for t in range(PACK):
                 i = b * PACK + t
-                nc.scalar.activation(sig[:, i * E : (i + 1) * E], up[i][:], SIGMOID, scale=undo_t[:, i : i + 1])
-                nc.vector.tensor_scalar_mul(x_rows[b][:, t * E : (t + 1) * E], sig[:, i * E : (i + 1) * E], gain_t[:, b, t : t + 1])
+                nc.scalar.activation(sig[i], up[i][:], SIGMOID, scale=undo_t[:, i : i + 1])
+                nc.vector.tensor_scalar_mul(x_rows[b][:, t * E : (t + 1) * E], sig[i], gain_t[:, b, t : t + 1])
             nc.scalar.copy(
-                x_bf[b][:].rearrange("p (c i t) -> p c t i", i=4, t=PACK),
-                x_rows[b][:].rearrange("p (t c i) -> p c t i", i=4, t=PACK),
+                x_bf[b][:].rearrange("p (m t) -> p m t", t=PACK),
+                x_rows[b][:].rearrange("p (t m) -> p m t", t=PACK),
             )
 
         def quantise_x(b):
@@ -195,32 +207,31 @@ def tile_list_ring_leak_blend_kernel(
 
         message(0)
         message(1)
-        w2_codes = at(80, "w2_codes", [P, GROUPS * GROUPS * KP], U32)
         w2_planes = held("w2_planes", [P, GROUPS * GROUPS * KP], U8)
-        w2_w = [[w2_codes[:, (b * GROUPS + c) * KP : (b * GROUPS + c + 1) * KP] for c in range(GROUPS)] for b in range(GROUPS)]
         w2_sc = [[w2_planes[:, (b * GROUPS + c) * KP : (b * GROUPS + c + 1) * KP] for c in range(GROUPS)] for b in range(GROUPS)]
+        w2_w = []
         for b in range(GROUPS):
+            codes = at((68, 94)[b], f"w2_codes{b}", [P, GROUPS * KP], U32)
+            w2_w.append([codes[:, c * KP : (c + 1) * KP] for c in range(GROUPS)])
             for c in range(GROUPS):
                 nc.vector.quantize_mx(out=w2_w[b][c].bitcast(FP8X4), scales=w2_sc[b][c], in_=w2_bf[b][c][:])
-        quantise_x(0)
-        own = [at(58 + 2 * i, f"own{i}", [P, E], F32) for i in range(EARLY_OWN)]
-        for i in range(EARLY_OWN):
-            nc.vector.tensor_copy(own[i][:], h[i][:].indirect(pos2_t[:]))
-        quantise_x(1)
+            quantise_x(b)
+        own.append(at(100, "own1", [P, E], F32))
+        nc.vector.tensor_copy(own[1][:], h[1][:].indirect(pos2_t[:]))
 
         banks = [psum.tile([P, BANK], F32, name="bank") for i in range(TILES)]
         for b in range(GROUPS):
-            for i in range(TILES):
-                c, t = divmod(i, PACK)
-                nc.tensor.matmul_mx(
-                    out=banks[i][:],
-                    lhsT=w2_w[b][c][:, P * t : P * (t + 1)].bitcast(FP8X4),
-                    lhsT_scale=w2_sc[b][c][:, P * t : P * (t + 1)],
-                    rhs=x_w[b][:].bitcast(FP8X4),
-                    rhs_scale=x_sc[b][:],
-                    start=(b == 0),
-                    stop=(b == GROUPS - 1),
-                )
+            for c in range(GROUPS):
+                for t in range(PACK):
+                    nc.tensor.matmul_mx(
+                        out=banks[c * PACK + t][:],
+                        lhsT=w2_w[b][c][:, P * t : P * (t + 1)].bitcast(FP8X4),
+                        lhsT_scale=w2_sc[b][c][:, P * t : P * (t + 1)],
+                        rhs=x_w[b][:].bitcast(FP8X4),
+                        rhs_scale=x_sc[b][:],
+                        start=(b == 0),
+                        stop=(b == GROUPS - 1),
+                    )
 
         rows = out.rearrange("(c p t) m -> p c t m", p=P, t=PACK)
         for i in range(TILES):

@@ -27,6 +27,8 @@ TILES = GROUPS * PACK
 BANK = 512
 HALVES = S // BANK
 QUADS = 4
+RUN = 2 * PACK
+PAIRS = P // 2
 KB = 1024
 EARLY_SIG = 3
 EARLY_OWN = 2
@@ -61,7 +63,12 @@ def tile_list_ring_leak_blend_kernel(
 
         tab_w = [at(16 * a, f"tab_w{a}", [P, T], I32) for a in range(PASSES1 - 1)]
         w4_raw = at(104, "w4_raw", [P, PASSES1 * H // 2], I32)
-        blend_t = held("blend_t", [P, GROUPS, PACK], F32)
+        blend_t = held("blend_t", [P, GROUPS, RUN], F32)
+
+        def load_factors(tile, factors):
+            runs = factors.rearrange("(b v k) -> v b k", b=GROUPS, k=RUN)
+            for e in range(2):
+                nc.sync.dma_start(tile[e:P:2, :, 0 : RUN - 1], runs[:, :, e : e + RUN - 1])
 
         def load_table(a, cols=slice(0, T)):
             nc.sync.dma_start(tab_w[a][:, cols], tab_words[a].rearrange("p t i -> p (t i)").bitcast(I32)[:, cols])
@@ -70,7 +77,7 @@ def tile_list_ring_leak_blend_kernel(
         nc.sync.dma_start(pos1_t[:], pos1)
         load_table(0, slice(0, T // 2))
         nc.sync.dma_start(pos2_t[:], pos2)
-        nc.sync.dma_start(blend_t[:], blend.rearrange("(b p t) -> p b t", p=P, t=PACK))
+        load_factors(blend_t, blend)
         nc.sync.dma_start(tab_sc[0 : 6 * 16 : 2, :], tab_scales.bitcast(I32).rearrange("a j c -> j a c"))
         nc.sync.dma_start(w4_sc_raw[0 : 6 * 16 : 2, :], w4_scales.bitcast(I32).rearrange("a j c -> j a c"))
         load_table(0, slice(T // 2, T))
@@ -83,8 +90,8 @@ def tile_list_ring_leak_blend_kernel(
         nc.vector.tensor_copy(picked_sc[:].bitcast(U8), tab_sc[:].bitcast(U8).indirect(offs_t[:]))
         both_sc = held("both_sc", [P, (S + H) // 4], I32)
         nc.vector.tensor_copy(
-            both_sc[:, S // 4 :].bitcast(U8).rearrange("p (g t m) -> p g t m", t=PACK, m=P),
-            w4_sc_raw[:].bitcast(U8).rearrange("p (g m t) -> p g t m", t=PACK, m=P),
+            both_sc[:, S // 4 :].bitcast(U16).rearrange("p (g t v) -> p g t v", t=PACK, v=PAIRS),
+            w4_sc_raw[:].bitcast(U16).rearrange("p (g v t) -> p g t v", t=PACK, v=PAIRS),
         )
         nc.vector.tensor_copy(both_sc[:, 0 : S // 4], picked_sc[:])
         for q in range(QUADS):
@@ -106,31 +113,29 @@ def tile_list_ring_leak_blend_kernel(
 
         w4_w = held("w4_w", [P, PASSES1 * 2 * H], U8)
         nc.vector.tensor_copy(
-            w4_w[:].bitcast(U16).rearrange("p (g t m) -> p g t m", t=PACK, m=P),
-            w4_raw[:].bitcast(U16).rearrange("p (g m t) -> p g t m", t=PACK, m=P),
+            w4_w[:].bitcast(I32).rearrange("p (g t v) -> p g t v", t=PACK, v=PAIRS),
+            w4_raw[:].rearrange("p (g v t) -> p g t v", t=PACK, v=PAIRS),
         )
 
-        blend_cols = blend_t[:].rearrange("p b t -> p (b t)")
         keep_t = [at(60 + 2 * (i - PACK), f"keep{i}", [P, 1], F32) if i >= PACK else held(f"keep{i}", [P, 1], F32) for i in range(TILES)]
         for i in range(TILES):
-            nc.scalar.activation(keep_t[i][:], blend_cols[:, i : i + 1], COPY, scale=-1.0, bias=1.0)
+            nc.scalar.activation(keep_t[i][:], blend_t[:, i // PACK, 2 * (i % PACK) : 2 * (i % PACK) + 1], COPY, scale=-1.0, bias=1.0)
         keep_all = held("keep_all", [P, TILES], F32)
         undo_t = held("undo_t", [P, TILES], F32)
-        nc.vector.tensor_scalar(keep_all[:], blend_cols, -1.0, 1.0, MULT, ADD)
+        nc.vector.tensor_scalar(keep_all[:].rearrange("p (b t) -> p b t", b=GROUPS), blend_t[:, :, 0 : RUN - 1 : 2], -1.0, 1.0, MULT, ADD)
         nc.vector.reciprocal(undo_t[:], keep_all[:])
 
-        gain_t = at(104, "gain_t", [P, GROUPS, PACK], F32)
-        nc.sync.dma_start(gain_t[:], gain.rearrange("(b p t) -> p b t", p=P, t=PACK))
+        gain_t = at(104, "gain_t", [P, GROUPS, RUN], F32)
+        load_factors(gain_t, gain)
         gather_words(1)
         gather_words(2)
 
         w2_raw = [[at(16 * b + 8 * c, f"w2_raw{b}{c}", [P, PACK, KP], F32) for c in range(GROUPS)] for b in range(GROUPS)]
         for b in range(GROUPS):
             for c in range(GROUPS):
-                nc.sync.dma_start(
-                    w2_raw[b][c][:],
-                    w2[b * KP : (b + 1) * KP, c * KP : (c + 1) * KP].rearrange("(p j) n -> p j n", j=PACK),
-                )
+                block = w2[b * KP : (b + 1) * KP, c * KP : (c + 1) * KP].rearrange("(v j e) n -> e v j n", j=PACK, e=2)
+                for e in range(2):
+                    nc.sync.dma_start(w2_raw[b][c][e:P:2], block[e])
 
         def pass1(bank, i, s, a):
             nc.tensor.matmul_mx(
@@ -170,8 +175,8 @@ def tile_list_ring_leak_blend_kernel(
         for b in range(GROUPS):
             for c in range(GROUPS):
                 nc.gpsimd.tensor_scalar(
-                    w2_bf[b][c][:].rearrange("p (t m j) -> p m t j", t=PACK, j=PACK),
-                    w2_raw[b][c][:].rearrange("p j (m t) -> p m t j", t=PACK),
+                    w2_bf[b][c][:].rearrange("p (t v e j) -> p v t e j", t=PACK, e=2, j=PACK),
+                    w2_raw[b][c][:].rearrange("p j (v t e) -> p v t e j", t=PACK, e=2),
                     1.0,
                     0.0,
                     MULT,
@@ -196,7 +201,7 @@ def tile_list_ring_leak_blend_kernel(
             for t in range(PACK):
                 i = b * PACK + t
                 nc.scalar.activation(sig[i], up[i][:], SIGMOID, scale=undo_t[:, i : i + 1])
-                nc.vector.tensor_scalar_mul(x_rows[b][:, t * E : (t + 1) * E], sig[i], gain_t[:, b, t : t + 1])
+                nc.vector.tensor_scalar_mul(x_rows[b][:, t * E : (t + 1) * E], sig[i], gain_t[:, b, 2 * t : 2 * t + 1])
             nc.scalar.copy(
                 x_bf[b][:].rearrange("p (m t) -> p m t", t=PACK),
                 x_rows[b][:].rearrange("p (t m) -> p m t", t=PACK),
@@ -233,14 +238,14 @@ def tile_list_ring_leak_blend_kernel(
                         stop=(b == GROUPS - 1),
                     )
 
-        rows = out.rearrange("(c p t) m -> p c t m", p=P, t=PACK)
+        rows = out.rearrange("(c v t e) m -> c t v e m", v=PAIRS, t=PACK, e=2)
         for i in range(TILES):
             c, t = divmod(i, PACK)
             res = held(f"res{i}", [P, E], F32)
             if i < EARLY_OWN:
-                nc.vector.scalar_tensor_tensor(res[:], banks[i][:], blend_t[:, c, t : t + 1], own[i][:], MULT, ADD)
+                nc.vector.scalar_tensor_tensor(res[:], banks[i][:], blend_t[:, c, 2 * t : 2 * t + 1], own[i][:], MULT, ADD)
             else:
                 share = held(f"share{i}", [P, E], F32)
-                nc.scalar.activation(share[:], banks[i][:], COPY, scale=blend_t[:, c, t : t + 1])
+                nc.scalar.activation(share[:], banks[i][:], COPY, scale=blend_t[:, c, 2 * t : 2 * t + 1])
                 nc.vector.tensor_tensor(res[:], h[i][:].indirect(pos2_t[:]), share[:], ADD)
-            nc.sync.dma_start(rows[:, c, t, :], res[:])
+            nc.sync.dma_start(rows[c, t], res[:])

@@ -31,7 +31,7 @@ RUN = 2 * PACK
 PAIRS = P // 2
 KB = 1024
 EARLY_SIG = 3
-EARLY_OWN = 2
+EARLY_OWN = 4
 
 
 def tile_list_ring_leak_blend_kernel(
@@ -54,16 +54,22 @@ def tile_list_ring_leak_blend_kernel(
         pos1_t = lists.tile([P, E // 16], U16, name="pos1_t")
         pos2_t = lists.tile([P, E // 16], U16, name="pos2_t")
 
-        tab_sc = held("tab_sc", [P, T // 4], I32)
+        tab_sc = at(76, "tab_sc", [P, T // 4], I32)
         w4_sc_raw = held("w4_sc_raw", [P, H // 4], I32)
-        planes = held("planes", [P, PASSES1 * (S + H) // 4], I32)
+        early_planes = held("early_planes", [P, 2 * (S + H) // 4], I32)
         nc.vector.memset(tab_sc[:], 0)
         nc.vector.memset(w4_sc_raw[:], 0)
-        nc.vector.memset(planes[:], 0)
+        nc.vector.memset(early_planes[:], 0)
 
         tab_w = [at(16 * a, f"tab_w{a}", [P, T], I32) for a in range(PASSES1 - 1)]
-        w4_raw = at(104, "w4_raw", [P, PASSES1 * H // 2], I32)
-        blend_t = held("blend_t", [P, GROUPS, RUN], F32)
+        w4_raw = [at(104, "w4_raw0", [P, PASSES1 * KP // 2], I32)]
+
+        def load_w4(b):
+            nc.sync.dma_start(
+                w4_raw[b][:].rearrange("p (a c) -> p a c", a=PASSES1),
+                w4_words.bitcast(I32)[:, :, b * KP // 2 : (b + 1) * KP // 2].rearrange("a p c -> p a c"),
+            )
+
 
         def load_factors(tile, factors):
             runs = factors.rearrange("(b v k) -> v b k", b=GROUPS, k=RUN)
@@ -77,27 +83,27 @@ def tile_list_ring_leak_blend_kernel(
         nc.sync.dma_start(pos1_t[:], pos1)
         load_table(0, slice(0, T // 2))
         nc.sync.dma_start(pos2_t[:], pos2)
-        load_factors(blend_t, blend)
-        nc.sync.dma_start(tab_sc[0 : 6 * 16 : 2, :], tab_scales.bitcast(I32).rearrange("a j c -> j a c"))
-        nc.sync.dma_start(w4_sc_raw[0 : 6 * 16 : 2, :], w4_scales.bitcast(I32).rearrange("a j c -> j a c"))
+        for tile, scales in ((tab_sc, tab_scales), (w4_sc_raw, w4_scales)):
+            nc.sync.dma_start(tile[4:68:2, :], scales.bitcast(I32)[0:2].rearrange("a j c -> j a c"))
+            nc.sync.dma_start(tile[5:P:8, :], scales.bitcast(I32)[2])
         load_table(0, slice(T // 2, T))
-        nc.sync.dma_start(
-            w4_raw[:].rearrange("p (a c) -> p a c", a=PASSES1), w4_words.bitcast(I32).rearrange("a p c -> p a c")
-        )
+        load_w4(0)
         load_table(1)
 
         picked_sc = at(32, "picked_sc", [P, S // 4], I32)
         nc.vector.tensor_copy(picked_sc[:].bitcast(U8), tab_sc[:].bitcast(U8).indirect(offs_t[:]))
-        both_sc = held("both_sc", [P, (S + H) // 4], I32)
+        both_sc = at(44, "both_sc", [P, (S + H) // 4], I32)
         nc.vector.tensor_copy(
             both_sc[:, S // 4 :].bitcast(U16).rearrange("p (g t v) -> p g t v", t=PACK, v=PAIRS),
             w4_sc_raw[:].bitcast(U16).rearrange("p (g v t) -> p g t v", t=PACK, v=PAIRS),
         )
         nc.vector.tensor_copy(both_sc[:, 0 : S // 4], picked_sc[:])
+        blend_t = at(76, "blend_t", [P, GROUPS, RUN], F32)
+        load_factors(blend_t, blend)
         for q in range(QUADS):
-            (nc.scalar, nc.sync)[q % 2].dma_start(
-                planes[32 * q : 32 * q + 4, :].rearrange("r (a c) -> r a c", a=PASSES1),
-                both_sc[24 * q : 24 * q + 24 : 2, :],
+            nc.scalar.dma_start(
+                early_planes[32 * q : 32 * q + 4, :].rearrange("r (a c) -> r a c", a=2),
+                both_sc[4 + 16 * q : 4 + 16 * (q + 1) : 2, :],
             )
 
         v_w = [[at(48 + 2 * (HALVES * a + s), f"v_w{a}{s}", [P, BANK], U32) for s in range(HALVES)] for a in range(PASSES1)]
@@ -107,16 +113,27 @@ def tile_list_ring_leak_blend_kernel(
                 cols = slice(s * BANK // 16, (s + 1) * BANK // 16)
                 nc.vector.tensor_copy(v_w[a][s][:], tab_w[a][:].bitcast(U32).indirect(offs_t[:, cols]))
 
-        tab_w.append(at(32, "tab_w2", [P, T], I32))
-        load_table(2)
         gather_words(0)
+        tab_w.append(at(0, "tab_w2", [P, T], I32))
+        load_table(2)
+        w4_w = [held(f"w4_w{b}", [P, PASSES1 * 2 * KP], U8) for b in range(GROUPS)]
 
-        w4_w = held("w4_w", [P, PASSES1 * 2 * H], U8)
-        nc.vector.tensor_copy(
-            w4_w[:].bitcast(I32).rearrange("p (g t v) -> p g t v", t=PACK, v=PAIRS),
-            w4_raw[:].rearrange("p (g v t) -> p g t v", t=PACK, v=PAIRS),
-        )
+        def order_w4(b):
+            nc.vector.tensor_copy(
+                w4_w[b][:].bitcast(I32).rearrange("p (t c i) -> p c t i", t=PACK, i=4),
+                w4_raw[b][:].rearrange("p (c i t) -> p c t i", t=PACK, i=4),
+            )
 
+        order_w4(0)
+        last_plane = at(104, "last_plane", [P, (S + H) // 4], I32)
+        nc.vector.memset(last_plane[:], 0)
+        for q in range(QUADS):
+            nc.sync.dma_start(last_plane[32 * q : 32 * q + 4, :], both_sc[5 + 32 * q : 32 * (q + 1) : 8, :])
+        planes = [early_planes[:].bitcast(U8)[:, a * (S + H) : (a + 1) * (S + H)] for a in range(2)]
+        planes.append(last_plane[:].bitcast(U8))
+
+        w4_raw.append(at(106, "w4_raw1", [P, PASSES1 * KP // 2], I32))
+        load_w4(1)
         keep_t = [at(60 + 2 * (i - PACK), f"keep{i}", [P, 1], F32) if i >= PACK else held(f"keep{i}", [P, 1], F32) for i in range(TILES)]
         for i in range(TILES):
             nc.scalar.activation(keep_t[i][:], blend_t[:, i // PACK, 2 * (i % PACK) : 2 * (i % PACK) + 1], COPY, scale=-1.0, bias=1.0)
@@ -125,25 +142,27 @@ def tile_list_ring_leak_blend_kernel(
         nc.vector.tensor_scalar(keep_all[:].rearrange("p (b t) -> p b t", b=GROUPS), blend_t[:, :, 0 : RUN - 1 : 2], -1.0, 1.0, MULT, ADD)
         nc.vector.reciprocal(undo_t[:], keep_all[:])
 
-        gain_t = at(104, "gain_t", [P, GROUPS, RUN], F32)
-        load_factors(gain_t, gain)
         gather_words(1)
         gather_words(2)
+        order_w4(1)
 
-        w2_raw = [[at(16 * b + 8 * c, f"w2_raw{b}{c}", [P, PACK, KP], F32) for c in range(GROUPS)] for b in range(GROUPS)]
+        w2_raw = [[at(16 * (1 - b) + 8 * c, f"w2_raw{b}{c}", [P, PACK, KP], F32) for c in range(GROUPS)] for b in range(GROUPS)]
         for b in range(GROUPS):
             for c in range(GROUPS):
                 block = w2[b * KP : (b + 1) * KP, c * KP : (c + 1) * KP].rearrange("(v j e) n -> e v j n", j=PACK, e=2)
                 for e in range(2):
                     nc.sync.dma_start(w2_raw[b][c][e:P:2], block[e])
 
+        gain_t = at(44, "gain_t", [P, GROUPS, RUN], F32)
+        load_factors(gain_t, gain)
+
         def pass1(bank, i, s, a):
             nc.tensor.matmul_mx(
                 out=bank[:],
-                lhsT=w4_w[:, 2 * (a * H + P * i) : 2 * (a * H + P * (i + 1))].bitcast(FP4X4),
-                lhsT_scale=planes[:].bitcast(U8)[:, a * (S + H) + S + P * i : a * (S + H) + S + P * (i + 1)],
+                lhsT=w4_w[i // PACK][:, 2 * P * (PASSES1 * (i % PACK) + a) : 2 * P * (PASSES1 * (i % PACK) + a + 1)].bitcast(FP4X4),
+                lhsT_scale=planes[a][:, S + P * i : S + P * (i + 1)],
                 rhs=v_w[a][s][:].bitcast(FP8X4),
-                rhs_scale=planes[:].bitcast(U8)[:, a * (S + H) + s * BANK : a * (S + H) + (s + 1) * BANK],
+                rhs_scale=planes[a][:, s * BANK : (s + 1) * BANK],
                 start=(a == 0),
                 stop=(a == PASSES1 - 1),
             )
@@ -171,7 +190,7 @@ def tile_list_ring_leak_blend_kernel(
                     pass1(bank, i, s, a)
                 empty(bank, i, s)
 
-        w2_bf = [[at(32 + 4 * (GROUPS * b + c), f"w2_bf{b}{c}", [P, PACK * KP], BF16) for c in range(GROUPS)] for b in range(GROUPS)]
+        w2_bf = [[at((32, 36, 40, 120)[GROUPS * b + c], f"w2_bf{b}{c}", [P, PACK * KP], BF16) for c in range(GROUPS)] for b in range(GROUPS)]
         for b in range(GROUPS):
             for c in range(GROUPS):
                 nc.gpsimd.tensor_scalar(
@@ -183,16 +202,16 @@ def tile_list_ring_leak_blend_kernel(
                     ADD,
                 )
 
-        up = [at(80 + 2 * i, f"up{i}", [P, E], F32) for i in range(TILES)]
+        up = [at(112 if i == EARLY_SIG else 80 + 2 * i, f"up{i}", [P, E], F32) for i in range(TILES)]
         for i in range(TILES):
             nc.vector.tensor_copy(up[i][:], h[i][:].indirect(pos1_t[:]))
 
-        own = [at(58, "own0", [P, E], F32)]
-        nc.vector.tensor_copy(own[0][:], h[0][:].indirect(pos2_t[:]))
+        first_own = at(58, "first_own", [P, E], F32)
+        nc.vector.tensor_copy(first_own[:], h[0][:].indirect(pos2_t[:]))
         sig = [at(60 + 2 * i, f"sig{i}", [P, E], F32) for i in range(EARLY_SIG)]
         late_sig = at(66, "late_sig", [P, (TILES - EARLY_SIG) * E], F32)
         sig = [tile[:] for tile in sig] + [late_sig[:, i * E : (i + 1) * E] for i in range(TILES - EARLY_SIG)]
-        x_rows = [at(24 + 4 * b, f"x_rows{b}", [P, PACK * E], BF16) for b in range(GROUPS)]
+        x_rows = [at(8 + 4 * b, f"x_rows{b}", [P, PACK * E], BF16) for b in range(GROUPS)]
         x_bf = [at(94 + 6 * b, f"x_bf{b}", [P, E * PACK], BF16) for b in range(GROUPS)]
         x_w = [held(f"x_w{b}", [P, E], U32) for b in range(GROUPS)]
         x_sc = [held(f"x_sc{b}", [P, E], U8) for b in range(GROUPS)]
@@ -201,7 +220,7 @@ def tile_list_ring_leak_blend_kernel(
             for t in range(PACK):
                 i = b * PACK + t
                 nc.scalar.activation(sig[i], up[i][:], SIGMOID, scale=undo_t[:, i : i + 1])
-                nc.vector.tensor_scalar_mul(x_rows[b][:, t * E : (t + 1) * E], sig[i], gain_t[:, b, 2 * t : 2 * t + 1])
+                nc.gpsimd.tensor_scalar(x_rows[b][:, t * E : (t + 1) * E], sig[i], gain_t[:, b, 2 * t : 2 * t + 1], 0.0, MULT, ADD)
             nc.scalar.copy(
                 x_bf[b][:].rearrange("p (m t) -> p m t", t=PACK),
                 x_rows[b][:].rearrange("p (t m) -> p m t", t=PACK),
@@ -212,22 +231,28 @@ def tile_list_ring_leak_blend_kernel(
 
         message(0)
         message(1)
-        w2_planes = held("w2_planes", [P, GROUPS * GROUPS * KP], U8)
-        w2_sc = [[w2_planes[:, (b * GROUPS + c) * KP : (b * GROUPS + c + 1) * KP] for c in range(GROUPS)] for b in range(GROUPS)]
-        w2_w = []
-        for b in range(GROUPS):
-            codes = at((68, 94)[b], f"w2_codes{b}", [P, GROUPS * KP], U32)
-            w2_w.append([codes[:, c * KP : (c + 1) * KP] for c in range(GROUPS)])
-            for c in range(GROUPS):
-                nc.vector.quantize_mx(out=w2_w[b][c].bitcast(FP8X4), scales=w2_sc[b][c], in_=w2_bf[b][c][:])
-            quantise_x(b)
-        own.append(at(100, "own1", [P, E], F32))
-        nc.vector.tensor_copy(own[1][:], h[1][:].indirect(pos2_t[:]))
+        later_own = at(112, "later_own", [P, (EARLY_OWN - 1) * E], F32)
+        own = [first_own[:]] + [later_own[:, i * E : (i + 1) * E] for i in range(EARLY_OWN - 1)]
+        for i in range(1, EARLY_OWN):
+            nc.vector.tensor_copy(own[i], h[i][:].indirect(pos2_t[:]))
+        w2_sc = [[held(f"w2_sc{b}{c}", [P, KP], U8) for c in range(GROUPS)] for b in range(GROUPS)]
+        w2_w = [[None] * GROUPS for b in range(GROUPS)]
+
+        def quantise_w2(b, c, kb):
+            w2_w[b][c] = at(kb, f"w2_w{b}{c}", [P, KP], U32)
+            nc.vector.quantize_mx(out=w2_w[b][c][:].bitcast(FP8X4), scales=w2_sc[b][c][:], in_=w2_bf[b][c][:])
+
+        quantise_w2(0, 0, 68)
+        quantise_x(0)
+        quantise_w2(1, 0, 94)
+        quantise_w2(0, 1, 96)
+        quantise_x(1)
+        quantise_w2(1, 1, 102)
 
         banks = [psum.tile([P, BANK], F32, name="bank") for i in range(TILES)]
-        for b in range(GROUPS):
-            for c in range(GROUPS):
-                for t in range(PACK):
+        for c in range(GROUPS):
+            for t in range(PACK):
+                for b in range(GROUPS):
                     nc.tensor.matmul_mx(
                         out=banks[c * PACK + t][:],
                         lhsT=w2_w[b][c][:, P * t : P * (t + 1)].bitcast(FP8X4),
@@ -243,7 +268,7 @@ def tile_list_ring_leak_blend_kernel(
             c, t = divmod(i, PACK)
             res = held(f"res{i}", [P, E], F32)
             if i < EARLY_OWN:
-                nc.vector.scalar_tensor_tensor(res[:], banks[i][:], blend_t[:, c, 2 * t : 2 * t + 1], own[i][:], MULT, ADD)
+                nc.vector.scalar_tensor_tensor(res[:], banks[i][:], blend_t[:, c, 2 * t : 2 * t + 1], own[i], MULT, ADD)
             else:
                 share = held(f"share{i}", [P, E], F32)
                 nc.scalar.activation(share[:], banks[i][:], COPY, scale=blend_t[:, c, 2 * t : 2 * t + 1])

@@ -31,7 +31,7 @@ RUN = 2 * PACK
 PAIRS = P // 2
 KB = 1024
 EARLY_SIG = 3
-EARLY_OWN = 4
+EARLY_OWN = 2
 
 
 def tile_list_ring_leak_blend_kernel(
@@ -146,9 +146,9 @@ def tile_list_ring_leak_blend_kernel(
         gather_words(2)
         order_w4(1)
 
-        w2_raw = [[at(16 * (1 - b) + 8 * c, f"w2_raw{b}{c}", [P, PACK, KP], F32) for c in range(GROUPS)] for b in range(GROUPS)]
-        for b in range(GROUPS):
-            for c in range(GROUPS):
+        w2_raw = [[at(16 * (1 - c) + 8 * b, f"w2_raw{b}{c}", [P, PACK, KP], F32) for c in range(GROUPS)] for b in range(GROUPS)]
+        for c in range(GROUPS):
+            for b in range(GROUPS):
                 block = w2[b * KP : (b + 1) * KP, c * KP : (c + 1) * KP].rearrange("(v j e) n -> e v j n", j=PACK, e=2)
                 for e in range(2):
                     nc.sync.dma_start(w2_raw[b][c][e:P:2], block[e])
@@ -190,19 +190,19 @@ def tile_list_ring_leak_blend_kernel(
                     pass1(bank, i, s, a)
                 empty(bank, i, s)
 
-        w2_bf = [[at((32, 36, 40, 120)[GROUPS * b + c], f"w2_bf{b}{c}", [P, PACK * KP], BF16) for c in range(GROUPS)] for b in range(GROUPS)]
-        for b in range(GROUPS):
-            for c in range(GROUPS):
-                nc.gpsimd.tensor_scalar(
-                    w2_bf[b][c][:].rearrange("p (t v e j) -> p v t e j", t=PACK, e=2, j=PACK),
-                    w2_raw[b][c][:].rearrange("p j (v t e) -> p v t e j", t=PACK, e=2),
-                    1.0,
-                    0.0,
-                    MULT,
-                    ADD,
-                )
+        w2_bf = [[None] * GROUPS for b in range(GROUPS)]
 
-        up = [at(112 if i == EARLY_SIG else 80 + 2 * i, f"up{i}", [P, E], F32) for i in range(TILES)]
+        def rounding(b, c, kb):
+            w2_bf[b][c] = at(kb, f"w2_bf{b}{c}", [P, PACK * KP], BF16)
+            return (
+                w2_bf[b][c][:].rearrange("p (t v e j) -> p v t e j", t=PACK, e=2, j=PACK),
+                w2_raw[b][c][:].rearrange("p j (v t e) -> p v t e j", t=PACK, e=2),
+            )
+
+        for b in range(GROUPS):
+            nc.gpsimd.tensor_scalar(*rounding(b, 0, 36 + 4 * b), 1.0, 0.0, MULT, ADD)
+
+        up = [at(32 if i == EARLY_SIG else 80 + 2 * i, f"up{i}", [P, E], F32) for i in range(TILES)]
         for i in range(TILES):
             nc.vector.tensor_copy(up[i][:], h[i][:].indirect(pos1_t[:]))
 
@@ -211,7 +211,7 @@ def tile_list_ring_leak_blend_kernel(
         sig = [at(60 + 2 * i, f"sig{i}", [P, E], F32) for i in range(EARLY_SIG)]
         late_sig = at(66, "late_sig", [P, (TILES - EARLY_SIG) * E], F32)
         sig = [tile[:] for tile in sig] + [late_sig[:, i * E : (i + 1) * E] for i in range(TILES - EARLY_SIG)]
-        x_rows = [at(8 + 4 * b, f"x_rows{b}", [P, PACK * E], BF16) for b in range(GROUPS)]
+        x_rows = [at((30, 24)[b], f"x_rows{b}", [P, PACK * E], BF16) for b in range(GROUPS)]
         x_bf = [at(94 + 6 * b, f"x_bf{b}", [P, E * PACK], BF16) for b in range(GROUPS)]
         x_w = [held(f"x_w{b}", [P, E], U32) for b in range(GROUPS)]
         x_sc = [held(f"x_sc{b}", [P, E], U8) for b in range(GROUPS)]
@@ -220,7 +220,7 @@ def tile_list_ring_leak_blend_kernel(
             for t in range(PACK):
                 i = b * PACK + t
                 nc.scalar.activation(sig[i], up[i][:], SIGMOID, scale=undo_t[:, i : i + 1])
-                nc.gpsimd.tensor_scalar(x_rows[b][:, t * E : (t + 1) * E], sig[i], gain_t[:, b, 2 * t : 2 * t + 1], 0.0, MULT, ADD)
+                nc.vector.tensor_scalar_mul(x_rows[b][:, t * E : (t + 1) * E], sig[i], gain_t[:, b, 2 * t : 2 * t + 1])
             nc.scalar.copy(
                 x_bf[b][:].rearrange("p (m t) -> p m t", t=PACK),
                 x_rows[b][:].rearrange("p (t m) -> p m t", t=PACK),
@@ -231,10 +231,8 @@ def tile_list_ring_leak_blend_kernel(
 
         message(0)
         message(1)
-        later_own = at(112, "later_own", [P, (EARLY_OWN - 1) * E], F32)
-        own = [first_own[:]] + [later_own[:, i * E : (i + 1) * E] for i in range(EARLY_OWN - 1)]
-        for i in range(1, EARLY_OWN):
-            nc.vector.tensor_copy(own[i], h[i][:].indirect(pos2_t[:]))
+        nc.vector.tensor_copy(*rounding(0, 1, 72))
+        nc.scalar.copy(*rounding(1, 1, 24))
         w2_sc = [[held(f"w2_sc{b}{c}", [P, KP], U8) for c in range(GROUPS)] for b in range(GROUPS)]
         w2_w = [[None] * GROUPS for b in range(GROUPS)]
 
@@ -247,7 +245,10 @@ def tile_list_ring_leak_blend_kernel(
         quantise_w2(1, 0, 94)
         quantise_w2(0, 1, 96)
         quantise_x(1)
-        quantise_w2(1, 1, 102)
+        second_own = at(100, "second_own", [P, E], F32)
+        nc.vector.tensor_copy(second_own[:], h[1][:].indirect(pos2_t[:]))
+        own = [first_own[:], second_own[:]]
+        quantise_w2(1, 1, 112)
 
         banks = [psum.tile([P, BANK], F32, name="bank") for i in range(TILES)]
         for c in range(GROUPS):

@@ -200,7 +200,11 @@ def tile_list_ring_leak_blend_kernel(
             )
 
         for b in range(GROUPS):
-            nc.gpsimd.tensor_scalar(*rounding(b, 0, 36 + 4 * b), 1.0, 0.0, MULT, ADD)
+            rounded, raw = rounding(b, 0, 36 + 4 * b)
+            for t in range(PACK):
+                nc.gpsimd.tensor_scalar(
+                    rounded[:, :, t].rearrange("p v e j -> p v j e"), raw[:, :, t].rearrange("p v e j -> p v j e"), 1.0, 0.0, MULT, ADD
+                )
 
         up = [at(32 if i == EARLY_SIG else 80 + 2 * i, f"up{i}", [P, E], F32) for i in range(TILES)]
         for i in range(TILES):
@@ -273,5 +277,11 @@ def tile_list_ring_leak_blend_kernel(
             else:
                 share = held(f"share{i}", [P, E], F32)
                 nc.scalar.activation(share[:], banks[i][:], COPY, scale=blend_t[:, c, 2 * t : 2 * t + 1])
+                if i == TILES - 1:
+                    for cols in (slice(0, E // 2), slice(E // 2, E)):
+                        picks = pos2_t[:, cols.start // 16 : cols.stop // 16]
+                        nc.vector.tensor_tensor(res[:, cols], h[i][:].indirect(picks), share[:, cols], ADD)
+                        nc.sync.dma_start(rows[c, t][:, :, cols], res[:, cols])
+                    continue
                 nc.vector.tensor_tensor(res[:], h[i][:].indirect(pos2_t[:]), share[:], ADD)
             nc.sync.dma_start(rows[c, t], res[:])

@@ -60,6 +60,10 @@ def tile_list_ring_leak_blend_kernel(
         nc.vector.memset(tab_sc[:], 0)
         nc.vector.memset(w4_sc_raw[:], 0)
         nc.vector.memset(early_planes[:], 0)
+        warm_in = held("warm_in", [P, 1], F32)
+        warm_out = held("warm_out", [P, 1], F32)
+        nc.vector.memset(warm_in[:], 0.0)
+        nc.scalar.activation(warm_out[:], warm_in[:], SIGMOID)
 
         tab_w = [at(16 * a, f"tab_w{a}", [P, T], I32) for a in range(PASSES1 - 1)]
         w4_raw = [at(104, "w4_raw0", [P, PASSES1 * KP // 2], I32)]

@@ -30,8 +30,8 @@ QUADS = 4
 RUN = 2 * PACK
 PAIRS = P // 2
 KB = 1024
-EARLY_SIG = 3
-EARLY_OWN = 2
+EARLY_OWN = 5
+FUSED = TILES - EARLY_OWN
 
 
 def tile_list_ring_leak_blend_kernel(
@@ -139,8 +139,9 @@ def tile_list_ring_leak_blend_kernel(
         w4_raw.append(at(106, "w4_raw1", [P, PASSES1 * KP // 2], I32))
         load_w4(1)
         keep_t = [at(60 + 2 * (i - PACK), f"keep{i}", [P, 1], F32) if i >= PACK else held(f"keep{i}", [P, 1], F32) for i in range(TILES)]
-        for i in range(TILES):
-            nc.scalar.activation(keep_t[i][:], blend_t[:, i // PACK, 2 * (i % PACK) : 2 * (i % PACK) + 1], COPY, scale=-1.0, bias=1.0)
+        keep_last = at(162, "keep_last", [P, 1], F32)
+        for i, tile in list(enumerate(keep_t)) + [(TILES - 1, keep_last)]:
+            nc.scalar.activation(tile[:], blend_t[:, i // PACK, 2 * (i % PACK) : 2 * (i % PACK) + 1], COPY, scale=-1.0, bias=1.0)
         keep_all = held("keep_all", [P, TILES], F32)
         undo_t = held("undo_t", [P, TILES], F32)
         nc.vector.tensor_scalar(keep_all[:].rearrange("p (b t) -> p b t", b=GROUPS), blend_t[:, :, 0 : RUN - 1 : 2], -1.0, 1.0, MULT, ADD)
@@ -150,15 +151,14 @@ def tile_list_ring_leak_blend_kernel(
         gather_words(2)
         order_w4(1)
 
+        gain_t = at(44, "gain_t", [P, GROUPS, RUN], F32)
+        load_factors(gain_t, gain)
         w2_raw = [[at(16 * (1 - c) + 8 * b, f"w2_raw{b}{c}", [P, PACK, KP], F32) for c in range(GROUPS)] for b in range(GROUPS)]
         for c in range(GROUPS):
             for b in range(GROUPS):
                 block = w2[b * KP : (b + 1) * KP, c * KP : (c + 1) * KP].rearrange("(v j e) n -> e v j n", j=PACK, e=2)
                 for e in range(2):
                     nc.sync.dma_start(w2_raw[b][c][e:P:2], block[e])
-
-        gain_t = at(44, "gain_t", [P, GROUPS, RUN], F32)
-        load_factors(gain_t, gain)
 
         def pass1(bank, i, s, a):
             nc.tensor.matmul_mx(
@@ -171,10 +171,10 @@ def tile_list_ring_leak_blend_kernel(
                 stop=(a == PASSES1 - 1),
             )
 
-        h = [held(f"h{i}", [P, S], F32) for i in range(TILES)]
+        h = [at(130 + 4 * i, f"h{i}", [P, S], F32) for i in range(TILES)]
 
         def empty(bank, i, s):
-            nc.scalar.activation(h[i][:, s * BANK : (s + 1) * BANK], bank[:], COPY, scale=keep_t[i][:])
+            nc.scalar.activation(h[i][:, s * BANK : (s + 1) * BANK], bank[:], COPY, scale=(keep_last if (i, s) == (TILES - 1, HALVES - 1) else keep_t[i])[:])
 
         first = [[psum.tile([P, BANK], F32, name="bank") for s in range(HALVES)] for i in range(PACK)]
         for a in range(PASSES1 - 1):
@@ -194,74 +194,62 @@ def tile_list_ring_leak_blend_kernel(
                     pass1(bank, i, s, a)
                 empty(bank, i, s)
 
-        w2_bf = [[None] * GROUPS for b in range(GROUPS)]
+        w2_bf = [[at(114 + 4 * (GROUPS * c + b), f"w2_bf{b}{c}", [P, PACK * KP], BF16) for c in range(GROUPS)] for b in range(GROUPS)]
+        for c in range(GROUPS):
+            for b in range(GROUPS):
+                rounded = w2_bf[b][c][:].rearrange("p (t v e j) -> p v t e j", t=PACK, e=2, j=PACK)
+                raw = w2_raw[b][c][:].rearrange("p j (v t e) -> p v t e j", t=PACK, e=2)
+                for v in (slice(0, PAIRS // 2), slice(PAIRS // 2, PAIRS)):
+                    nc.gpsimd.tensor_scalar(rounded[:, v], raw[:, v], 1.0, 0.0, MULT, ADD)
 
-        def rounding(b, c, kb):
-            w2_bf[b][c] = at(kb, f"w2_bf{b}{c}", [P, PACK * KP], BF16)
-            return (
-                w2_bf[b][c][:].rearrange("p (t v e j) -> p v t e j", t=PACK, e=2, j=PACK),
-                w2_raw[b][c][:].rearrange("p j (v t e) -> p v t e j", t=PACK, e=2),
-            )
-
-        for b in range(GROUPS):
-            rounded, raw = rounding(b, 0, 36 + 4 * b)
-            for t in range(PACK):
-                nc.gpsimd.tensor_scalar(
-                    rounded[:, :, t].rearrange("p v e j -> p v j e"), raw[:, :, t].rearrange("p v e j -> p v j e"), 1.0, 0.0, MULT, ADD
-                )
-
-        up = [at(32 if i == EARLY_SIG else 80 + 2 * i, f"up{i}", [P, E], F32) for i in range(TILES)]
+        up = [at(80 + 2 * i, f"up{i}", [P, E], F32) for i in range(TILES)]
         for i in range(TILES):
             nc.vector.tensor_copy(up[i][:], h[i][:].indirect(pos1_t[:]))
+        own = at(162, "own", [P, EARLY_OWN, E], F32)
+        for i in range(EARLY_OWN):
+            nc.vector.tensor_copy(own[:, i, :], h[FUSED + i][:].indirect(pos2_t[:]))
 
-        first_own = at(58, "first_own", [P, E], F32)
-        nc.vector.tensor_copy(first_own[:], h[0][:].indirect(pos2_t[:]))
-        sig = [at(60 + 2 * i, f"sig{i}", [P, E], F32) for i in range(EARLY_SIG)]
-        late_sig = at(66, "late_sig", [P, (TILES - EARLY_SIG) * E], F32)
-        sig = [tile[:] for tile in sig] + [late_sig[:, i * E : (i + 1) * E] for i in range(TILES - EARLY_SIG)]
-        x_rows = [at((30, 24)[b], f"x_rows{b}", [P, PACK * E], BF16) for b in range(GROUPS)]
-        x_bf = [at(94 + 6 * b, f"x_bf{b}", [P, E * PACK], BF16) for b in range(GROUPS)]
-        x_w = [held(f"x_w{b}", [P, E], U32) for b in range(GROUPS)]
+        sig = [at(60 + 2 * (i if i < PACK else TILES - 1 - i), f"sig{i}", [P, E], F32)[:] for i in range(TILES)]
+        x_rows = [at((56, 96)[b], f"x_rows{b}", [P, PACK * E], BF16) for b in range(GROUPS)]
+        x_bf = [at((8, 110)[b], f"x_bf{b}", [P, E * PACK], BF16) for b in range(GROUPS)]
         x_sc = [held(f"x_sc{b}", [P, E], U8) for b in range(GROUPS)]
 
-        def message(b):
+        for b in range(GROUPS):
             for t in range(PACK):
                 i = b * PACK + t
                 nc.scalar.activation(sig[i], up[i][:], SIGMOID, scale=undo_t[:, i : i + 1])
-                nc.vector.tensor_scalar_mul(x_rows[b][:, t * E : (t + 1) * E], sig[i], gain_t[:, b, 2 * t : 2 * t + 1])
-            nc.scalar.copy(
-                x_bf[b][:].rearrange("p (m t) -> p m t", t=PACK),
-                x_rows[b][:].rearrange("p (t m) -> p m t", t=PACK),
-            )
+            for t in range(PACK):
+                nc.scalar.activation(x_rows[b][:, t * E : (t + 1) * E], sig[b * PACK + t], COPY, scale=gain_t[:, b, 2 * t : 2 * t + 1])
+        woven = [x_bf[b][:].rearrange("p (m t) -> p m t", t=PACK) for b in range(GROUPS)]
+        rows_of = [x_rows[b][:].rearrange("p (t m) -> p m t", t=PACK) for b in range(GROUPS)]
+        for m in (slice(0, E // 2), slice(E // 2, E)):
+            nc.gpsimd.tensor_scalar(woven[0][:, m], rows_of[0][:, m], 1.0, 0.0, MULT, ADD)
+        nc.scalar.copy(woven[1], rows_of[1])
 
-        def quantise_x(b):
-            nc.vector.quantize_mx(out=x_w[b][:].bitcast(FP8X4), scales=x_sc[b][:], in_=x_bf[b][:])
-
-        message(0)
-        message(1)
-        nc.vector.tensor_copy(*rounding(0, 1, 72))
-        nc.scalar.copy(*rounding(1, 1, 24))
         w2_sc = [[held(f"w2_sc{b}{c}", [P, KP], U8) for c in range(GROUPS)] for b in range(GROUPS)]
         w2_w = [[None] * GROUPS for b in range(GROUPS)]
+        x_w = [None] * GROUPS
 
         def quantise_w2(b, c, kb):
             w2_w[b][c] = at(kb, f"w2_w{b}{c}", [P, KP], U32)
             nc.vector.quantize_mx(out=w2_w[b][c][:].bitcast(FP8X4), scales=w2_sc[b][c][:], in_=w2_bf[b][c][:])
 
-        quantise_w2(0, 0, 68)
-        quantise_x(0)
-        quantise_w2(1, 0, 94)
-        quantise_w2(0, 1, 96)
-        quantise_x(1)
-        second_own = at(100, "second_own", [P, E], F32)
-        nc.vector.tensor_copy(second_own[:], h[1][:].indirect(pos2_t[:]))
-        own = [first_own[:], second_own[:]]
+        def quantise_x(b, kb):
+            x_w[b] = at(kb, f"x_w{b}", [P, E], U32)
+            nc.vector.quantize_mx(out=x_w[b][:].bitcast(FP8X4), scales=x_sc[b][:], in_=x_bf[b][:])
+
+        last_own = 130 + 4 * (TILES - 1)
+        quantise_w2(0, 0, last_own)
+        quantise_x(0, 114)
+        quantise_w2(1, 0, 8)
+        quantise_x(1, 118)
+        quantise_w2(0, 1, 110)
         quantise_w2(1, 1, 112)
 
         banks = [psum.tile([P, BANK], F32, name="bank") for i in range(TILES)]
         for c in range(GROUPS):
-            for t in range(PACK):
-                for b in range(GROUPS):
+            for b, t in [(b, t) for b in range(GROUPS) for t in range(PACK)] if c == 0 else [(b, t) for t in range(PACK) for b in range(GROUPS)]:
+                if True:
                     nc.tensor.matmul_mx(
                         out=banks[c * PACK + t][:],
                         lhsT=w2_w[b][c][:, P * t : P * (t + 1)].bitcast(FP8X4),
@@ -276,16 +264,13 @@ def tile_list_ring_leak_blend_kernel(
         for i in range(TILES):
             c, t = divmod(i, PACK)
             res = held(f"res{i}", [P, E], F32)
-            if i < EARLY_OWN:
-                nc.vector.scalar_tensor_tensor(res[:], banks[i][:], blend_t[:, c, 2 * t : 2 * t + 1], own[i], MULT, ADD)
-            else:
+            factor = blend_t[:, c, 2 * t : 2 * t + 1]
+            if i < FUSED:
                 share = held(f"share{i}", [P, E], F32)
-                nc.scalar.activation(share[:], banks[i][:], COPY, scale=blend_t[:, c, 2 * t : 2 * t + 1])
-                if i == TILES - 1:
-                    for cols in (slice(0, E // 2), slice(E // 2, E)):
-                        picks = pos2_t[:, cols.start // 16 : cols.stop // 16]
-                        nc.vector.tensor_tensor(res[:, cols], h[i][:].indirect(picks), share[:, cols], ADD)
-                        nc.sync.dma_start(rows[c, t][:, :, cols], res[:, cols])
-                    continue
+                nc.scalar.activation(share[:], banks[i][:], COPY, scale=factor)
                 nc.vector.tensor_tensor(res[:], h[i][:].indirect(pos2_t[:]), share[:], ADD)
-            nc.sync.dma_start(rows[c, t], res[:])
+                nc.sync.dma_start(rows[c, t], res[:])
+            else:
+                for cols in (slice(0, E // 2), slice(E // 2, E)) if i == TILES - 1 else (slice(0, E),):
+                    nc.vector.scalar_tensor_tensor(res[:, cols], banks[i][:, cols], factor, own[:, i - FUSED, cols], MULT, ADD)
+                    nc.sync.dma_start(rows[c, t][:, :, cols], res[:, cols])

@@ -120,15 +120,13 @@ def tile_list_ring_leak_blend_kernel(
         gather_words(0)
         tab_w.append(at(0, "tab_w2", [P, T], I32))
         load_table(2)
-        w4_w = [held(f"w4_w{b}", [P, PASSES1 * 2 * KP], U8) for b in range(GROUPS)]
-
-        def order_w4(b):
-            nc.vector.tensor_copy(
-                w4_w[b][:].bitcast(I32).rearrange("p (t c i) -> p c t i", t=PACK, i=4),
-                w4_raw[b][:].rearrange("p (c i t) -> p c t i", t=PACK, i=4),
-            )
-
-        order_w4(0)
+        tile_bytes = PASSES1 * 2 * P
+        w4_first = held("w4_first", [P, PACK * tile_bytes], U8)
+        nc.vector.tensor_copy(
+            w4_first[:].bitcast(I32).rearrange("p (t c i) -> p c t i", t=PACK, i=4),
+            w4_raw[0][:].rearrange("p (c i t) -> p c t i", t=PACK, i=4),
+        )
+        w4_w = [w4_first[:, t * tile_bytes : (t + 1) * tile_bytes] for t in range(PACK)]
         last_plane = at(104, "last_plane", [P, (S + H) // 4], I32)
         nc.vector.memset(last_plane[:], 0)
         for q in range(QUADS):
@@ -138,7 +136,7 @@ def tile_list_ring_leak_blend_kernel(
 
         w4_raw.append(at(106, "w4_raw1", [P, PASSES1 * KP // 2], I32))
         load_w4(1)
-        keep_t = [at(60 + 2 * (i - PACK), f"keep{i}", [P, 1], F32) if i >= PACK else held(f"keep{i}", [P, 1], F32) for i in range(TILES)]
+        keep_t = [held(f"keep{i}", [P, 1], F32) for i in range(TILES)]
         keep_last = at(162, "keep_last", [P, 1], F32)
         for i, tile in list(enumerate(keep_t)) + [(TILES - 1, keep_last)]:
             nc.scalar.activation(tile[:], blend_t[:, i // PACK, 2 * (i % PACK) : 2 * (i % PACK) + 1], COPY, scale=-1.0, bias=1.0)
@@ -149,7 +147,10 @@ def tile_list_ring_leak_blend_kernel(
 
         gather_words(1)
         gather_words(2)
-        order_w4(1)
+        for t in range(PACK):
+            words = at((62, 64, 66, 68)[t], f"w4_w{PACK + t}", [P, tile_bytes], U8)
+            nc.vector.tensor_copy(words[:].bitcast(I32), w4_raw[1][:, t::PACK])
+            w4_w.append(words[:])
 
         gain_t = at(44, "gain_t", [P, GROUPS, RUN], F32)
         load_factors(gain_t, gain)
@@ -163,7 +164,7 @@ def tile_list_ring_leak_blend_kernel(
         def pass1(bank, i, s, a):
             nc.tensor.matmul_mx(
                 out=bank[:],
-                lhsT=w4_w[i // PACK][:, 2 * P * (PASSES1 * (i % PACK) + a) : 2 * P * (PASSES1 * (i % PACK) + a + 1)].bitcast(FP4X4),
+                lhsT=w4_w[i][:, 2 * P * a : 2 * P * (a + 1)].bitcast(FP4X4),
                 lhsT_scale=planes[a][:, S + P * i : S + P * (i + 1)],
                 rhs=v_w[a][s][:].bitcast(FP8X4),
                 rhs_scale=planes[a][:, s * BANK : (s + 1) * BANK],
@@ -199,8 +200,7 @@ def tile_list_ring_leak_blend_kernel(
             for b in range(GROUPS):
                 rounded = w2_bf[b][c][:].rearrange("p (t v e j) -> p v t e j", t=PACK, e=2, j=PACK)
                 raw = w2_raw[b][c][:].rearrange("p j (v t e) -> p v t e j", t=PACK, e=2)
-                for v in (slice(0, PAIRS // 2), slice(PAIRS // 2, PAIRS)):
-                    nc.gpsimd.tensor_scalar(rounded[:, v], raw[:, v], 1.0, 0.0, MULT, ADD)
+                nc.gpsimd.tensor_scalar(rounded, raw, 1.0, 0.0, MULT, ADD)
 
         up = [at(80 + 2 * i, f"up{i}", [P, E], F32) for i in range(TILES)]
         for i in range(TILES):
@@ -209,8 +209,8 @@ def tile_list_ring_leak_blend_kernel(
         for i in range(EARLY_OWN):
             nc.vector.tensor_copy(own[:, i, :], h[FUSED + i][:].indirect(pos2_t[:]))
 
-        sig = [at(60 + 2 * (i if i < PACK else TILES - 1 - i), f"sig{i}", [P, E], F32)[:] for i in range(TILES)]
-        x_rows = [at((56, 96)[b], f"x_rows{b}", [P, PACK * E], BF16) for b in range(GROUPS)]
+        sig = [at((62, 64, 66, 56, 66, 56, 62, 64)[i], f"sig{i}", [P, E], F32)[:] for i in range(TILES)]
+        x_rows = [at((58, 96)[b], f"x_rows{b}", [P, PACK * E], BF16) for b in range(GROUPS)]
         x_bf = [at((8, 110)[b], f"x_bf{b}", [P, E * PACK], BF16) for b in range(GROUPS)]
         x_sc = [held(f"x_sc{b}", [P, E], U8) for b in range(GROUPS)]
 
@@ -238,11 +238,11 @@ def tile_list_ring_leak_blend_kernel(
             x_w[b] = at(kb, f"x_w{b}", [P, E], U32)
             nc.vector.quantize_mx(out=x_w[b][:].bitcast(FP8X4), scales=x_sc[b][:], in_=x_bf[b][:])
 
-        last_own = 130 + 4 * (TILES - 1)
-        quantise_w2(0, 0, last_own)
-        quantise_x(0, 114)
+        fourth_own = 130 + 4 * (TILES - 2)
+        quantise_w2(0, 0, fourth_own)
+        quantise_x(0, fourth_own + 2)
         quantise_w2(1, 0, 8)
-        quantise_x(1, 118)
+        quantise_x(1, 10)
         quantise_w2(0, 1, 110)
         quantise_w2(1, 1, 112)
 

@@ -31,7 +31,7 @@ RUN = 2 * PACK
 PAIRS = P // 2
 KB = 1024
 EARLY_OWN = 5
-FUSED = TILES - EARLY_OWN
+FIRST_FUSED = 2
 
 
 def tile_list_ring_leak_blend_kernel(
@@ -207,7 +207,7 @@ def tile_list_ring_leak_blend_kernel(
             nc.vector.tensor_copy(up[i][:], h[i][:].indirect(pos1_t[:]))
         own = at(162, "own", [P, EARLY_OWN, E], F32)
         for i in range(EARLY_OWN):
-            nc.vector.tensor_copy(own[:, i, :], h[FUSED + i][:].indirect(pos2_t[:]))
+            nc.vector.tensor_copy(own[:, i, :], h[FIRST_FUSED + i][:].indirect(pos2_t[:]))
 
         sig = [at((62, 64, 66, 56, 66, 56, 62, 64)[i], f"sig{i}", [P, E], F32)[:] for i in range(TILES)]
         x_rows = [at((58, 96)[b], f"x_rows{b}", [P, PACK * E], BF16) for b in range(GROUPS)]
@@ -238,7 +238,7 @@ def tile_list_ring_leak_blend_kernel(
             x_w[b] = at(kb, f"x_w{b}", [P, E], U32)
             nc.vector.quantize_mx(out=x_w[b][:].bitcast(FP8X4), scales=x_sc[b][:], in_=x_bf[b][:])
 
-        fourth_own = 130 + 4 * (TILES - 2)
+        fourth_own = 130 + 4 * (FIRST_FUSED + EARLY_OWN - 2)
         quantise_w2(0, 0, fourth_own)
         quantise_x(0, fourth_own + 2)
         quantise_w2(1, 0, 8)
@@ -263,14 +263,21 @@ def tile_list_ring_leak_blend_kernel(
         rows = out.rearrange("(c v t e) m -> c t v e m", v=PAIRS, t=PACK, e=2)
         for i in range(TILES):
             c, t = divmod(i, PACK)
-            res = held(f"res{i}", [P, E], F32)
             factor = blend_t[:, c, 2 * t : 2 * t + 1]
-            if i < FUSED:
-                share = held(f"share{i}", [P, E], F32)
-                nc.scalar.activation(share[:], banks[i][:], COPY, scale=factor)
-                nc.vector.tensor_tensor(res[:], h[i][:].indirect(pos2_t[:]), share[:], ADD)
+            if FIRST_FUSED < i < TILES - 1:
+                res = held(f"res{i}", [P, E], F32)
+                nc.vector.scalar_tensor_tensor(res[:], banks[i][:], factor, own[:, i - FIRST_FUSED, :], MULT, ADD)
                 nc.sync.dma_start(rows[c, t], res[:])
-            else:
-                for cols in (slice(0, E // 2), slice(E // 2, E)) if i == TILES - 1 else (slice(0, E),):
-                    nc.vector.scalar_tensor_tensor(res[:, cols], banks[i][:, cols], factor, own[:, i - FUSED, cols], MULT, ADD)
-                    nc.sync.dma_start(rows[c, t][:, :, cols], res[:, cols])
+                continue
+            share = held(f"share{i}", [P, E], F32)
+            nc.scalar.activation(share[:], banks[i][:], COPY, scale=factor)
+            if i == FIRST_FUSED:
+                res = at(130 + 4 * (FIRST_FUSED - 1), f"res{i}", [P, E], F32)
+                nc.gpsimd.tensor_tensor(res[:], own[:, 0, :], share[:], ADD)
+                nc.scalar.dma_start(rows[c, t], res[:])
+                continue
+            res = held(f"res{i}", [P, E], F32)
+            for cols in (slice(0, E // 2), slice(E // 2, E)) if i == TILES - 1 else (slice(0, E),):
+                picks = pos2_t[:, cols.start // 16 : cols.stop // 16]
+                nc.vector.tensor_tensor(res[:, cols], h[i][:].indirect(picks), share[:, cols], ADD)
+                nc.sync.dma_start(rows[c, t][:, :, cols], res[:, cols])

@@ -31,7 +31,7 @@ RUN = 2 * PACK
 PAIRS = P // 2
 KB = 1024
 EARLY_OWN = 5
-FIRST_FUSED = 2
+AHEAD = 3
 
 
 def tile_list_ring_leak_blend_kernel(
@@ -207,7 +207,7 @@ def tile_list_ring_leak_blend_kernel(
             nc.vector.tensor_copy(up[i][:], h[i][:].indirect(pos1_t[:]))
         own = at(162, "own", [P, EARLY_OWN, E], F32)
         for i in range(EARLY_OWN):
-            nc.vector.tensor_copy(own[:, i, :], h[FIRST_FUSED + i][:].indirect(pos2_t[:]))
+            nc.vector.tensor_copy(own[:, i, :], h[i][:].indirect(pos2_t[:]))
 
         sig = [at((62, 64, 66, 56, 66, 56, 62, 64)[i], f"sig{i}", [P, E], F32)[:] for i in range(TILES)]
         x_rows = [at((58, 96)[b], f"x_rows{b}", [P, PACK * E], BF16) for b in range(GROUPS)]
@@ -224,7 +224,8 @@ def tile_list_ring_leak_blend_kernel(
         rows_of = [x_rows[b][:].rearrange("p (t m) -> p m t", t=PACK) for b in range(GROUPS)]
         for m in (slice(0, E // 2), slice(E // 2, E)):
             nc.gpsimd.tensor_scalar(woven[0][:, m], rows_of[0][:, m], 1.0, 0.0, MULT, ADD)
-        nc.scalar.copy(woven[1], rows_of[1])
+        for m in (slice(0, E // 2), slice(E // 2, E)):
+            nc.scalar.copy(woven[1][:, m], rows_of[1][:, m])
 
         w2_sc = [[held(f"w2_sc{b}{c}", [P, KP], U8) for c in range(GROUPS)] for b in range(GROUPS)]
         w2_w = [[None] * GROUPS for b in range(GROUPS)]
@@ -236,9 +237,10 @@ def tile_list_ring_leak_blend_kernel(
 
         def quantise_x(b, kb):
             x_w[b] = at(kb, f"x_w{b}", [P, E], U32)
-            nc.vector.quantize_mx(out=x_w[b][:].bitcast(FP8X4), scales=x_sc[b][:], in_=x_bf[b][:])
+            for m in (slice(0, E // 2), slice(E // 2, E)) if b == GROUPS - 1 else (slice(0, E),):
+                nc.vector.quantize_mx(out=x_w[b][:, m].bitcast(FP8X4), scales=x_sc[b][:, m], in_=x_bf[b][:, PACK * m.start : PACK * m.stop])
 
-        fourth_own = 130 + 4 * (FIRST_FUSED + EARLY_OWN - 2)
+        fourth_own = 130 + 4 * (EARLY_OWN - 2)
         quantise_w2(0, 0, fourth_own)
         quantise_x(0, fourth_own + 2)
         quantise_w2(1, 0, 8)
@@ -248,7 +250,8 @@ def tile_list_ring_leak_blend_kernel(
 
         banks = [psum.tile([P, BANK], F32, name="bank") for i in range(TILES)]
         for c in range(GROUPS):
-            for b, t in [(b, t) for b in range(GROUPS) for t in range(PACK)] if c == 0 else [(b, t) for t in range(PACK) for b in range(GROUPS)]:
+            ahead = AHEAD if c == 0 else 0
+            for b, t in [(b, t) for b in range(GROUPS) for t in range(ahead)] + [(b, t) for t in range(ahead, PACK) for b in (1, 0)]:
                 if True:
                     nc.tensor.matmul_mx(
                         out=banks[c * PACK + t][:],
@@ -256,23 +259,23 @@ def tile_list_ring_leak_blend_kernel(
                         lhsT_scale=w2_sc[b][c][:, P * t : P * (t + 1)],
                         rhs=x_w[b][:].bitcast(FP8X4),
                         rhs_scale=x_sc[b][:],
-                        start=(b == 0),
-                        stop=(b == GROUPS - 1),
+                        start=(b == 0) == (t < ahead),
+                        stop=(b == 1) == (t < ahead),
                     )
 
         rows = out.rearrange("(c v t e) m -> c t v e m", v=PAIRS, t=PACK, e=2)
         for i in range(TILES):
             c, t = divmod(i, PACK)
             factor = blend_t[:, c, 2 * t : 2 * t + 1]
-            if FIRST_FUSED < i < TILES - 1:
+            if 0 < i < EARLY_OWN:
                 res = held(f"res{i}", [P, E], F32)
-                nc.vector.scalar_tensor_tensor(res[:], banks[i][:], factor, own[:, i - FIRST_FUSED, :], MULT, ADD)
+                nc.vector.scalar_tensor_tensor(res[:], banks[i][:], factor, own[:, i, :], MULT, ADD)
                 nc.sync.dma_start(rows[c, t], res[:])
                 continue
             share = held(f"share{i}", [P, E], F32)
             nc.scalar.activation(share[:], banks[i][:], COPY, scale=factor)
-            if i == FIRST_FUSED:
-                res = at(130 + 4 * (FIRST_FUSED - 1), f"res{i}", [P, E], F32)
+            if i == 0:
+                res = at(126, f"res{i}", [P, E], F32)
                 nc.gpsimd.tensor_tensor(res[:], own[:, 0, :], share[:], ADD)
                 nc.scalar.dma_start(rows[c, t], res[:])
                 continue

@@ -32,6 +32,7 @@ PAIRS = P // 2
 KB = 1024
 EARLY_OWN = 5
 AHEAD = 3
+LAST_KB = 172
 
 
 def tile_list_ring_leak_blend_kernel(
@@ -54,11 +55,12 @@ def tile_list_ring_leak_blend_kernel(
         pos1_t = lists.tile([P, E // 16], U16, name="pos1_t")
         pos2_t = lists.tile([P, E // 16], U16, name="pos2_t")
 
-        tab_sc = at(76, "tab_sc", [P, T // 4], I32)
-        w4_sc_raw = held("w4_sc_raw", [P, H // 4], I32)
+        tab_sc = [at(72 + 4 * a, f"tab_sc{a}", [P, T // 4], I32) for a in range(2)]
+        w4_sc_raw = held("w4_sc_raw", [P, 2 * H // 4], I32)
         early_planes = held("early_planes", [P, 2 * (S + H) // 4], I32)
-        nc.vector.memset(tab_sc[:], 0)
         nc.vector.memset(w4_sc_raw[:], 0)
+        nc.vector.memset(tab_sc[0][:], 0)
+        nc.gpsimd.memset(tab_sc[1][:], 0)
         nc.vector.memset(early_planes[:], 0)
         warm_in = held("warm_in", [P, 1], F32)
         warm_out = held("warm_out", [P, 1], F32)
@@ -85,30 +87,33 @@ def tile_list_ring_leak_blend_kernel(
 
         nc.sync.dma_start(offs_t[:], offs)
         nc.sync.dma_start(pos1_t[:], pos1)
-        load_table(0, slice(0, T // 2))
+        load_table(0, slice(0, T // 4))
         nc.sync.dma_start(pos2_t[:], pos2)
-        for tile, scales in ((tab_sc, tab_scales), (w4_sc_raw, w4_scales)):
-            nc.sync.dma_start(tile[4:68:2, :], scales.bitcast(I32)[0:2].rearrange("a j c -> j a c"))
-            nc.sync.dma_start(tile[5:P:8, :], scales.bitcast(I32)[2])
-        load_table(0, slice(T // 2, T))
+        w4_sc_slots = w4_sc_raw[:].rearrange("p (a c) -> p a c", a=2)
+        nc.sync.dma_start(w4_sc_slots[5:P:8], w4_scales.bitcast(I32)[0:2].rearrange("a j c -> j a c"))
+        nc.sync.dma_start(w4_sc_slots[6:P:8, 0], w4_scales.bitcast(I32)[2])
+        for a, tile, first_row in ((0, tab_sc[0], 5), (2, tab_sc[0], 6), (1, tab_sc[1], 5)):
+            nc.sync.dma_start(tile[first_row:P:8, :], tab_scales.bitcast(I32)[a])
+        load_table(0, slice(T // 4, T))
         load_w4(0)
         load_table(1)
 
-        picked_sc = at(32, "picked_sc", [P, S // 4], I32)
-        nc.vector.tensor_copy(picked_sc[:].bitcast(U8), tab_sc[:].bitcast(U8).indirect(offs_t[:]))
-        both_sc = at(44, "both_sc", [P, (S + H) // 4], I32)
+        both_sc = at(44, "both_sc", [P, 2 * (S + H) // 4], I32)
+        both_slots = both_sc[:].rearrange("p (a c) -> p a c", a=2)
         nc.vector.tensor_copy(
-            both_sc[:, S // 4 :].bitcast(U16).rearrange("p (g t v) -> p g t v", t=PACK, v=PAIRS),
-            w4_sc_raw[:].bitcast(U16).rearrange("p (g v t) -> p g t v", t=PACK, v=PAIRS),
+            both_slots[:, :, S // 4 :].bitcast(U16).rearrange("p a (g t v) -> p a g t v", t=PACK, v=PAIRS),
+            w4_sc_raw[:].bitcast(U16).rearrange("p (a g v t) -> p a g t v", a=2, t=PACK, v=PAIRS),
         )
-        nc.vector.tensor_copy(both_sc[:, 0 : S // 4], picked_sc[:])
+        picked_sc = at(LAST_KB, "picked_sc", [P, 2 * S // 4], I32)
+        for a in range(2):
+            nc.vector.tensor_copy(picked_sc[:].bitcast(U8)[:, a * S : (a + 1) * S], tab_sc[a][:].bitcast(U8).indirect(offs_t[:]))
+        nc.vector.tensor_copy(both_slots[:, :, 0 : S // 4], picked_sc[:].rearrange("p (a c) -> p a c", a=2))
         blend_t = at(76, "blend_t", [P, GROUPS, RUN], F32)
         load_factors(blend_t, blend)
-        for q in range(QUADS):
-            nc.scalar.dma_start(
-                early_planes[32 * q : 32 * q + 4, :].rearrange("r (a c) -> r a c", a=2),
-                both_sc[4 + 16 * q : 4 + 16 * (q + 1) : 2, :],
-            )
+        for r in range(QUADS):
+            nc.sync.dma_start(early_planes[r:P:32, :], both_sc[5 + 8 * r : P : 32, :])
+        tab_w.append(at(LAST_KB, "tab_w2", [P, T], I32))
+        load_table(2)
 
         v_w = [[at(48 + 2 * (HALVES * a + s), f"v_w{a}{s}", [P, BANK], U32) for s in range(HALVES)] for a in range(PASSES1)]
 
@@ -117,24 +122,22 @@ def tile_list_ring_leak_blend_kernel(
                 cols = slice(s * BANK // 16, (s + 1) * BANK // 16)
                 nc.vector.tensor_copy(v_w[a][s][:], tab_w[a][:].bitcast(U32).indirect(offs_t[:, cols]))
 
-        gather_words(0)
-        tab_w.append(at(0, "tab_w2", [P, T], I32))
-        load_table(2)
         tile_bytes = PASSES1 * 2 * P
         w4_first = held("w4_first", [P, PACK * tile_bytes], U8)
         nc.vector.tensor_copy(
             w4_first[:].bitcast(I32).rearrange("p (t c i) -> p c t i", t=PACK, i=4),
             w4_raw[0][:].rearrange("p (c i t) -> p c t i", t=PACK, i=4),
         )
+        gather_words(0)
         w4_w = [w4_first[:, t * tile_bytes : (t + 1) * tile_bytes] for t in range(PACK)]
-        last_plane = at(104, "last_plane", [P, (S + H) // 4], I32)
+        last_plane = at(0, "last_plane", [P, (S + H) // 4], I32)
         nc.vector.memset(last_plane[:], 0)
-        for q in range(QUADS):
-            nc.sync.dma_start(last_plane[32 * q : 32 * q + 4, :], both_sc[5 + 32 * q : 32 * (q + 1) : 8, :])
+        for r in range(QUADS):
+            nc.sync.dma_start(last_plane[r:P:32, :], both_slots[6 + 8 * r : P : 32, 0])
         planes = [early_planes[:].bitcast(U8)[:, a * (S + H) : (a + 1) * (S + H)] for a in range(2)]
         planes.append(last_plane[:].bitcast(U8))
 
-        w4_raw.append(at(106, "w4_raw1", [P, PASSES1 * KP // 2], I32))
+        w4_raw.append(at(2, "w4_raw1", [P, PASSES1 * KP // 2], I32))
         load_w4(1)
         keep_t = [held(f"keep{i}", [P, 1], F32) for i in range(TILES)]
         keep_last = at(162, "keep_last", [P, 1], F32)
@@ -154,7 +157,7 @@ def tile_list_ring_leak_blend_kernel(
 
         gain_t = at(44, "gain_t", [P, GROUPS, RUN], F32)
         load_factors(gain_t, gain)
-        w2_raw = [[at(16 * (1 - c) + 8 * b, f"w2_raw{b}{c}", [P, PACK, KP], F32) for c in range(GROUPS)] for b in range(GROUPS)]
+        w2_raw = [[at((16, LAST_KB)[c] + 8 * b, f"w2_raw{b}{c}", [P, PACK, KP], F32) for c in range(GROUPS)] for b in range(GROUPS)]
         for c in range(GROUPS):
             for b in range(GROUPS):
                 block = w2[b * KP : (b + 1) * KP, c * KP : (c + 1) * KP].rearrange("(v j e) n -> e v j n", j=PACK, e=2)
@@ -211,7 +214,7 @@ def tile_list_ring_leak_blend_kernel(
 
         sig = [at((62, 64, 66, 56, 66, 56, 62, 64)[i], f"sig{i}", [P, E], F32)[:] for i in range(TILES)]
         x_rows = [at((58, 96)[b], f"x_rows{b}", [P, PACK * E], BF16) for b in range(GROUPS)]
-        x_bf = [at((8, 110)[b], f"x_bf{b}", [P, E * PACK], BF16) for b in range(GROUPS)]
+        x_bf = [at((LAST_KB + 8, 110)[b], f"x_bf{b}", [P, E * PACK], BF16) for b in range(GROUPS)]
         x_sc = [held(f"x_sc{b}", [P, E], U8) for b in range(GROUPS)]
 
         for b in range(GROUPS):
@@ -243,8 +246,8 @@ def tile_list_ring_leak_blend_kernel(
         fourth_own = 130 + 4 * (EARLY_OWN - 2)
         quantise_w2(0, 0, fourth_own)
         quantise_x(0, fourth_own + 2)
-        quantise_w2(1, 0, 8)
-        quantise_x(1, 10)
+        quantise_w2(1, 0, LAST_KB + 8)
+        quantise_x(1, LAST_KB + 10)
         quantise_w2(0, 1, 110)
         quantise_w2(1, 1, 112)
 

@@ -58,10 +58,13 @@ def tile_list_ring_leak_blend_kernel(
         tab_sc = [at(72 + 4 * a, f"tab_sc{a}", [P, T // 4], I32) for a in range(2)]
         w4_sc_raw = held("w4_sc_raw", [P, 2 * H // 4], I32)
         early_planes = held("early_planes", [P, 2 * (S + H) // 4], I32)
-        nc.vector.memset(w4_sc_raw[:], 0)
-        nc.vector.memset(tab_sc[0][:], 0)
+        for tile in (w4_sc_raw, tab_sc[0]):
+            nc.vector.memset(tile[:, 0:1], 0)
+            nc.vector.memset(tile[:, 1:], 0)
         nc.gpsimd.memset(tab_sc[1][:], 0)
         nc.vector.memset(early_planes[:], 0)
+        last_plane = held("last_plane", [P, (S + H) // 4], I32)
+        nc.vector.memset(last_plane[:], 0)
         warm_in = held("warm_in", [P, 1], F32)
         warm_out = held("warm_out", [P, 1], F32)
         nc.vector.memset(warm_in[:], 0.0)
@@ -87,14 +90,14 @@ def tile_list_ring_leak_blend_kernel(
 
         nc.sync.dma_start(offs_t[:], offs)
         nc.sync.dma_start(pos1_t[:], pos1)
-        load_table(0, slice(0, T // 4))
+        load_table(0, slice(0, 5 * T // 16))
         nc.sync.dma_start(pos2_t[:], pos2)
         w4_sc_slots = w4_sc_raw[:].rearrange("p (a c) -> p a c", a=2)
         nc.sync.dma_start(w4_sc_slots[5:P:8], w4_scales.bitcast(I32)[0:2].rearrange("a j c -> j a c"))
         nc.sync.dma_start(w4_sc_slots[6:P:8, 0], w4_scales.bitcast(I32)[2])
         for a, tile, first_row in ((0, tab_sc[0], 5), (2, tab_sc[0], 6), (1, tab_sc[1], 5)):
             nc.sync.dma_start(tile[first_row:P:8, :], tab_scales.bitcast(I32)[a])
-        load_table(0, slice(T // 4, T))
+        load_table(0, slice(5 * T // 16, T))
         load_w4(0)
         load_table(1)
 
@@ -114,6 +117,8 @@ def tile_list_ring_leak_blend_kernel(
             nc.sync.dma_start(early_planes[r:P:32, :], both_sc[5 + 8 * r : P : 32, :])
         tab_w.append(at(LAST_KB, "tab_w2", [P, T], I32))
         load_table(2)
+        for r in range(QUADS):
+            nc.sync.dma_start(last_plane[r:P:32, :], both_slots[6 + 8 * r : P : 32, 0])
 
         v_w = [[at(48 + 2 * (HALVES * a + s), f"v_w{a}{s}", [P, BANK], U32) for s in range(HALVES)] for a in range(PASSES1)]
 
@@ -130,10 +135,6 @@ def tile_list_ring_leak_blend_kernel(
         )
         gather_words(0)
         w4_w = [w4_first[:, t * tile_bytes : (t + 1) * tile_bytes] for t in range(PACK)]
-        last_plane = at(0, "last_plane", [P, (S + H) // 4], I32)
-        nc.vector.memset(last_plane[:], 0)
-        for r in range(QUADS):
-            nc.sync.dma_start(last_plane[r:P:32, :], both_slots[6 + 8 * r : P : 32, 0])
         planes = [early_planes[:].bitcast(U8)[:, a * (S + H) : (a + 1) * (S + H)] for a in range(2)]
         planes.append(last_plane[:].bitcast(U8))
 
@@ -155,7 +156,7 @@ def tile_list_ring_leak_blend_kernel(
             nc.vector.tensor_copy(words[:].bitcast(I32), w4_raw[1][:, t::PACK])
             w4_w.append(words[:])
 
-        gain_t = at(44, "gain_t", [P, GROUPS, RUN], F32)
+        gain_t = at(2, "gain_t", [P, GROUPS, RUN], F32)
         load_factors(gain_t, gain)
         w2_raw = [[at((16, LAST_KB)[c] + 8 * b, f"w2_raw{b}{c}", [P, PACK, KP], F32) for c in range(GROUPS)] for b in range(GROUPS)]
         for c in range(GROUPS):

@@ -226,8 +226,7 @@ def tile_list_ring_leak_blend_kernel(
                 nc.scalar.activation(x_rows[b][:, t * E : (t + 1) * E], sig[b * PACK + t], COPY, scale=gain_t[:, b, 2 * t : 2 * t + 1])
         woven = [x_bf[b][:].rearrange("p (m t) -> p m t", t=PACK) for b in range(GROUPS)]
         rows_of = [x_rows[b][:].rearrange("p (t m) -> p m t", t=PACK) for b in range(GROUPS)]
-        for m in (slice(0, E // 2), slice(E // 2, E)):
-            nc.gpsimd.tensor_scalar(woven[0][:, m], rows_of[0][:, m], 1.0, 0.0, MULT, ADD)
+        nc.gpsimd.tensor_scalar(woven[0], rows_of[0], 1.0, 0.0, MULT, ADD)
         for m in (slice(0, E // 2), slice(E // 2, E)):
             nc.scalar.copy(woven[1][:, m], rows_of[1][:, m])
 
@@ -255,7 +254,7 @@ def tile_list_ring_leak_blend_kernel(
         banks = [psum.tile([P, BANK], F32, name="bank") for i in range(TILES)]
         for c in range(GROUPS):
             ahead = AHEAD if c == 0 else 0
-            for b, t in [(b, t) for b in range(GROUPS) for t in range(ahead)] + [(b, t) for t in range(ahead, PACK) for b in (1, 0)]:
+            for b, t in [(b, t) for b in range(GROUPS) for t in range(ahead)] + [(b, t) for t in (range(ahead, PACK) if c == 0 else (1, 0, 2, 3)) for b in (1, 0)]:
                 if True:
                     nc.tensor.matmul_mx(
                         out=banks[c * PACK + t][:],
@@ -268,23 +267,27 @@ def tile_list_ring_leak_blend_kernel(
                     )
 
         rows = out.rearrange("(c v t e) m -> c t v e m", v=PAIRS, t=PACK, e=2)
+        summed = at(126, "summed", [P, E], F32)
         for i in range(TILES):
             c, t = divmod(i, PACK)
             factor = blend_t[:, c, 2 * t : 2 * t + 1]
-            if 0 < i < EARLY_OWN:
-                res = held(f"res{i}", [P, E], F32)
-                nc.vector.scalar_tensor_tensor(res[:], banks[i][:], factor, own[:, i, :], MULT, ADD)
-                nc.sync.dma_start(rows[c, t], res[:])
+            if i < EARLY_OWN:
+                cut = E if i == 0 else 0
+                if cut:
+                    share = held(f"share{i}", [P, cut], F32)
+                    nc.scalar.activation(share[:], banks[i][:, 0:cut], COPY, scale=factor)
+                    res = summed[:, i * E : i * E + cut]
+                    nc.gpsimd.tensor_tensor(res, own[:, i, 0:cut], share[:], ADD)
+                    nc.sync.dma_start(rows[c, t][:, :, 0:cut], res)
+                if cut < E:
+                    res = held(f"res{i}", [P, E - cut], F32)
+                    nc.vector.scalar_tensor_tensor(res[:], banks[i][:, cut:E], factor, own[:, i, cut:E], MULT, ADD)
+                    nc.sync.dma_start(rows[c, t][:, :, cut:E], res[:])
                 continue
             share = held(f"share{i}", [P, E], F32)
             nc.scalar.activation(share[:], banks[i][:], COPY, scale=factor)
-            if i == 0:
-                res = at(126, f"res{i}", [P, E], F32)
-                nc.gpsimd.tensor_tensor(res[:], own[:, 0, :], share[:], ADD)
-                nc.scalar.dma_start(rows[c, t], res[:])
-                continue
             res = held(f"res{i}", [P, E], F32)
-            for cols in (slice(0, E // 2), slice(E // 2, E)) if i == TILES - 1 else (slice(0, E),):
+            for cols in (slice(0, E // 2), slice(E // 2, 3 * E // 4), slice(3 * E // 4, E)) if i == TILES - 1 else (slice(0, E),):
                 picks = pos2_t[:, cols.start // 16 : cols.stop // 16]
                 nc.vector.tensor_tensor(res[:, cols], h[i][:].indirect(picks), share[:, cols], ADD)
                 nc.sync.dma_start(rows[c, t][:, :, cols], res[:, cols])

@@ -278,7 +278,7 @@ def tile_list_ring_leak_blend_kernel(
                     nc.scalar.activation(share[:], banks[i][:, 0:cut], COPY, scale=factor)
                     res = summed[:, i * E : i * E + cut]
                     nc.gpsimd.tensor_tensor(res, own[:, i, 0:cut], share[:], ADD)
-                    nc.sync.dma_start(rows[c, t][:, :, 0:cut], res)
+                    nc.gpsimd.dma_start(rows[c, t][:, :, 0:cut], res)
                 if cut < E:
                     res = held(f"res{i}", [P, E - cut], F32)
                     nc.vector.scalar_tensor_tensor(res[:], banks[i][:, cut:E], factor, own[:, i, cut:E], MULT, ADD)

@@ -33,6 +33,8 @@ KB = 1024
 EARLY_OWN = 5
 AHEAD = 3
 LAST_KB = 172
+SLOT = S + KP
+FIRST_KB = 0
 
 
 def tile_list_ring_leak_blend_kernel(
@@ -56,21 +58,22 @@ def tile_list_ring_leak_blend_kernel(
         pos2_t = lists.tile([P, E // 16], U16, name="pos2_t")
 
         tab_sc = [at(72 + 4 * a, f"tab_sc{a}", [P, T // 4], I32) for a in range(2)]
-        w4_sc_raw = held("w4_sc_raw", [P, 2 * H // 4], I32)
-        early_planes = held("early_planes", [P, 2 * (S + H) // 4], I32)
-        for tile in (w4_sc_raw, tab_sc[0]):
+        early_sc = held("early_sc", [P, 2 * KP // 4], I32)
+        late_sc = at(38, "late_sc", [P, 4 * KP // 4], I32)
+        early_planes = held("early_planes", [P, 2 * SLOT // 4], I32)
+        late_planes = held("late_planes", [P, 2 * SLOT // 4], I32)
+        for tile in (early_sc, tab_sc[0]):
             nc.vector.memset(tile[:, 0:1], 0)
             nc.vector.memset(tile[:, 1:], 0)
         nc.gpsimd.memset(tab_sc[1][:], 0)
-        nc.vector.memset(early_planes[:], 0)
-        last_plane = held("last_plane", [P, (S + H) // 4], I32)
-        nc.vector.memset(last_plane[:], 0)
+        for tile in (late_sc, early_planes, late_planes):
+            nc.vector.memset(tile[:], 0)
         warm_in = held("warm_in", [P, 1], F32)
         warm_out = held("warm_out", [P, 1], F32)
         nc.vector.memset(warm_in[:], 0.0)
         nc.scalar.activation(warm_out[:], warm_in[:], SIGMOID)
 
-        tab_w = [at(16 * a, f"tab_w{a}", [P, T], I32) for a in range(PASSES1 - 1)]
+        tab_w = [at((FIRST_KB, 16)[a], f"tab_w{a}", [P, T], I32) for a in range(PASSES1 - 1)]
         w4_raw = [at(104, "w4_raw0", [P, PASSES1 * KP // 2], I32)]
 
         def load_w4(b):
@@ -92,33 +95,34 @@ def tile_list_ring_leak_blend_kernel(
         nc.sync.dma_start(pos1_t[:], pos1)
         load_table(0, slice(0, 5 * T // 16))
         nc.sync.dma_start(pos2_t[:], pos2)
-        w4_sc_slots = w4_sc_raw[:].rearrange("p (a c) -> p a c", a=2)
-        nc.sync.dma_start(w4_sc_slots[5:P:8], w4_scales.bitcast(I32)[0:2].rearrange("a j c -> j a c"))
-        nc.sync.dma_start(w4_sc_slots[6:P:8, 0], w4_scales.bitcast(I32)[2])
+        w4_sc_rows = w4_scales.bitcast(I32).rearrange("a j c -> j a c")
+        nc.sync.dma_start(early_sc[5:P:8].rearrange("j (a c) -> j a c", a=2), w4_sc_rows[:, 0:2, 0 : KP // 4])
         for a, tile, first_row in ((0, tab_sc[0], 5), (2, tab_sc[0], 6), (1, tab_sc[1], 5)):
             nc.sync.dma_start(tile[first_row:P:8, :], tab_scales.bitcast(I32)[a])
         load_table(0, slice(5 * T // 16, T))
+        nc.sync.dma_start(late_sc[6:P:8, 0 : H // 4], w4_sc_rows[:, 2])
+        nc.sync.dma_start(late_sc[6:P:8, H // 4 :].rearrange("j (a c) -> j a c", a=2), w4_sc_rows[:, 0:2, KP // 4 :])
         load_w4(0)
         load_table(1)
 
-        both_sc = at(44, "both_sc", [P, 2 * (S + H) // 4], I32)
-        both_slots = both_sc[:].rearrange("p (a c) -> p a c", a=2)
-        nc.vector.tensor_copy(
-            both_slots[:, :, S // 4 :].bitcast(U16).rearrange("p a (g t v) -> p a g t v", t=PACK, v=PAIRS),
-            w4_sc_raw[:].bitcast(U16).rearrange("p (a g v t) -> p a g t v", a=2, t=PACK, v=PAIRS),
-        )
-        picked_sc = at(LAST_KB, "picked_sc", [P, 2 * S // 4], I32)
+        def order_scales(dst, src):
+            nc.vector.tensor_copy(
+                dst.bitcast(U16).rearrange("p g (t v) -> p g t v", t=PACK),
+                src[:].bitcast(U16).rearrange("p (g v t) -> p g t v", t=PACK, v=PAIRS),
+            )
+
+        early_rows = at(44, "early_rows", [P, 2, SLOT // 4], I32)
+        order_scales(early_rows[:, :, S // 4 :], early_sc)
+        picked_sc = [at((32, LAST_KB)[a], f"picked_sc{a}", [P, S // 4], I32) for a in range(2)]
         for a in range(2):
-            nc.vector.tensor_copy(picked_sc[:].bitcast(U8)[:, a * S : (a + 1) * S], tab_sc[a][:].bitcast(U8).indirect(offs_t[:]))
-        nc.vector.tensor_copy(both_slots[:, :, 0 : S // 4], picked_sc[:].rearrange("p (a c) -> p a c", a=2))
+            nc.vector.tensor_copy(picked_sc[a][:].bitcast(U8), tab_sc[a][:].bitcast(U8).indirect(offs_t[:]))
+            nc.vector.tensor_copy(early_rows[:, a, 0 : S // 4], picked_sc[a][:])
         blend_t = at(76, "blend_t", [P, GROUPS, RUN], F32)
         load_factors(blend_t, blend)
         for r in range(QUADS):
-            nc.sync.dma_start(early_planes[r:P:32, :], both_sc[5 + 8 * r : P : 32, :])
+            nc.sync.dma_start(early_planes[r:P:32, :], early_rows[5 + 8 * r : P : 32].rearrange("q a c -> q (a c)"))
         tab_w.append(at(LAST_KB, "tab_w2", [P, T], I32))
         load_table(2)
-        for r in range(QUADS):
-            nc.sync.dma_start(last_plane[r:P:32, :], both_slots[6 + 8 * r : P : 32, 0])
 
         v_w = [[at(48 + 2 * (HALVES * a + s), f"v_w{a}{s}", [P, BANK], U32) for s in range(HALVES)] for a in range(PASSES1)]
 
@@ -135,10 +139,17 @@ def tile_list_ring_leak_blend_kernel(
         )
         gather_words(0)
         w4_w = [w4_first[:, t * tile_bytes : (t + 1) * tile_bytes] for t in range(PACK)]
-        planes = [early_planes[:].bitcast(U8)[:, a * (S + H) : (a + 1) * (S + H)] for a in range(2)]
-        planes.append(last_plane[:].bitcast(U8))
+        late_rows = at(104, "late_rows", [P, 2 * SLOT // 4], I32)
+        nc.vector.tensor_copy(late_rows[:, 0 : S // 4], picked_sc[0][:])
+        order_scales(late_rows[:, S // 4 :].rearrange("p (g c) -> p g c", g=4), late_sc)
+        for r in range(QUADS):
+            nc.sync.dma_start(late_planes[r:P:32, :], late_rows[6 + 8 * r : P : 32, :])
+        early_bytes, late_bytes = early_planes[:].bitcast(U8), late_planes[:].bitcast(U8)
+        v_planes = [early_bytes[:, 0:S], early_bytes[:, SLOT : SLOT + S], late_bytes[:, 0:S]]
+        late_w4 = [late_bytes[:, S + KP * g : S + KP * (g + 1)] for g in range(4)]
+        w4_planes = [[early_bytes[:, S:SLOT], early_bytes[:, SLOT + S :], late_w4[0]], [late_w4[2], late_w4[3], late_w4[1]]]
 
-        w4_raw.append(at(2, "w4_raw1", [P, PASSES1 * KP // 2], I32))
+        w4_raw.append(at(36, "w4_raw1", [P, PASSES1 * KP // 2], I32))
         load_w4(1)
         keep_t = [held(f"keep{i}", [P, 1], F32) for i in range(TILES)]
         keep_last = at(162, "keep_last", [P, 1], F32)
@@ -156,7 +167,7 @@ def tile_list_ring_leak_blend_kernel(
             nc.vector.tensor_copy(words[:].bitcast(I32), w4_raw[1][:, t::PACK])
             w4_w.append(words[:])
 
-        gain_t = at(2, "gain_t", [P, GROUPS, RUN], F32)
+        gain_t = at(36, "gain_t", [P, GROUPS, RUN], F32)
         load_factors(gain_t, gain)
         w2_raw = [[at((16, LAST_KB)[c] + 8 * b, f"w2_raw{b}{c}", [P, PACK, KP], F32) for c in range(GROUPS)] for b in range(GROUPS)]
         for c in range(GROUPS):
@@ -169,9 +180,9 @@ def tile_list_ring_leak_blend_kernel(
             nc.tensor.matmul_mx(
                 out=bank[:],
                 lhsT=w4_w[i][:, 2 * P * a : 2 * P * (a + 1)].bitcast(FP4X4),
-                lhsT_scale=planes[a][:, S + P * i : S + P * (i + 1)],
+                lhsT_scale=w4_planes[i // PACK][a][:, P * (i % PACK) : P * (i % PACK + 1)],
                 rhs=v_w[a][s][:].bitcast(FP8X4),
-                rhs_scale=planes[a][:, s * BANK : (s + 1) * BANK],
+                rhs_scale=v_planes[a][:, s * BANK : (s + 1) * BANK],
                 start=(a == 0),
                 stop=(a == PASSES1 - 1),
             )
@@ -287,7 +298,7 @@ def tile_list_ring_leak_blend_kernel(
             share = held(f"share{i}", [P, E], F32)
             nc.scalar.activation(share[:], banks[i][:], COPY, scale=factor)
             res = held(f"res{i}", [P, E], F32)
-            for cols in (slice(0, E // 2), slice(E // 2, 3 * E // 4), slice(3 * E // 4, E)) if i == TILES - 1 else (slice(0, E),):
+            for cols in (slice(0, E // 2), slice(E // 2, E)) if i == TILES - 1 else (slice(0, E),):
                 picks = pos2_t[:, cols.start // 16 : cols.stop // 16]
                 nc.vector.tensor_tensor(res[:, cols], h[i][:].indirect(picks), share[:, cols], ADD)
                 nc.sync.dma_start(rows[c, t][:, :, cols], res[:, cols])

@@ -30,11 +30,11 @@ QUADS = 4
 RUN = 2 * PACK
 PAIRS = P // 2
 KB = 1024
-EARLY_OWN = 5
-AHEAD = 3
-LAST_KB = 172
-SLOT = S + KP
-FIRST_KB = 0
+PLAIN = 5
+FIRST_PIECE = 5 * T // 16
+SECOND_PIECE = 11 * T // 16
+THIRD_PIECE = 7 * T // 16
+SCALAR_COLS = 384
 
 
 def tile_list_ring_leak_blend_kernel(
@@ -45,36 +45,38 @@ def tile_list_ring_leak_blend_kernel(
         lists = ctx.enter_context(tc.tile_pool(name="lists", bufs=1))
         keep = ctx.enter_context(tc.tile_pool(name="keep", bufs=1))
         laid = ctx.enter_context(tc.tile_pool(name="laid", bufs=1))
-        psum = ctx.enter_context(tc.psum_pool(name="psum", bufs=8))
+        psum = ctx.enter_context(tc.psum_pool(name="psum", bufs=1))
 
         def held(name, shape, dtype):
             return keep.tile(shape, dtype, name=name, align_bytes=64)
 
         def at(kb, name, shape, dtype):
-            return laid.tile(shape, dtype, name=name, offset=kb * KB, align_bytes=64)
+            return laid.tile(shape, dtype, name=name, offset=int(kb * KB), align_bytes=64)
+
+        def bank_tile(k):
+            return psum.tile([P, BANK], F32, name=f"bank{k}")
 
         offs_t = lists.tile([P, S // 16], U16, name="offs_t")
         pos1_t = lists.tile([P, E // 16], U16, name="pos1_t")
         pos2_t = lists.tile([P, E // 16], U16, name="pos2_t")
 
-        tab_sc = [at(72 + 4 * a, f"tab_sc{a}", [P, T // 4], I32) for a in range(2)]
         early_sc = held("early_sc", [P, 2 * KP // 4], I32)
-        late_sc = at(38, "late_sc", [P, 4 * KP // 4], I32)
-        early_planes = held("early_planes", [P, 2 * SLOT // 4], I32)
-        late_planes = held("late_planes", [P, 2 * SLOT // 4], I32)
-        for tile in (early_sc, tab_sc[0]):
-            nc.vector.memset(tile[:, 0:1], 0)
-            nc.vector.memset(tile[:, 1:], 0)
-        nc.gpsimd.memset(tab_sc[1][:], 0)
-        for tile in (late_sc, early_planes, late_planes):
+        tab_sc = held("tab_sc", [P, T // 4], I32)
+        late_sc = at(60, "late_sc", [P, 4 * KP // 4], I32)
+        early_planes = held("early_planes", [P, (S + 2 * KP) // 4], I32)
+        mid_plane = held("mid_plane", [P, S // 4], I32)
+        late_planes = held("late_planes", [P, (S + 4 * KP) // 4], I32)
+        for tile in (early_sc, tab_sc, late_sc, early_planes, mid_plane, late_planes):
             nc.vector.memset(tile[:], 0)
         warm_in = held("warm_in", [P, 1], F32)
         warm_out = held("warm_out", [P, 1], F32)
         nc.vector.memset(warm_in[:], 0.0)
         nc.scalar.activation(warm_out[:], warm_in[:], SIGMOID)
 
-        tab_w = [at((FIRST_KB, 16)[a], f"tab_w{a}", [P, T], I32) for a in range(PASSES1 - 1)]
-        w4_raw = [at(104, "w4_raw0", [P, PASSES1 * KP // 2], I32)]
+        tab_w = [at((0, 16, 33)[a], f"tab_w{a}", [P, T], I32) for a in range(PASSES1)]
+        w4_raw = [at(64, "w4_raw0", [P, PASSES1 * KP // 2], I32)]
+        blend_t = held("blend_t", [P, GROUPS, RUN], F32)
+        gain_t = held("gain_t", [P, GROUPS, RUN], F32)
 
         def load_w4(b):
             nc.sync.dma_start(
@@ -82,104 +84,112 @@ def tile_list_ring_leak_blend_kernel(
                 w4_words.bitcast(I32)[:, :, b * KP // 2 : (b + 1) * KP // 2].rearrange("a p c -> p a c"),
             )
 
-
-        def load_factors(tile, factors):
+        def load_factors(tile, factors, e):
             runs = factors.rearrange("(b v k) -> v b k", b=GROUPS, k=RUN)
-            for e in range(2):
-                nc.sync.dma_start(tile[e:P:2, :, 0 : RUN - 1], runs[:, :, e : e + RUN - 1])
+            nc.sync.dma_start(tile[e:P:2, :, 0 : RUN - 1], runs[:, :, e : e + RUN - 1])
 
-        def load_table(a, cols=slice(0, T)):
+        def load_table(a, cols):
             nc.sync.dma_start(tab_w[a][:, cols], tab_words[a].rearrange("p t i -> p (t i)").bitcast(I32)[:, cols])
 
-        nc.sync.dma_start(offs_t[:], offs)
-        nc.sync.dma_start(pos1_t[:], pos1)
-        load_table(0, slice(0, 5 * T // 16))
-        nc.sync.dma_start(pos2_t[:], pos2)
-        w4_sc_rows = w4_scales.bitcast(I32).rearrange("a j c -> j a c")
-        nc.sync.dma_start(early_sc[5:P:8].rearrange("j (a c) -> j a c", a=2), w4_sc_rows[:, 0:2, 0 : KP // 4])
-        for a, tile, first_row in ((0, tab_sc[0], 5), (2, tab_sc[0], 6), (1, tab_sc[1], 5)):
-            nc.sync.dma_start(tile[first_row:P:8, :], tab_scales.bitcast(I32)[a])
-        load_table(0, slice(5 * T // 16, T))
-        nc.sync.dma_start(late_sc[6:P:8, 0 : H // 4], w4_sc_rows[:, 2])
-        nc.sync.dma_start(late_sc[6:P:8, H // 4 :].rearrange("j (a c) -> j a c", a=2), w4_sc_rows[:, 0:2, KP // 4 :])
-        load_w4(0)
-        load_table(1)
+        def move_rows(planes, rows, first_row):
+            for r in range(QUADS):
+                nc.sync.dma_start(planes[r:P:32, :], rows[first_row + 8 * r : P : 32, :])
 
         def order_scales(dst, src):
             nc.vector.tensor_copy(
-                dst.bitcast(U16).rearrange("p g (t v) -> p g t v", t=PACK),
+                dst.bitcast(U16).rearrange("p (g t v) -> p g t v", t=PACK, v=PAIRS),
                 src[:].bitcast(U16).rearrange("p (g v t) -> p g t v", t=PACK, v=PAIRS),
             )
 
-        early_rows = at(44, "early_rows", [P, 2, SLOT // 4], I32)
-        order_scales(early_rows[:, :, S // 4 :], early_sc)
-        picked_sc = [at((32, LAST_KB)[a], f"picked_sc{a}", [P, S // 4], I32) for a in range(2)]
-        for a in range(2):
-            nc.vector.tensor_copy(picked_sc[a][:].bitcast(U8), tab_sc[a][:].bitcast(U8).indirect(offs_t[:]))
-            nc.vector.tensor_copy(early_rows[:, a, 0 : S // 4], picked_sc[a][:])
-        blend_t = at(76, "blend_t", [P, GROUPS, RUN], F32)
-        load_factors(blend_t, blend)
-        for r in range(QUADS):
-            nc.sync.dma_start(early_planes[r:P:32, :], early_rows[5 + 8 * r : P : 32].rearrange("q a c -> q (a c)"))
-        tab_w.append(at(LAST_KB, "tab_w2", [P, T], I32))
-        load_table(2)
+        nc.sync.dma_start(offs_t[:], offs)
+        nc.sync.dma_start(pos1_t[:], pos1)
+        load_table(0, slice(0, FIRST_PIECE))
+        load_factors(gain_t, gain, 0)
+        w4_sc_rows = w4_scales.bitcast(I32).rearrange("a j c -> j a c")
+        nc.sync.dma_start(early_sc[5:P:8].rearrange("j (a c) -> j a c", a=2), w4_sc_rows[:, 0:2, 0 : KP // 4])
+        for a in range(PASSES1):
+            nc.sync.dma_start(tab_sc[5 + a : P : 8, :], tab_scales.bitcast(I32)[a])
+        load_table(0, slice(FIRST_PIECE, T))
+        load_w4(0)
+        nc.sync.dma_start(late_sc[7:P:8, 0 : H // 4], w4_sc_rows[:, 2])
+        nc.sync.dma_start(late_sc[7:P:8, H // 4 :].rearrange("j (a c) -> j a c", a=2), w4_sc_rows[:, 0:2, KP // 4 :])
+        load_factors(gain_t, gain, 1)
+        for e in range(2):
+            load_factors(blend_t, blend, e)
+        load_table(1, slice(0, SECOND_PIECE))
 
-        v_w = [[at(48 + 2 * (HALVES * a + s), f"v_w{a}{s}", [P, BANK], U32) for s in range(HALVES)] for a in range(PASSES1)]
+        early_rows = held("early_rows", [P, (S + 2 * KP) // 4], I32)
+        picked = held("picked", [P, S // 4], I32)
+        order_scales(early_rows[:, S // 4 :], early_sc)
+        nc.vector.tensor_copy(picked[:].bitcast(U8), tab_sc[:].bitcast(U8).indirect(offs_t[:]))
+        nc.vector.tensor_copy(early_rows[:, 0 : S // 4], picked[:])
+        move_rows(early_planes, early_rows, 5)
+        load_table(1, slice(SECOND_PIECE, T))
+        load_table(2, slice(0, THIRD_PIECE))
+        move_rows(mid_plane, picked, 6)
+        load_table(2, slice(THIRD_PIECE, T))
 
-        def gather_words(a):
-            for s in range(HALVES):
-                cols = slice(s * BANK // 16, (s + 1) * BANK // 16)
-                nc.vector.tensor_copy(v_w[a][s][:], tab_w[a][:].bitcast(U32).indirect(offs_t[:, cols]))
+        v_w = [[at(68 + 2 * (HALVES * a + s), f"v_w{a}{s}", [P, BANK], U32) for s in range(HALVES)] for a in range(PASSES1)]
+
+        def gather_words(a, s):
+            cols = slice(s * BANK // 16, (s + 1) * BANK // 16)
+            nc.vector.tensor_copy(v_w[a][s][:], tab_w[a][:].bitcast(U32).indirect(offs_t[:, cols]))
 
         tile_bytes = PASSES1 * 2 * P
-        w4_first = held("w4_first", [P, PACK * tile_bytes], U8)
-        nc.vector.tensor_copy(
-            w4_first[:].bitcast(I32).rearrange("p (t c i) -> p c t i", t=PACK, i=4),
-            w4_raw[0][:].rearrange("p (c i t) -> p c t i", t=PACK, i=4),
-        )
-        gather_words(0)
-        w4_w = [w4_first[:, t * tile_bytes : (t + 1) * tile_bytes] for t in range(PACK)]
-        late_rows = at(104, "late_rows", [P, 2 * SLOT // 4], I32)
-        nc.vector.tensor_copy(late_rows[:, 0 : S // 4], picked_sc[0][:])
-        order_scales(late_rows[:, S // 4 :].rearrange("p (g c) -> p g c", g=4), late_sc)
-        for r in range(QUADS):
-            nc.sync.dma_start(late_planes[r:P:32, :], late_rows[6 + 8 * r : P : 32, :])
-        early_bytes, late_bytes = early_planes[:].bitcast(U8), late_planes[:].bitcast(U8)
-        v_planes = [early_bytes[:, 0:S], early_bytes[:, SLOT : SLOT + S], late_bytes[:, 0:S]]
-        late_w4 = [late_bytes[:, S + KP * g : S + KP * (g + 1)] for g in range(4)]
-        w4_planes = [[early_bytes[:, S:SLOT], early_bytes[:, SLOT + S :], late_w4[0]], [late_w4[2], late_w4[3], late_w4[1]]]
 
-        w4_raw.append(at(36, "w4_raw1", [P, PASSES1 * KP // 2], I32))
+        def order_words(dst, src):
+            nc.vector.tensor_copy(
+                dst[:].bitcast(I32).rearrange("p (t c i) -> p c t i", t=PACK, i=4),
+                src[:].rearrange("p (c i t) -> p c t i", t=PACK, i=4),
+            )
+
+        w4_w = [held("w4_w0", [P, PACK * tile_bytes], U8)]
+        gather_words(0, 0)
+        order_words(w4_w[0], w4_raw[0])
+        gather_words(0, 1)
+        late_rows = held("late_rows", [P, (S + 4 * KP) // 4], I32)
+        nc.vector.tensor_copy(late_rows[:, 0 : S // 4], picked[:])
+        order_scales(late_rows[:, S // 4 :], late_sc)
+        move_rows(late_planes, late_rows, 7)
+        early_bytes, late_bytes = early_planes[:].bitcast(U8), late_planes[:].bitcast(U8)
+        v_planes = [early_bytes[:, 0:S], mid_plane[:].bitcast(U8), late_bytes[:, 0:S]]
+        late_w4 = [late_bytes[:, S + KP * g : S + KP * (g + 1)] for g in range(4)]
+        w4_planes = [
+            [early_bytes[:, S : S + KP], early_bytes[:, S + KP :], late_w4[0]],
+            [late_w4[2], late_w4[3], late_w4[1]],
+        ]
+        w4_raw.append(at(60, "w4_raw1", [P, PASSES1 * KP // 2], I32))
         load_w4(1)
-        keep_t = [held(f"keep{i}", [P, 1], F32) for i in range(TILES)]
-        keep_last = at(162, "keep_last", [P, 1], F32)
-        for i, tile in list(enumerate(keep_t)) + [(TILES - 1, keep_last)]:
-            nc.scalar.activation(tile[:], blend_t[:, i // PACK, 2 * (i % PACK) : 2 * (i % PACK) + 1], COPY, scale=-1.0, bias=1.0)
+
         keep_all = held("keep_all", [P, TILES], F32)
-        undo_t = held("undo_t", [P, TILES], F32)
-        nc.vector.tensor_scalar(keep_all[:].rearrange("p (b t) -> p b t", b=GROUPS), blend_t[:, :, 0 : RUN - 1 : 2], -1.0, 1.0, MULT, ADD)
+        nc.scalar.activation(keep_all[:].rearrange("p (b t) -> p b t", b=GROUPS), blend_t[:, :, 0 : RUN - 1 : 2], COPY, scale=-1.0, bias=1.0)
+        gate = {}
+        for i, kb in ((5, 80), (6, 82), (7, 84)):
+            gate[i] = at(kb, f"keep_gate{i}", [P, 1], F32)
+            nc.scalar.activation(gate[i][:, 0:1], blend_t[:, i // PACK, 2 * (i % PACK) : 2 * (i % PACK) + 1], COPY, scale=-1.0, bias=1.0)
+        undo_t = at(64, "undo_t", [P, TILES], F32)
         nc.vector.reciprocal(undo_t[:], keep_all[:])
 
-        gather_words(1)
-        gather_words(2)
-        for t in range(PACK):
-            words = at((62, 64, 66, 68)[t], f"w4_w{PACK + t}", [P, tile_bytes], U8)
-            nc.vector.tensor_copy(words[:].bitcast(I32), w4_raw[1][:, t::PACK])
-            w4_w.append(words[:])
+        for a in range(1, PASSES1):
+            for s in range(HALVES):
+                gather_words(a, s)
+        w4_w.append(at(49 - 1 / 16, "w4_w1", [P, PACK * tile_bytes], U8))
+        order_words(w4_w[1], w4_raw[1])
 
-        gain_t = at(36, "gain_t", [P, GROUPS, RUN], F32)
-        load_factors(gain_t, gain)
-        w2_raw = [[at((16, LAST_KB)[c] + 8 * b, f"w2_raw{b}{c}", [P, PACK, KP], F32) for c in range(GROUPS)] for b in range(GROUPS)]
+        w2_raw = [[at((16, 24, 32.5, 40.5)[2 * c + b], f"w2_raw{b}{c}", [P, PACK, KP], F32) for c in range(GROUPS)] for b in range(GROUPS)]
         for c in range(GROUPS):
             for b in range(GROUPS):
                 block = w2[b * KP : (b + 1) * KP, c * KP : (c + 1) * KP].rearrange("(v j e) n -> e v j n", j=PACK, e=2)
                 for e in range(2):
                     nc.sync.dma_start(w2_raw[b][c][e:P:2], block[e])
+            if c == 0:
+                nc.sync.dma_start(pos2_t[:], pos2)
 
         def pass1(bank, i, s, a):
+            first_byte = tile_bytes * (i % PACK) + 2 * P * a
             nc.tensor.matmul_mx(
                 out=bank[:],
-                lhsT=w4_w[i][:, 2 * P * a : 2 * P * (a + 1)].bitcast(FP4X4),
+                lhsT=w4_w[i // PACK][:, first_byte : first_byte + 2 * P].bitcast(FP4X4),
                 lhsT_scale=w4_planes[i // PACK][a][:, P * (i % PACK) : P * (i % PACK + 1)],
                 rhs=v_w[a][s][:].bitcast(FP8X4),
                 rhs_scale=v_planes[a][:, s * BANK : (s + 1) * BANK],
@@ -187,117 +197,125 @@ def tile_list_ring_leak_blend_kernel(
                 stop=(a == PASSES1 - 1),
             )
 
-        h = [at(130 + 4 * i, f"h{i}", [P, S], F32) for i in range(TILES)]
+        h = [at(96 + 4 * i, f"h{i}", [P, S], F32) for i in range(TILES)]
 
         def empty(bank, i, s):
-            nc.scalar.activation(h[i][:, s * BANK : (s + 1) * BANK], bank[:], COPY, scale=(keep_last if (i, s) == (TILES - 1, HALVES - 1) else keep_t[i])[:])
+            factor = gate[i][:, 0:1] if s == 1 and i in gate else keep_all[:, i : i + 1]
+            if (i, s) == (0, 1):
+                nc.vector.tensor_scalar_mul(h[i][:, s * BANK : (s + 1) * BANK], bank[:], factor)
+            else:
+                nc.scalar.activation(h[i][:, s * BANK : (s + 1) * BANK], bank[:], COPY, scale=factor)
 
-        first = [[psum.tile([P, BANK], F32, name="bank") for s in range(HALVES)] for i in range(PACK)]
-        for a in range(PASSES1 - 1):
+        first = {(i, s): bank_tile(PACK * s + i) for s in range(HALVES) for i in range(PACK)}
+        for a in range(PASSES1):
             for s in range(HALVES):
                 for i in range(PACK):
-                    pass1(first[i][s], i, s, a)
-        for i, s in [(0, 0), (1, 0), (0, 1), (1, 1), (2, 0), (2, 1), (3, 0), (3, 1)]:
-            pass1(first[i][s], i, s, PASSES1 - 1)
-            if (i, s) == (0, 1):
-                nc.vector.tensor_scalar_mul(h[i][:, s * BANK : (s + 1) * BANK], first[i][s][:], keep_t[i][:])
-            else:
-                empty(first[i][s], i, s)
-        for i in range(PACK, TILES):
-            for s in range(HALVES):
-                bank = psum.tile([P, BANK], F32, name="bank")
-                for a in range(PASSES1):
-                    pass1(bank, i, s, a)
-                empty(bank, i, s)
+                    pass1(first[i, s], i, s, a)
+        emptied = [(0, 0), (1, 0), (2, 0), (0, 1), (1, 1), (2, 1), (3, 0), (3, 1)]
+        for i, s in emptied:
+            empty(first[i, s], i, s)
+        for k, (i, s) in enumerate(emptied):
+            bank = bank_tile(PACK * s + i)
+            for a in range(PASSES1):
+                pass1(bank, PACK + k // HALVES, k % HALVES, a)
+            empty(bank, PACK + k // HALVES, k % HALVES)
 
-        w2_bf = [[at(114 + 4 * (GROUPS * c + b), f"w2_bf{b}{c}", [P, PACK * KP], BF16) for c in range(GROUPS)] for b in range(GROUPS)]
+        w2_bf = [[at(4 * (GROUPS * c + b), f"w2_bf{b}{c}", [P, PACK * KP], BF16) for c in range(GROUPS)] for b in range(GROUPS)]
         for c in range(GROUPS):
             for b in range(GROUPS):
                 rounded = w2_bf[b][c][:].rearrange("p (t v e j) -> p v t e j", t=PACK, e=2, j=PACK)
                 raw = w2_raw[b][c][:].rearrange("p j (v t e) -> p v t e j", t=PACK, e=2)
                 nc.gpsimd.tensor_scalar(rounded, raw, 1.0, 0.0, MULT, ADD)
 
-        up = [at(80 + 2 * i, f"up{i}", [P, E], F32) for i in range(TILES)]
+        up = [at(128 + 2 * i, f"up{i}", [P, E], F32) for i in range(TILES)]
+        own = [at(80 + 2 * i, f"own{i}", [P, E], F32)[:] for i in range(2)]
+        own_rest = at(84, "own_rest", [P, PLAIN - 3, E], F32)
+        own.extend(own_rest[:, i, :] for i in range(PLAIN - 3))
+
+        def gather_own(i):
+            nc.vector.tensor_copy(own[i], h[i][:].indirect(pos2_t[:]))
+
         for i in range(TILES):
             nc.vector.tensor_copy(up[i][:], h[i][:].indirect(pos1_t[:]))
-        own = at(162, "own", [P, EARLY_OWN, E], F32)
-        for i in range(EARLY_OWN):
-            nc.vector.tensor_copy(own[:, i, :], h[i][:].indirect(pos2_t[:]))
+            if i >= 5:
+                gather_own(i - 5)
+        for i in range(3, PLAIN - 1):
+            gather_own(i)
 
-        sig = [at((62, 64, 66, 56, 66, 56, 62, 64)[i], f"sig{i}", [P, E], F32)[:] for i in range(TILES)]
-        x_rows = [at((58, 96)[b], f"x_rows{b}", [P, PACK * E], BF16) for b in range(GROUPS)]
-        x_bf = [at((LAST_KB + 8, 110)[b], f"x_bf{b}", [P, E * PACK], BF16) for b in range(GROUPS)]
-        x_sc = [held(f"x_sc{b}", [P, E], U8) for b in range(GROUPS)]
-
+        sig = [at(144 + 2 * i, f"sig{i}", [P, E], F32) for i in range(TILES)]
+        x_rows = [at(160 + 4 * b, f"x_rows{b}", [P, PACK * E], BF16) for b in range(GROUPS)]
         for b in range(GROUPS):
             for t in range(PACK):
                 i = b * PACK + t
-                nc.scalar.activation(sig[i], up[i][:], SIGMOID, scale=undo_t[:, i : i + 1])
+                nc.scalar.activation(sig[i][:], up[i][:], SIGMOID, scale=undo_t[:, i : i + 1])
             for t in range(PACK):
-                nc.scalar.activation(x_rows[b][:, t * E : (t + 1) * E], sig[b * PACK + t], COPY, scale=gain_t[:, b, 2 * t : 2 * t + 1])
-        woven = [x_bf[b][:].rearrange("p (m t) -> p m t", t=PACK) for b in range(GROUPS)]
+                nc.scalar.activation(x_rows[b][:, t * E : (t + 1) * E], sig[b * PACK + t][:], COPY, scale=gain_t[:, b, 2 * t : 2 * t + 1])
         rows_of = [x_rows[b][:].rearrange("p (t m) -> p m t", t=PACK) for b in range(GROUPS)]
-        nc.gpsimd.tensor_scalar(woven[0], rows_of[0], 1.0, 0.0, MULT, ADD)
-        for m in (slice(0, E // 2), slice(E // 2, E)):
-            nc.scalar.copy(woven[1][:, m], rows_of[1][:, m])
+        x_bf0 = at(41, "x_bf0", [P, E * PACK], BF16)
+        nc.gpsimd.tensor_scalar(x_bf0[:].rearrange("p (m t) -> p m t", t=PACK), rows_of[0], 1.0, 0.0, MULT, ADD)
 
         w2_sc = [[held(f"w2_sc{b}{c}", [P, KP], U8) for c in range(GROUPS)] for b in range(GROUPS)]
         w2_w = [[None] * GROUPS for b in range(GROUPS)]
-        x_w = [None] * GROUPS
+        x_sc = [held(f"x_sc{b}", [P, E], U8) for b in range(GROUPS)]
+        x_w = [held("x_w0", [P, E], U32)]
 
-        def quantise_w2(b, c, kb):
-            w2_w[b][c] = at(kb, f"w2_w{b}{c}", [P, KP], U32)
+        def quantise_w2(b, c):
+            w2_w[b][c] = at(160 + 4 * c + 2 * b, f"w2_w{b}{c}", [P, KP], U32)
             nc.vector.quantize_mx(out=w2_w[b][c][:].bitcast(FP8X4), scales=w2_sc[b][c][:], in_=w2_bf[b][c][:])
 
-        def quantise_x(b, kb):
-            x_w[b] = at(kb, f"x_w{b}", [P, E], U32)
-            for m in (slice(0, E // 2), slice(E // 2, E)) if b == GROUPS - 1 else (slice(0, E),):
-                nc.vector.quantize_mx(out=x_w[b][:, m].bitcast(FP8X4), scales=x_sc[b][:, m], in_=x_bf[b][:, PACK * m.start : PACK * m.stop])
+        quantise_w2(0, 0)
+        nc.vector.quantize_mx(out=x_w[0][:].bitcast(FP8X4), scales=x_sc[0][:], in_=x_bf0[:])
+        quantise_w2(1, 0)
+        own.append(at(0, "own_last", [P, E], F32)[:])
+        gather_own(PLAIN - 1)
 
-        fourth_own = 130 + 4 * (EARLY_OWN - 2)
-        quantise_w2(0, 0, fourth_own)
-        quantise_x(0, fourth_own + 2)
-        quantise_w2(1, 0, LAST_KB + 8)
-        quantise_x(1, LAST_KB + 10)
-        quantise_w2(0, 1, 110)
-        quantise_w2(1, 1, 112)
+        x_bf1 = [at(168, "x_bf1a", [P, SCALAR_COLS * PACK], BF16), at(4, "x_bf1b", [P, (E - SCALAR_COLS) * PACK], BF16)]
+        parts = (slice(0, SCALAR_COLS), slice(SCALAR_COLS, E))
+        x_w.append(at(41, "x_w1", [P, E], U32))
+        nc.scalar.copy(x_bf1[0][:].rearrange("p (m t) -> p m t", t=PACK), rows_of[1][:, parts[0]])
+        nc.gpsimd.tensor_scalar(x_bf1[1][:].rearrange("p (m t) -> p m t", t=PACK), rows_of[1][:, parts[1]], 1.0, 0.0, MULT, ADD)
+        for k in (1, 0):
+            nc.vector.quantize_mx(out=x_w[1][:, parts[k]].bitcast(FP8X4), scales=x_sc[1][:, parts[k]], in_=x_bf1[k][:])
+        quantise_w2(0, 1)
+        quantise_w2(1, 1)
 
-        banks = [psum.tile([P, BANK], F32, name="bank") for i in range(TILES)]
-        for c in range(GROUPS):
-            ahead = AHEAD if c == 0 else 0
-            for b, t in [(b, t) for b in range(GROUPS) for t in range(ahead)] + [(b, t) for t in (range(ahead, PACK) if c == 0 else (1, 0, 2, 3)) for b in (1, 0)]:
-                if True:
-                    nc.tensor.matmul_mx(
-                        out=banks[c * PACK + t][:],
-                        lhsT=w2_w[b][c][:, P * t : P * (t + 1)].bitcast(FP8X4),
-                        lhsT_scale=w2_sc[b][c][:, P * t : P * (t + 1)],
-                        rhs=x_w[b][:].bitcast(FP8X4),
-                        rhs_scale=x_sc[b][:],
-                        start=(b == 0) == (t < ahead),
-                        stop=(b == 1) == (t < ahead),
-                    )
+        banks = [bank_tile(k) for k in range(TILES)]
+
+        def pass2(c, t, b):
+            nc.tensor.matmul_mx(
+                out=banks[c * PACK + t][:],
+                lhsT=w2_w[b][c][:, P * t : P * (t + 1)].bitcast(FP8X4),
+                lhsT_scale=w2_sc[b][c][:, P * t : P * (t + 1)],
+                rhs=x_w[b][:].bitcast(FP8X4),
+                rhs_scale=x_sc[b][:],
+                start=(b == 0),
+                stop=(b == GROUPS - 1),
+            )
+
+        for b in range(GROUPS):
+            for t in range(PACK):
+                pass2(0, t, b)
+        for t in range(PACK):
+            for b in range(GROUPS):
+                pass2(1, t, b)
 
         rows = out.rearrange("(c v t e) m -> c t v e m", v=PAIRS, t=PACK, e=2)
-        summed = at(126, "summed", [P, E], F32)
         for i in range(TILES):
             c, t = divmod(i, PACK)
             factor = blend_t[:, c, 2 * t : 2 * t + 1]
-            if i < EARLY_OWN:
-                cut = E if i == 0 else 0
-                if cut:
-                    share = held(f"share{i}", [P, cut], F32)
-                    nc.scalar.activation(share[:], banks[i][:, 0:cut], COPY, scale=factor)
-                    res = summed[:, i * E : i * E + cut]
-                    nc.gpsimd.tensor_tensor(res, own[:, i, 0:cut], share[:], ADD)
-                    nc.gpsimd.dma_start(rows[c, t][:, :, 0:cut], res)
-                if cut < E:
-                    res = held(f"res{i}", [P, E - cut], F32)
-                    nc.vector.scalar_tensor_tensor(res[:], banks[i][:, cut:E], factor, own[:, i, cut:E], MULT, ADD)
-                    nc.sync.dma_start(rows[c, t][:, :, cut:E], res[:])
+            if 0 < i < PLAIN:
+                res = at(172 + 2 * i, f"res{i}", [P, E], F32)
+                nc.vector.scalar_tensor_tensor(res[:], banks[i][:], factor, own[i], MULT, ADD)
+                nc.sync.dma_start(rows[c, t], res[:])
                 continue
-            share = held(f"share{i}", [P, E], F32)
+            share = at(188 + 2 * (i % 4), f"share{i}", [P, E], F32)
             nc.scalar.activation(share[:], banks[i][:], COPY, scale=factor)
-            res = held(f"res{i}", [P, E], F32)
+            if i == 0:
+                res = at(12, "res0", [P, E], F32)
+                nc.gpsimd.tensor_tensor(res[:], own[i], share[:], ADD)
+                nc.gpsimd.dma_start(rows[c, t], res[:])
+                continue
+            res = at(172 + 2 * i, f"res{i}", [P, E], F32)
             for cols in (slice(0, E // 2), slice(E // 2, E)) if i == TILES - 1 else (slice(0, E),):
                 picks = pos2_t[:, cols.start // 16 : cols.stop // 16]
                 nc.vector.tensor_tensor(res[:, cols], h[i][:].indirect(picks), share[:, cols], ADD)

@@ -30,11 +30,10 @@ QUADS = 4
 RUN = 2 * PACK
 PAIRS = P // 2
 KB = 1024
-PLAIN = 5
+PLAIN = 6
 FIRST_PIECE = 5 * T // 16
 SECOND_PIECE = 11 * T // 16
 THIRD_PIECE = 7 * T // 16
-SCALAR_COLS = 384
 
 
 def tile_list_ring_leak_blend_kernel(
@@ -260,7 +259,7 @@ def tile_list_ring_leak_blend_kernel(
         x_w = [held("x_w0", [P, E], U32)]
 
         def quantise_w2(b, c):
-            w2_w[b][c] = at(160 + 4 * c + 2 * b, f"w2_w{b}{c}", [P, KP], U32)
+            w2_w[b][c] = at(160 + 8 * c + 2 * b, f"w2_w{b}{c}", [P, KP], U32)
             nc.vector.quantize_mx(out=w2_w[b][c][:].bitcast(FP8X4), scales=w2_sc[b][c][:], in_=w2_bf[b][c][:])
 
         quantise_w2(0, 0)
@@ -269,12 +268,12 @@ def tile_list_ring_leak_blend_kernel(
         own.append(at(0, "own_last", [P, E], F32)[:])
         gather_own(PLAIN - 1)
 
-        x_bf1 = [at(168, "x_bf1a", [P, SCALAR_COLS * PACK], BF16), at(4, "x_bf1b", [P, (E - SCALAR_COLS) * PACK], BF16)]
-        parts = (slice(0, SCALAR_COLS), slice(SCALAR_COLS, E))
+        x_bf1 = [at(168 + 2 * k, f"x_bf1{k}", [P, E // 2 * PACK], BF16) for k in range(2)]
+        parts = (slice(0, E // 2), slice(E // 2, E))
         x_w.append(at(41, "x_w1", [P, E], U32))
-        nc.scalar.copy(x_bf1[0][:].rearrange("p (m t) -> p m t", t=PACK), rows_of[1][:, parts[0]])
-        nc.gpsimd.tensor_scalar(x_bf1[1][:].rearrange("p (m t) -> p m t", t=PACK), rows_of[1][:, parts[1]], 1.0, 0.0, MULT, ADD)
-        for k in (1, 0):
+        for k in range(2):
+            nc.scalar.copy(x_bf1[k][:].rearrange("p (m t) -> p m t", t=PACK), rows_of[1][:, parts[k]])
+        for k in range(2):
             nc.vector.quantize_mx(out=x_w[1][:, parts[k]].bitcast(FP8X4), scales=x_sc[1][:, parts[k]], in_=x_bf1[k][:])
         quantise_w2(0, 1)
         quantise_w2(1, 1)

@@ -31,6 +31,7 @@ RUN = 2 * PACK
 PAIRS = P // 2
 KB = 1024
 PLAIN = 6
+AHEAD = 3
 FIRST_PIECE = 5 * T // 16
 SECOND_PIECE = 11 * T // 16
 THIRD_PIECE = 7 * T // 16
@@ -228,8 +229,8 @@ def tile_list_ring_leak_blend_kernel(
 
         up = [at(128 + 2 * i, f"up{i}", [P, E], F32) for i in range(TILES)]
         own = [at(80 + 2 * i, f"own{i}", [P, E], F32)[:] for i in range(2)]
-        own_rest = at(84, "own_rest", [P, PLAIN - 3, E], F32)
-        own.extend(own_rest[:, i, :] for i in range(PLAIN - 3))
+        own_rest = at(84, "own_rest", [P, PLAIN - 2, E], F32)
+        own.extend(own_rest[:, i, :] for i in range(PLAIN - 2))
 
         def gather_own(i):
             nc.vector.tensor_copy(own[i], h[i][:].indirect(pos2_t[:]))
@@ -238,7 +239,7 @@ def tile_list_ring_leak_blend_kernel(
             nc.vector.tensor_copy(up[i][:], h[i][:].indirect(pos1_t[:]))
             if i >= 5:
                 gather_own(i - 5)
-        for i in range(3, PLAIN - 1):
+        for i in range(3, PLAIN):
             gather_own(i)
 
         sig = [at(144 + 2 * i, f"sig{i}", [P, E], F32) for i in range(TILES)]
@@ -265,8 +266,6 @@ def tile_list_ring_leak_blend_kernel(
         quantise_w2(0, 0)
         nc.vector.quantize_mx(out=x_w[0][:].bitcast(FP8X4), scales=x_sc[0][:], in_=x_bf0[:])
         quantise_w2(1, 0)
-        own.append(at(0, "own_last", [P, E], F32)[:])
-        gather_own(PLAIN - 1)
 
         x_bf1 = [at(168 + 2 * k, f"x_bf1{k}", [P, E // 2 * PACK], BF16) for k in range(2)]
         parts = (slice(0, E // 2), slice(E // 2, E))
@@ -280,23 +279,23 @@ def tile_list_ring_leak_blend_kernel(
 
         banks = [bank_tile(k) for k in range(TILES)]
 
-        def pass2(c, t, b):
+        def pass2(c, t, b, opens):
             nc.tensor.matmul_mx(
                 out=banks[c * PACK + t][:],
                 lhsT=w2_w[b][c][:, P * t : P * (t + 1)].bitcast(FP8X4),
                 lhsT_scale=w2_sc[b][c][:, P * t : P * (t + 1)],
                 rhs=x_w[b][:].bitcast(FP8X4),
                 rhs_scale=x_sc[b][:],
-                start=(b == 0),
-                stop=(b == GROUPS - 1),
+                start=opens,
+                stop=not opens,
             )
 
         for b in range(GROUPS):
-            for t in range(PACK):
-                pass2(0, t, b)
-        for t in range(PACK):
-            for b in range(GROUPS):
-                pass2(1, t, b)
+            for t in range(AHEAD):
+                pass2(0, t, b, b == 0)
+        for i in range(AHEAD, TILES):
+            for b in (1, 0):
+                pass2(i // PACK, i % PACK, b, b == 1)
 
         rows = out.rearrange("(c v t e) m -> c t v e m", v=PAIRS, t=PACK, e=2)
         for i in range(TILES):

@@ -30,11 +30,9 @@ QUADS = 4
 RUN = 2 * PACK
 PAIRS = P // 2
 KB = 1024
-PLAIN = 6
-AHEAD = 3
+PLAIN = 4
+SLOT = S + KP
 FIRST_PIECE = 5 * T // 16
-SECOND_PIECE = 11 * T // 16
-THIRD_PIECE = 7 * T // 16
 
 
 def tile_list_ring_leak_blend_kernel(
@@ -60,23 +58,24 @@ def tile_list_ring_leak_blend_kernel(
         pos1_t = lists.tile([P, E // 16], U16, name="pos1_t")
         pos2_t = lists.tile([P, E // 16], U16, name="pos2_t")
 
+        tab_sc = [held("tab_sc0", [P, T // 4], I32), at(52, "tab_sc1", [P, T // 4], I32)]
         early_sc = held("early_sc", [P, 2 * KP // 4], I32)
-        tab_sc = held("tab_sc", [P, T // 4], I32)
         late_sc = at(60, "late_sc", [P, 4 * KP // 4], I32)
-        early_planes = held("early_planes", [P, (S + 2 * KP) // 4], I32)
-        mid_plane = held("mid_plane", [P, S // 4], I32)
-        late_planes = held("late_planes", [P, (S + 4 * KP) // 4], I32)
-        for tile in (early_sc, tab_sc, late_sc, early_planes, mid_plane, late_planes):
+        early_planes = held("early_planes", [P, 2 * SLOT // 4], I32)
+        late_planes = held("late_planes", [P, 2 * SLOT // 4], I32)
+        for tile in (early_sc, tab_sc[0]):
+            nc.vector.memset(tile[:, 0:1], 0)
+            nc.vector.memset(tile[:, 1:], 0)
+        nc.gpsimd.memset(tab_sc[1][:], 0)
+        for tile in (late_sc, early_planes, late_planes):
             nc.vector.memset(tile[:], 0)
         warm_in = held("warm_in", [P, 1], F32)
         warm_out = held("warm_out", [P, 1], F32)
         nc.vector.memset(warm_in[:], 0.0)
         nc.scalar.activation(warm_out[:], warm_in[:], SIGMOID)
 
-        tab_w = [at((0, 16, 33)[a], f"tab_w{a}", [P, T], I32) for a in range(PASSES1)]
+        tab_w = [at(16 * a, f"tab_w{a}", [P, T], I32) for a in range(PASSES1 - 1)]
         w4_raw = [at(64, "w4_raw0", [P, PASSES1 * KP // 2], I32)]
-        blend_t = held("blend_t", [P, GROUPS, RUN], F32)
-        gain_t = held("gain_t", [P, GROUPS, RUN], F32)
 
         def load_w4(b):
             nc.sync.dma_start(
@@ -84,9 +83,10 @@ def tile_list_ring_leak_blend_kernel(
                 w4_words.bitcast(I32)[:, :, b * KP // 2 : (b + 1) * KP // 2].rearrange("a p c -> p a c"),
             )
 
-        def load_factors(tile, factors, e):
+        def load_factors(tile, factors):
             runs = factors.rearrange("(b v k) -> v b k", b=GROUPS, k=RUN)
-            nc.sync.dma_start(tile[e:P:2, :, 0 : RUN - 1], runs[:, :, e : e + RUN - 1])
+            for e in range(2):
+                nc.sync.dma_start(tile[e:P:2, :, 0 : RUN - 1], runs[:, :, e : e + RUN - 1])
 
         def load_table(a, cols):
             nc.sync.dma_start(tab_w[a][:, cols], tab_words[a].rearrange("p t i -> p (t i)").bitcast(I32)[:, cols])
@@ -97,43 +97,43 @@ def tile_list_ring_leak_blend_kernel(
 
         def order_scales(dst, src):
             nc.vector.tensor_copy(
-                dst.bitcast(U16).rearrange("p (g t v) -> p g t v", t=PACK, v=PAIRS),
+                dst.bitcast(U16).rearrange("p g (t v) -> p g t v", t=PACK),
                 src[:].bitcast(U16).rearrange("p (g v t) -> p g t v", t=PACK, v=PAIRS),
             )
 
         nc.sync.dma_start(offs_t[:], offs)
         nc.sync.dma_start(pos1_t[:], pos1)
         load_table(0, slice(0, FIRST_PIECE))
-        load_factors(gain_t, gain, 0)
+        nc.sync.dma_start(pos2_t[:], pos2)
         w4_sc_rows = w4_scales.bitcast(I32).rearrange("a j c -> j a c")
         nc.sync.dma_start(early_sc[5:P:8].rearrange("j (a c) -> j a c", a=2), w4_sc_rows[:, 0:2, 0 : KP // 4])
-        for a in range(PASSES1):
-            nc.sync.dma_start(tab_sc[5 + a : P : 8, :], tab_scales.bitcast(I32)[a])
+        for a, tile, first_row in ((0, tab_sc[0], 5), (2, tab_sc[0], 6), (1, tab_sc[1], 5)):
+            nc.sync.dma_start(tile[first_row:P:8, :], tab_scales.bitcast(I32)[a])
         load_table(0, slice(FIRST_PIECE, T))
+        nc.sync.dma_start(late_sc[6:P:8, 0 : H // 4], w4_sc_rows[:, 2])
+        nc.sync.dma_start(late_sc[6:P:8, H // 4 :].rearrange("j (a c) -> j a c", a=2), w4_sc_rows[:, 0:2, KP // 4 :])
         load_w4(0)
-        nc.sync.dma_start(late_sc[7:P:8, 0 : H // 4], w4_sc_rows[:, 2])
-        nc.sync.dma_start(late_sc[7:P:8, H // 4 :].rearrange("j (a c) -> j a c", a=2), w4_sc_rows[:, 0:2, KP // 4 :])
-        load_factors(gain_t, gain, 1)
-        for e in range(2):
-            load_factors(blend_t, blend, e)
-        load_table(1, slice(0, SECOND_PIECE))
+        load_table(1, slice(0, T))
 
-        early_rows = held("early_rows", [P, (S + 2 * KP) // 4], I32)
-        picked = held("picked", [P, S // 4], I32)
-        order_scales(early_rows[:, S // 4 :], early_sc)
-        nc.vector.tensor_copy(picked[:].bitcast(U8), tab_sc[:].bitcast(U8).indirect(offs_t[:]))
-        nc.vector.tensor_copy(early_rows[:, 0 : S // 4], picked[:])
+        early_rows = held("early_rows", [P, 2 * SLOT // 4], I32)
+        early_slots = early_rows[:].rearrange("p (a c) -> p a c", a=2)
+        order_scales(early_slots[:, :, S // 4 :], early_sc)
+        picked = [held("picked0", [P, S // 4], I32), at(33, "picked1", [P, S // 4], I32)]
+        for a in range(2):
+            nc.vector.tensor_copy(picked[a][:].bitcast(U8), tab_sc[a][:].bitcast(U8).indirect(offs_t[:]))
+            nc.vector.tensor_copy(early_slots[:, a, 0 : S // 4], picked[a][:])
+        blend_t = at(52, "blend_t", [P, GROUPS, RUN], F32)
+        load_factors(blend_t, blend)
         move_rows(early_planes, early_rows, 5)
-        load_table(1, slice(SECOND_PIECE, T))
-        load_table(2, slice(0, THIRD_PIECE))
-        move_rows(mid_plane, picked, 6)
-        load_table(2, slice(THIRD_PIECE, T))
+        tab_w.append(at(33, "tab_w2", [P, T], I32))
+        load_table(2, slice(0, T))
 
         v_w = [[at(68 + 2 * (HALVES * a + s), f"v_w{a}{s}", [P, BANK], U32) for s in range(HALVES)] for a in range(PASSES1)]
 
-        def gather_words(a, s):
-            cols = slice(s * BANK // 16, (s + 1) * BANK // 16)
-            nc.vector.tensor_copy(v_w[a][s][:], tab_w[a][:].bitcast(U32).indirect(offs_t[:, cols]))
+        def gather_words(a):
+            for s in range(HALVES):
+                cols = slice(s * BANK // 16, (s + 1) * BANK // 16)
+                nc.vector.tensor_copy(v_w[a][s][:], tab_w[a][:].bitcast(U32).indirect(offs_t[:, cols]))
 
         tile_bytes = PASSES1 * 2 * P
 
@@ -144,46 +144,42 @@ def tile_list_ring_leak_blend_kernel(
             )
 
         w4_w = [held("w4_w0", [P, PACK * tile_bytes], U8)]
-        gather_words(0, 0)
         order_words(w4_w[0], w4_raw[0])
-        gather_words(0, 1)
-        late_rows = held("late_rows", [P, (S + 4 * KP) // 4], I32)
-        nc.vector.tensor_copy(late_rows[:, 0 : S // 4], picked[:])
-        order_scales(late_rows[:, S // 4 :], late_sc)
-        move_rows(late_planes, late_rows, 7)
+        gather_words(0)
+        late_rows = at(64, "late_rows", [P, 2 * SLOT // 4], I32)
+        nc.vector.tensor_copy(late_rows[:, 0 : S // 4], picked[0][:])
+        order_scales(late_rows[:, S // 4 :].rearrange("p (g c) -> p g c", g=4), late_sc)
+        move_rows(late_planes, late_rows, 6)
         early_bytes, late_bytes = early_planes[:].bitcast(U8), late_planes[:].bitcast(U8)
-        v_planes = [early_bytes[:, 0:S], mid_plane[:].bitcast(U8), late_bytes[:, 0:S]]
+        v_planes = [early_bytes[:, 0:S], early_bytes[:, SLOT : SLOT + S], late_bytes[:, 0:S]]
         late_w4 = [late_bytes[:, S + KP * g : S + KP * (g + 1)] for g in range(4)]
-        w4_planes = [
-            [early_bytes[:, S : S + KP], early_bytes[:, S + KP :], late_w4[0]],
-            [late_w4[2], late_w4[3], late_w4[1]],
-        ]
-        w4_raw.append(at(60, "w4_raw1", [P, PASSES1 * KP // 2], I32))
+        w4_planes = [[early_bytes[:, S:SLOT], early_bytes[:, SLOT + S :], late_w4[0]], [late_w4[2], late_w4[3], late_w4[1]]]
+        w4_raw.append(at(60 + 1 / 16, "w4_raw1", [P, PASSES1 * KP // 2], I32))
         load_w4(1)
 
         keep_all = held("keep_all", [P, TILES], F32)
         nc.scalar.activation(keep_all[:].rearrange("p (b t) -> p b t", b=GROUPS), blend_t[:, :, 0 : RUN - 1 : 2], COPY, scale=-1.0, bias=1.0)
         gate = {}
-        for i, kb in ((5, 80), (6, 82), (7, 84)):
+        for i, kb in ((6, 80), (7, 84)):
             gate[i] = at(kb, f"keep_gate{i}", [P, 1], F32)
             nc.scalar.activation(gate[i][:, 0:1], blend_t[:, i // PACK, 2 * (i % PACK) : 2 * (i % PACK) + 1], COPY, scale=-1.0, bias=1.0)
-        undo_t = at(64, "undo_t", [P, TILES], F32)
+        undo_t = at(60, "undo_t", [P, TILES], F32)
         nc.vector.reciprocal(undo_t[:], keep_all[:])
 
         for a in range(1, PASSES1):
-            for s in range(HALVES):
-                gather_words(a, s)
+            gather_words(a)
         w4_w.append(at(49 - 1 / 16, "w4_w1", [P, PACK * tile_bytes], U8))
         order_words(w4_w[1], w4_raw[1])
 
-        w2_raw = [[at((16, 24, 32.5, 40.5)[2 * c + b], f"w2_raw{b}{c}", [P, PACK, KP], F32) for c in range(GROUPS)] for b in range(GROUPS)]
+        w2_raw = [[at((16, 24 + 1 / 16, 32.5, 40.5)[2 * c + b], f"w2_raw{b}{c}", [P, PACK, KP], F32) for c in range(GROUPS)] for b in range(GROUPS)]
+        gain_t = at(24, "gain_t", [P, GROUPS, RUN], F32)
         for c in range(GROUPS):
             for b in range(GROUPS):
                 block = w2[b * KP : (b + 1) * KP, c * KP : (c + 1) * KP].rearrange("(v j e) n -> e v j n", j=PACK, e=2)
                 for e in range(2):
                     nc.sync.dma_start(w2_raw[b][c][e:P:2], block[e])
-            if c == 0:
-                nc.sync.dma_start(pos2_t[:], pos2)
+                if (b, c) == (0, 0):
+                    load_factors(gain_t, gain)
 
         def pass1(bank, i, s, a):
             first_byte = tile_bytes * (i % PACK) + 2 * P * a
@@ -214,88 +210,115 @@ def tile_list_ring_leak_blend_kernel(
         emptied = [(0, 0), (1, 0), (2, 0), (0, 1), (1, 1), (2, 1), (3, 0), (3, 1)]
         for i, s in emptied:
             empty(first[i, s], i, s)
-        for k, (i, s) in enumerate(emptied):
-            bank = bank_tile(PACK * s + i)
-            for a in range(PASSES1):
-                pass1(bank, PACK + k // HALVES, k % HALVES, a)
-            empty(bank, PACK + k // HALVES, k % HALVES)
 
-        w2_bf = [[at(4 * (GROUPS * c + b), f"w2_bf{b}{c}", [P, PACK * KP], BF16) for c in range(GROUPS)] for b in range(GROUPS)]
-        for c in range(GROUPS):
-            for b in range(GROUPS):
-                rounded = w2_bf[b][c][:].rearrange("p (t v e j) -> p v t e j", t=PACK, e=2, j=PACK)
-                raw = w2_raw[b][c][:].rearrange("p j (v t e) -> p v t e j", t=PACK, e=2)
-                nc.gpsimd.tensor_scalar(rounded, raw, 1.0, 0.0, MULT, ADD)
+        def second_group(i):
+            for s in range(HALVES):
+                was_i, was_s = emptied[HALVES * (i - PACK) + s]
+                bank = bank_tile(PACK * was_s + was_i)
+                for a in range(PASSES1):
+                    pass1(bank, i, s, a)
+                empty(bank, i, s)
+
+        def round_w2(dst, b, c, tiles):
+            rounded = dst[:].rearrange("p (t v e j) -> p v t e j", v=PAIRS, e=2, j=PACK)
+            raw = w2_raw[b][c][:].rearrange("p j (v t e) -> p v t e j", t=PACK, e=2)
+            nc.gpsimd.tensor_scalar(rounded, raw[:, :, tiles], 1.0, 0.0, MULT, ADD)
+
+        w2_bf = {(b, c): at(4 * (GROUPS * c + b), f"w2_bf{b}{c}", [P, PACK * KP], BF16) for b, c in ((0, 0), (1, 0), (0, 1))}
+        for b, c in w2_bf:
+            round_w2(w2_bf[b, c], b, c, slice(0, PACK))
+        last_bf = [at(12, "last_bf0", [P, 2 * KP], BF16)]
+        round_w2(last_bf[0], 1, 1, slice(0, 2))
 
         up = [at(128 + 2 * i, f"up{i}", [P, E], F32) for i in range(TILES)]
-        own = [at(80 + 2 * i, f"own{i}", [P, E], F32)[:] for i in range(2)]
-        own_rest = at(84, "own_rest", [P, PLAIN - 2, E], F32)
-        own.extend(own_rest[:, i, :] for i in range(PLAIN - 2))
-
-        def gather_own(i):
-            nc.vector.tensor_copy(own[i], h[i][:].indirect(pos2_t[:]))
-
-        for i in range(TILES):
-            nc.vector.tensor_copy(up[i][:], h[i][:].indirect(pos1_t[:]))
-            if i >= 5:
-                gather_own(i - 5)
-        for i in range(3, PLAIN):
-            gather_own(i)
-
         sig = [at(144 + 2 * i, f"sig{i}", [P, E], F32) for i in range(TILES)]
-        x_rows = [at(160 + 4 * b, f"x_rows{b}", [P, PACK * E], BF16) for b in range(GROUPS)]
-        for b in range(GROUPS):
-            for t in range(PACK):
-                i = b * PACK + t
-                nc.scalar.activation(sig[i][:], up[i][:], SIGMOID, scale=undo_t[:, i : i + 1])
-            for t in range(PACK):
-                nc.scalar.activation(x_rows[b][:, t * E : (t + 1) * E], sig[b * PACK + t][:], COPY, scale=gain_t[:, b, 2 * t : 2 * t + 1])
+        x_rows = [at((91, 160)[b], f"x_rows{b}", [P, PACK * E], BF16) for b in range(GROUPS)]
+        own = []
+
+        def gather_up(i):
+            nc.vector.tensor_copy(up[i][:], h[i][:].indirect(pos1_t[:]))
+
+        def gather_own(dst):
+            nc.vector.tensor_copy(dst, h[len(own)][:].indirect(pos2_t[:]))
+            own.append(dst)
+
+        def sigmoid(i):
+            nc.scalar.activation(sig[i][:], up[i][:], SIGMOID, scale=undo_t[:, i : i + 1])
+
+        def apply_gain(i):
+            b, t = divmod(i, PACK)
+            nc.scalar.activation(x_rows[b][:, t * E : (t + 1) * E], sig[i][:], COPY, scale=gain_t[:, b, 2 * t : 2 * t + 1])
+
+        for i in range(PACK):
+            gather_up(i)
+        for i in (4, 5):
+            second_group(i)
+            gather_up(i)
+            sigmoid(2 * (i - PACK))
+            sigmoid(2 * (i - PACK) + 1)
+        second_group(6)
+        gather_up(6)
+        own_pair = at(80, "own_pair", [P, 2, E], F32)
+        for k in range(2):
+            gather_own(own_pair[:, k, :])
+        for i in range(PACK):
+            apply_gain(i)
+        second_group(7)
+        gather_up(7)
+        gather_own(at(84, "own2", [P, E], F32)[:])
+        for pair in ((4, 5), (6, 7)):
+            for i in pair:
+                sigmoid(i)
+            for i in pair:
+                apply_gain(i)
+
         rows_of = [x_rows[b][:].rearrange("p (t m) -> p m t", t=PACK) for b in range(GROUPS)]
-        x_bf0 = at(41, "x_bf0", [P, E * PACK], BF16)
+        x_bf0 = at(33, "x_bf0", [P, E * PACK], BF16)
         nc.gpsimd.tensor_scalar(x_bf0[:].rearrange("p (m t) -> p m t", t=PACK), rows_of[0], 1.0, 0.0, MULT, ADD)
 
-        w2_sc = [[held(f"w2_sc{b}{c}", [P, KP], U8) for c in range(GROUPS)] for b in range(GROUPS)]
-        w2_w = [[None] * GROUPS for b in range(GROUPS)]
+        w2_sc, w2_w = {}, {}
         x_sc = [held(f"x_sc{b}", [P, E], U8) for b in range(GROUPS)]
         x_w = [held("x_w0", [P, E], U32)]
 
-        def quantise_w2(b, c):
-            w2_w[b][c] = at(160 + 8 * c + 2 * b, f"w2_w{b}{c}", [P, KP], U32)
-            nc.vector.quantize_mx(out=w2_w[b][c][:].bitcast(FP8X4), scales=w2_sc[b][c][:], in_=w2_bf[b][c][:])
+        def quantise_w2(kb, src, b, c, tiles):
+            words = at(kb, f"w2_w{b}{c}{tiles[0]}", [P, P * len(tiles)], U32)
+            scales = held(f"w2_sc{b}{c}{tiles[0]}", [P, P * len(tiles)], U8)
+            nc.vector.quantize_mx(out=words[:].bitcast(FP8X4), scales=scales[:], in_=src[:])
+            for k, t in enumerate(tiles):
+                w2_w[b, c, t] = words[:, P * k : P * (k + 1)]
+                w2_sc[b, c, t] = scales[:, P * k : P * (k + 1)]
 
-        quantise_w2(0, 0)
+        quantise_w2(90, w2_bf[0, 0], 0, 0, range(PACK))
         nc.vector.quantize_mx(out=x_w[0][:].bitcast(FP8X4), scales=x_sc[0][:], in_=x_bf0[:])
-        quantise_w2(1, 0)
+        quantise_w2(92, w2_bf[1, 0], 1, 0, range(PACK))
+        quantise_w2(94, w2_bf[0, 1], 0, 1, range(PACK))
+        quantise_w2(2, last_bf[0], 1, 1, range(2))
+        gather_own(at(0, "own3", [P, E], F32)[:])
+        last_bf.append(at(12, "last_bf1", [P, 2 * KP], BF16))
+        round_w2(last_bf[1], 1, 1, slice(2, PACK))
 
-        x_bf1 = [at(168 + 2 * k, f"x_bf1{k}", [P, E // 2 * PACK], BF16) for k in range(2)]
+        x_bf1 = [at(164 + 2 * k, f"x_bf1{k}", [P, E // 2 * PACK], BF16) for k in range(2)]
         parts = (slice(0, E // 2), slice(E // 2, E))
-        x_w.append(at(41, "x_w1", [P, E], U32))
+        x_w.append(at(33, "x_w1", [P, E], U32))
         for k in range(2):
             nc.scalar.copy(x_bf1[k][:].rearrange("p (m t) -> p m t", t=PACK), rows_of[1][:, parts[k]])
         for k in range(2):
             nc.vector.quantize_mx(out=x_w[1][:, parts[k]].bitcast(FP8X4), scales=x_sc[1][:, parts[k]], in_=x_bf1[k][:])
-        quantise_w2(0, 1)
-        quantise_w2(1, 1)
+        quantise_w2(164, last_bf[1], 1, 1, range(2, PACK))
 
         banks = [bank_tile(k) for k in range(TILES)]
-
-        def pass2(c, t, b, opens):
-            nc.tensor.matmul_mx(
-                out=banks[c * PACK + t][:],
-                lhsT=w2_w[b][c][:, P * t : P * (t + 1)].bitcast(FP8X4),
-                lhsT_scale=w2_sc[b][c][:, P * t : P * (t + 1)],
-                rhs=x_w[b][:].bitcast(FP8X4),
-                rhs_scale=x_sc[b][:],
-                start=opens,
-                stop=not opens,
-            )
-
         for b in range(GROUPS):
-            for t in range(AHEAD):
-                pass2(0, t, b, b == 0)
-        for i in range(AHEAD, TILES):
-            for b in (1, 0):
-                pass2(i // PACK, i % PACK, b, b == 1)
+            for i in range(TILES):
+                c, t = divmod(i, PACK)
+                nc.tensor.matmul_mx(
+                    out=banks[i][:],
+                    lhsT=w2_w[b, c, t].bitcast(FP8X4),
+                    lhsT_scale=w2_sc[b, c, t],
+                    rhs=x_w[b][:].bitcast(FP8X4),
+                    rhs_scale=x_sc[b][:],
+                    start=(b == 0),
+                    stop=(b == GROUPS - 1),
+                )
 
         rows = out.rearrange("(c v t e) m -> c t v e m", v=PAIRS, t=PACK, e=2)
         for i in range(TILES):
@@ -306,7 +329,7 @@ def tile_list_ring_leak_blend_kernel(
                 nc.vector.scalar_tensor_tensor(res[:], banks[i][:], factor, own[i], MULT, ADD)
                 nc.sync.dma_start(rows[c, t], res[:])
                 continue
-            share = at(188 + 2 * (i % 4), f"share{i}", [P, E], F32)
+            share = at(188 + 2 * max(0, i - PLAIN + 1), f"share{i}", [P, E], F32)
             nc.scalar.activation(share[:], banks[i][:], COPY, scale=factor)
             if i == 0:
                 res = at(12, "res0", [P, E], F32)

@@ -30,7 +30,9 @@ QUADS = 4
 RUN = 2 * PACK
 PAIRS = P // 2
 KB = 1024
-PLAIN = 4
+PLAIN = 5
+AHEAD = 3
+SUMMED = 1
 SLOT = S + KP
 FIRST_PIECE = 5 * T // 16
 
@@ -58,7 +60,7 @@ def tile_list_ring_leak_blend_kernel(
         pos1_t = lists.tile([P, E // 16], U16, name="pos1_t")
         pos2_t = lists.tile([P, E // 16], U16, name="pos2_t")
 
-        tab_sc = [held("tab_sc0", [P, T // 4], I32), at(52, "tab_sc1", [P, T // 4], I32)]
+        tab_sc = [held("tab_sc0", [P, T // 4], I32), at(56, "tab_sc1", [P, T // 4], I32)]
         early_sc = held("early_sc", [P, 2 * KP // 4], I32)
         late_sc = at(60, "late_sc", [P, 4 * KP // 4], I32)
         early_planes = held("early_planes", [P, 2 * SLOT // 4], I32)
@@ -75,13 +77,14 @@ def tile_list_ring_leak_blend_kernel(
         nc.scalar.activation(warm_out[:], warm_in[:], SIGMOID)
 
         tab_w = [at(16 * a, f"tab_w{a}", [P, T], I32) for a in range(PASSES1 - 1)]
-        w4_raw = [at(64, "w4_raw0", [P, PASSES1 * KP // 2], I32)]
 
-        def load_w4(b):
+        def load_w4(kb, b, passes):
+            raw = at(kb, f"w4_raw{b}{passes.start}", [P, (passes.stop - passes.start) * KP // 2], I32)
             nc.sync.dma_start(
-                w4_raw[b][:].rearrange("p (a c) -> p a c", a=PASSES1),
-                w4_words.bitcast(I32)[:, :, b * KP // 2 : (b + 1) * KP // 2].rearrange("a p c -> p a c"),
+                raw[:].rearrange("p (a c) -> p a c", c=KP // 2),
+                w4_words.bitcast(I32)[passes, :, b * KP // 2 : (b + 1) * KP // 2].rearrange("a p c -> p a c"),
             )
+            return raw
 
         def load_factors(tile, factors):
             runs = factors.rearrange("(b v k) -> v b k", b=GROUPS, k=RUN)
@@ -112,39 +115,43 @@ def tile_list_ring_leak_blend_kernel(
         load_table(0, slice(FIRST_PIECE, T))
         nc.sync.dma_start(late_sc[6:P:8, 0 : H // 4], w4_sc_rows[:, 2])
         nc.sync.dma_start(late_sc[6:P:8, H // 4 :].rearrange("j (a c) -> j a c", a=2), w4_sc_rows[:, 0:2, KP // 4 :])
-        load_w4(0)
+        w4_first = load_w4(64, 0, slice(0, 1))
         load_table(1, slice(0, T))
 
         early_rows = held("early_rows", [P, 2 * SLOT // 4], I32)
         early_slots = early_rows[:].rearrange("p (a c) -> p a c", a=2)
         order_scales(early_slots[:, :, S // 4 :], early_sc)
-        picked = [held("picked0", [P, S // 4], I32), at(33, "picked1", [P, S // 4], I32)]
+        picked = [held("picked0", [P, S // 4], I32), at(35.25, "picked1", [P, S // 4], I32)]
         for a in range(2):
             nc.vector.tensor_copy(picked[a][:].bitcast(U8), tab_sc[a][:].bitcast(U8).indirect(offs_t[:]))
             nc.vector.tensor_copy(early_slots[:, a, 0 : S // 4], picked[a][:])
-        blend_t = at(52, "blend_t", [P, GROUPS, RUN], F32)
-        load_factors(blend_t, blend)
         move_rows(early_planes, early_rows, 5)
-        tab_w.append(at(33, "tab_w2", [P, T], I32))
+        w4_rest = load_w4(56, 0, slice(1, PASSES1))
+        tab_w.append(at(36, "tab_w2", [P, T], I32))
         load_table(2, slice(0, T))
+        blend_t = at(35.5, "blend_t", [P, GROUPS, RUN], F32)
+        load_factors(blend_t, blend)
 
-        v_w = [[at(68 + 2 * (HALVES * a + s), f"v_w{a}{s}", [P, BANK], U32) for s in range(HALVES)] for a in range(PASSES1)]
+        v_w = [[at(55 + 2 * s if a == 2 else 68 + 2 * (HALVES * a + s), f"v_w{a}{s}", [P, BANK], U32) for s in range(HALVES)] for a in range(PASSES1)]
 
         def gather_words(a):
             for s in range(HALVES):
                 cols = slice(s * BANK // 16, (s + 1) * BANK // 16)
                 nc.vector.tensor_copy(v_w[a][s][:], tab_w[a][:].bitcast(U32).indirect(offs_t[:, cols]))
 
-        tile_bytes = PASSES1 * 2 * P
+        w4_w = {}
 
-        def order_words(dst, src):
+        def order_words(dst, src, b, passes):
             nc.vector.tensor_copy(
-                dst[:].bitcast(I32).rearrange("p (t c i) -> p c t i", t=PACK, i=4),
+                dst[:].rearrange("p (t c i) -> p c t i", t=PACK, i=4),
                 src[:].rearrange("p (c i t) -> p c t i", t=PACK, i=4),
             )
+            for t in range(PACK):
+                for k, a in enumerate(passes):
+                    first_word = PAIRS * (len(passes) * t + k)
+                    w4_w[PACK * b + t, a] = dst[:, first_word : first_word + PAIRS].bitcast(U8)
 
-        w4_w = [held("w4_w0", [P, PACK * tile_bytes], U8)]
-        order_words(w4_w[0], w4_raw[0])
+        order_words(held("w4_w0", [P, PACK * PAIRS], I32), w4_first, 0, range(1))
         gather_words(0)
         late_rows = at(64, "late_rows", [P, 2 * SLOT // 4], I32)
         nc.vector.tensor_copy(late_rows[:, 0 : S // 4], picked[0][:])
@@ -154,38 +161,38 @@ def tile_list_ring_leak_blend_kernel(
         v_planes = [early_bytes[:, 0:S], early_bytes[:, SLOT : SLOT + S], late_bytes[:, 0:S]]
         late_w4 = [late_bytes[:, S + KP * g : S + KP * (g + 1)] for g in range(4)]
         w4_planes = [[early_bytes[:, S:SLOT], early_bytes[:, SLOT + S :], late_w4[0]], [late_w4[2], late_w4[3], late_w4[1]]]
-        w4_raw.append(at(60 + 1 / 16, "w4_raw1", [P, PASSES1 * KP // 2], I32))
-        load_w4(1)
+        w4_second = load_w4(60, 1, slice(0, PASSES1))
+        order_words(held("w4_w1", [P, 2 * PACK * PAIRS], I32), w4_rest, 0, range(1, PASSES1))
 
         keep_all = held("keep_all", [P, TILES], F32)
         nc.scalar.activation(keep_all[:].rearrange("p (b t) -> p b t", b=GROUPS), blend_t[:, :, 0 : RUN - 1 : 2], COPY, scale=-1.0, bias=1.0)
         gate = {}
-        for i, kb in ((6, 80), (7, 84)):
+        for i, kb in ((5, 80), (6, 82), (7, 86)):
             gate[i] = at(kb, f"keep_gate{i}", [P, 1], F32)
             nc.scalar.activation(gate[i][:, 0:1], blend_t[:, i // PACK, 2 * (i % PACK) : 2 * (i % PACK) + 1], COPY, scale=-1.0, bias=1.0)
-        undo_t = at(60, "undo_t", [P, TILES], F32)
-        nc.vector.reciprocal(undo_t[:], keep_all[:])
 
         for a in range(1, PASSES1):
             gather_words(a)
-        w4_w.append(at(49 - 1 / 16, "w4_w1", [P, PACK * tile_bytes], U8))
-        order_words(w4_w[1], w4_raw[1])
+        order_words(at(52 - 1 / 16, "w4_w2", [P, PASSES1 * PACK * PAIRS], I32), w4_second, 1, range(PASSES1))
+        undo_t = at(61, "undo_t", [P, TILES], F32)
+        nc.vector.reciprocal(undo_t[:], keep_all[:])
 
-        w2_raw = [[at((16, 24 + 1 / 16, 32.5, 40.5)[2 * c + b], f"w2_raw{b}{c}", [P, PACK, KP], F32) for c in range(GROUPS)] for b in range(GROUPS)]
+        pieces = [(b, c, slice(0, PAIRS)) for c in range(GROUPS) for b in range(GROUPS)]
+        w2_raw = []
         gain_t = at(24, "gain_t", [P, GROUPS, RUN], F32)
-        for c in range(GROUPS):
-            for b in range(GROUPS):
-                block = w2[b * KP : (b + 1) * KP, c * KP : (c + 1) * KP].rearrange("(v j e) n -> e v j n", j=PACK, e=2)
-                for e in range(2):
-                    nc.sync.dma_start(w2_raw[b][c][e:P:2], block[e])
-                if (b, c) == (0, 0):
-                    load_factors(gain_t, gain)
+        for k, (b, c, vs) in enumerate(pieces):
+            cols = slice(c * KP + RUN * vs.start, c * KP + RUN * vs.stop)
+            w2_raw.append(at((16, 24 + 1 / 16, 35.625, 43.625)[k], f"w2_raw{k}", [P, PACK, cols.stop - cols.start], F32))
+            block = w2[b * KP : (b + 1) * KP, cols].rearrange("(v j e) n -> e v j n", j=PACK, e=2)
+            for e in range(2):
+                nc.sync.dma_start(w2_raw[k][e:P:2], block[e])
+            if k == 0:
+                load_factors(gain_t, gain)
 
         def pass1(bank, i, s, a):
-            first_byte = tile_bytes * (i % PACK) + 2 * P * a
             nc.tensor.matmul_mx(
                 out=bank[:],
-                lhsT=w4_w[i // PACK][:, first_byte : first_byte + 2 * P].bitcast(FP4X4),
+                lhsT=w4_w[i, a].bitcast(FP4X4),
                 lhsT_scale=w4_planes[i // PACK][a][:, P * (i % PACK) : P * (i % PACK + 1)],
                 rhs=v_w[a][s][:].bitcast(FP8X4),
                 rhs_scale=v_planes[a][:, s * BANK : (s + 1) * BANK],
@@ -219,16 +226,11 @@ def tile_list_ring_leak_blend_kernel(
                     pass1(bank, i, s, a)
                 empty(bank, i, s)
 
-        def round_w2(dst, b, c, tiles):
-            rounded = dst[:].rearrange("p (t v e j) -> p v t e j", v=PAIRS, e=2, j=PACK)
-            raw = w2_raw[b][c][:].rearrange("p j (v t e) -> p v t e j", t=PACK, e=2)
-            nc.gpsimd.tensor_scalar(rounded, raw[:, :, tiles], 1.0, 0.0, MULT, ADD)
-
-        w2_bf = {(b, c): at(4 * (GROUPS * c + b), f"w2_bf{b}{c}", [P, PACK * KP], BF16) for b, c in ((0, 0), (1, 0), (0, 1))}
-        for b, c in w2_bf:
-            round_w2(w2_bf[b, c], b, c, slice(0, PACK))
-        last_bf = [at(12, "last_bf0", [P, 2 * KP], BF16)]
-        round_w2(last_bf[0], 1, 1, slice(0, 2))
+        w2_bf = {(b, c): at(4 * (GROUPS * c + b), f"w2_bf{b}{c}", [P, PACK * KP], BF16) for c in range(GROUPS) for b in range(GROUPS)}
+        for k, (b, c, vs) in enumerate(pieces):
+            rounded = w2_bf[b, c][:].rearrange("p (t v e j) -> p v t e j", v=PAIRS, e=2, j=PACK)
+            raw = w2_raw[k][:].rearrange("p j (v t e) -> p v t e j", t=PACK, e=2)
+            nc.gpsimd.tensor_scalar(rounded[:, vs], raw, 1.0, 0.0, MULT, ADD)
 
         up = [at(128 + 2 * i, f"up{i}", [P, E], F32) for i in range(TILES)]
         sig = [at(144 + 2 * i, f"sig{i}", [P, E], F32) for i in range(TILES)]
@@ -256,88 +258,86 @@ def tile_list_ring_leak_blend_kernel(
             gather_up(i)
             sigmoid(2 * (i - PACK))
             sigmoid(2 * (i - PACK) + 1)
+        gather_own(at(80, "own_first", [P, E], F32)[:])
         second_group(6)
         gather_up(6)
-        own_pair = at(80, "own_pair", [P, 2, E], F32)
+        own_pair = at(82, "own_pair", [P, 2, E], F32)
         for k in range(2):
             gather_own(own_pair[:, k, :])
         for i in range(PACK):
             apply_gain(i)
         second_group(7)
         gather_up(7)
-        gather_own(at(84, "own2", [P, E], F32)[:])
+        own_next = at(86, "own_next", [P, 2, E], F32)
+        for k in range(2):
+            gather_own(own_next[:, k, :])
         for pair in ((4, 5), (6, 7)):
             for i in pair:
                 sigmoid(i)
             for i in pair:
                 apply_gain(i)
 
-        rows_of = [x_rows[b][:].rearrange("p (t m) -> p m t", t=PACK) for b in range(GROUPS)]
-        x_bf0 = at(33, "x_bf0", [P, E * PACK], BF16)
-        nc.gpsimd.tensor_scalar(x_bf0[:].rearrange("p (m t) -> p m t", t=PACK), rows_of[0], 1.0, 0.0, MULT, ADD)
-
         w2_sc, w2_w = {}, {}
         x_sc = [held(f"x_sc{b}", [P, E], U8) for b in range(GROUPS)]
         x_w = [held("x_w0", [P, E], U32)]
 
-        def quantise_w2(kb, src, b, c, tiles):
-            words = at(kb, f"w2_w{b}{c}{tiles[0]}", [P, P * len(tiles)], U32)
-            scales = held(f"w2_sc{b}{c}{tiles[0]}", [P, P * len(tiles)], U8)
-            nc.vector.quantize_mx(out=words[:].bitcast(FP8X4), scales=scales[:], in_=src[:])
-            for k, t in enumerate(tiles):
-                w2_w[b, c, t] = words[:, P * k : P * (k + 1)]
-                w2_sc[b, c, t] = scales[:, P * k : P * (k + 1)]
+        def quantise_w2(kb, b, c):
+            words = at(kb, f"w2_w{b}{c}", [P, KP], U32)
+            scales = held(f"w2_sc{b}{c}", [P, KP], U8)
+            nc.vector.quantize_mx(out=words[:].bitcast(FP8X4), scales=scales[:], in_=w2_bf[b, c][:])
+            for t in range(PACK):
+                w2_w[b, c, t] = words[:, P * t : P * (t + 1)]
+                w2_sc[b, c, t] = scales[:, P * t : P * (t + 1)]
 
-        quantise_w2(90, w2_bf[0, 0], 0, 0, range(PACK))
+        rows_of = [x_rows[b][:].rearrange("p (t m) -> p m t", t=PACK) for b in range(GROUPS)]
+        x_bf0 = at(44, "x_bf0", [P, E * PACK], BF16)
+        nc.gpsimd.tensor_scalar(x_bf0[:].rearrange("p (m t) -> p m t", t=PACK), rows_of[0], 1.0, 0.0, MULT, ADD)
+        quantise_w2(91, 0, 0)
         nc.vector.quantize_mx(out=x_w[0][:].bitcast(FP8X4), scales=x_sc[0][:], in_=x_bf0[:])
-        quantise_w2(92, w2_bf[1, 0], 1, 0, range(PACK))
-        quantise_w2(94, w2_bf[0, 1], 0, 1, range(PACK))
-        quantise_w2(2, last_bf[0], 1, 1, range(2))
-        gather_own(at(0, "own3", [P, E], F32)[:])
-        last_bf.append(at(12, "last_bf1", [P, 2 * KP], BF16))
-        round_w2(last_bf[1], 1, 1, slice(2, PACK))
+        quantise_w2(93, 1, 0)
 
         x_bf1 = [at(164 + 2 * k, f"x_bf1{k}", [P, E // 2 * PACK], BF16) for k in range(2)]
         parts = (slice(0, E // 2), slice(E // 2, E))
-        x_w.append(at(33, "x_w1", [P, E], U32))
+        x_w.append(at(44, "x_w1", [P, E], U32))
         for k in range(2):
             nc.scalar.copy(x_bf1[k][:].rearrange("p (m t) -> p m t", t=PACK), rows_of[1][:, parts[k]])
         for k in range(2):
             nc.vector.quantize_mx(out=x_w[1][:, parts[k]].bitcast(FP8X4), scales=x_sc[1][:, parts[k]], in_=x_bf1[k][:])
-        quantise_w2(164, last_bf[1], 1, 1, range(2, PACK))
+        quantise_w2(164, 0, 1)
+        quantise_w2(166, 1, 1)
 
         banks = [bank_tile(k) for k in range(TILES)]
-        for b in range(GROUPS):
-            for i in range(TILES):
-                c, t = divmod(i, PACK)
-                nc.tensor.matmul_mx(
-                    out=banks[i][:],
-                    lhsT=w2_w[b, c, t].bitcast(FP8X4),
-                    lhsT_scale=w2_sc[b, c, t],
-                    rhs=x_w[b][:].bitcast(FP8X4),
-                    rhs_scale=x_sc[b][:],
-                    start=(b == 0),
-                    stop=(b == GROUPS - 1),
-                )
+        order = [(i, b, b == 0) for b in range(GROUPS) for i in range(AHEAD)] + [(i, b, b == 1) for i in (3, 5, 4, 6, 7) for b in (1, 0)]
+        for i, b, opens in order:
+            c, t = divmod(i, PACK)
+            nc.tensor.matmul_mx(
+                out=banks[i][:],
+                lhsT=w2_w[b, c, t].bitcast(FP8X4),
+                lhsT_scale=w2_sc[b, c, t],
+                rhs=x_w[b][:].bitcast(FP8X4),
+                rhs_scale=x_sc[b][:],
+                start=opens,
+                stop=not opens,
+            )
 
         rows = out.rearrange("(c v t e) m -> c t v e m", v=PAIRS, t=PACK, e=2)
         for i in range(TILES):
             c, t = divmod(i, PACK)
             factor = blend_t[:, c, 2 * t : 2 * t + 1]
-            if 0 < i < PLAIN:
+            if i < PLAIN and i != SUMMED:
                 res = at(172 + 2 * i, f"res{i}", [P, E], F32)
                 nc.vector.scalar_tensor_tensor(res[:], banks[i][:], factor, own[i], MULT, ADD)
                 nc.sync.dma_start(rows[c, t], res[:])
                 continue
             share = at(188 + 2 * max(0, i - PLAIN + 1), f"share{i}", [P, E], F32)
             nc.scalar.activation(share[:], banks[i][:], COPY, scale=factor)
-            if i == 0:
-                res = at(12, "res0", [P, E], F32)
+            if i == SUMMED:
+                res = at(12, "summed", [P, E], F32)
                 nc.gpsimd.tensor_tensor(res[:], own[i], share[:], ADD)
                 nc.gpsimd.dma_start(rows[c, t], res[:])
                 continue
             res = at(172 + 2 * i, f"res{i}", [P, E], F32)
-            for cols in (slice(0, E // 2), slice(E // 2, E)) if i == TILES - 1 else (slice(0, E),):
+            for cols in (slice(0, E // 2), slice(E // 2, 3 * E // 4), slice(3 * E // 4, E)) if i == TILES - 1 else (slice(0, E),):
                 picks = pos2_t[:, cols.start // 16 : cols.stop // 16]
                 nc.vector.tensor_tensor(res[:, cols], h[i][:].indirect(picks), share[:, cols], ADD)
                 nc.sync.dma_start(rows[c, t][:, :, cols], res[:, cols])

@@ -31,7 +31,7 @@ RUN = 2 * PACK
 PAIRS = P // 2
 KB = 1024
 PLAIN = 5
-AHEAD = 3
+AHEAD = 5
 SUMMED = 1
 SLOT = S + KP
 FIRST_PIECE = 5 * T // 16
@@ -141,14 +141,14 @@ def tile_list_ring_leak_blend_kernel(
 
         w4_w = {}
 
-        def order_words(dst, src, b, passes):
+        def order_words(dst, src, b, passes, tiles=range(PACK)):
             nc.vector.tensor_copy(
-                dst[:].rearrange("p (t c i) -> p c t i", t=PACK, i=4),
-                src[:].rearrange("p (c i t) -> p c t i", t=PACK, i=4),
+                dst[:].rearrange("p (t c i) -> p c t i", t=len(tiles), i=4),
+                src[:].rearrange("p (c i t) -> p c t i", t=PACK, i=4)[:, :, tiles.start : tiles.stop],
             )
-            for t in range(PACK):
+            for t in tiles:
                 for k, a in enumerate(passes):
-                    first_word = PAIRS * (len(passes) * t + k)
+                    first_word = PAIRS * (len(passes) * (t - tiles.start) + k)
                     w4_w[PACK * b + t, a] = dst[:, first_word : first_word + PAIRS].bitcast(U8)
 
         order_words(held("w4_w0", [P, PACK * PAIRS], I32), w4_first, 0, range(1))
@@ -167,15 +167,13 @@ def tile_list_ring_leak_blend_kernel(
         keep_all = held("keep_all", [P, TILES], F32)
         nc.scalar.activation(keep_all[:].rearrange("p (b t) -> p b t", b=GROUPS), blend_t[:, :, 0 : RUN - 1 : 2], COPY, scale=-1.0, bias=1.0)
         gate = {}
-        for i, kb in ((5, 80), (6, 82), (7, 86)):
-            gate[i] = at(kb, f"keep_gate{i}", [P, 1], F32)
-            nc.scalar.activation(gate[i][:, 0:1], blend_t[:, i // PACK, 2 * (i % PACK) : 2 * (i % PACK) + 1], COPY, scale=-1.0, bias=1.0)
+        for (i, s), kb in (((0, 1), 104), ((1, 1), 108), ((4, 1), 80), ((6, 1), 82), ((7, 1), 86)):
+            gate[i, s] = at(kb, f"keep_gate{i}", [P, 1], F32)
+            nc.scalar.activation(gate[i, s][:, 0:1], blend_t[:, i // PACK, 2 * (i % PACK) : 2 * (i % PACK) + 1], COPY, scale=-1.0, bias=1.0)
 
         for a in range(1, PASSES1):
             gather_words(a)
         order_words(at(52 - 1 / 16, "w4_w2", [P, PASSES1 * PACK * PAIRS], I32), w4_second, 1, range(PASSES1))
-        undo_t = at(61, "undo_t", [P, TILES], F32)
-        nc.vector.reciprocal(undo_t[:], keep_all[:])
 
         pieces = [(b, c, slice(0, PAIRS)) for c in range(GROUPS) for b in range(GROUPS)]
         w2_raw = []
@@ -203,20 +201,19 @@ def tile_list_ring_leak_blend_kernel(
         h = [at(96 + 4 * i, f"h{i}", [P, S], F32) for i in range(TILES)]
 
         def empty(bank, i, s):
-            factor = gate[i][:, 0:1] if s == 1 and i in gate else keep_all[:, i : i + 1]
-            if (i, s) == (0, 1):
-                nc.vector.tensor_scalar_mul(h[i][:, s * BANK : (s + 1) * BANK], bank[:], factor)
-            else:
-                nc.scalar.activation(h[i][:, s * BANK : (s + 1) * BANK], bank[:], COPY, scale=factor)
+            factor = gate[i, s][:, 0:1] if (i, s) in gate else keep_all[:, i : i + 1]
+            nc.scalar.activation(h[i][:, s * BANK : (s + 1) * BANK], bank[:], COPY, scale=factor)
 
         first = {(i, s): bank_tile(PACK * s + i) for s in range(HALVES) for i in range(PACK)}
         for a in range(PASSES1):
             for s in range(HALVES):
                 for i in range(PACK):
                     pass1(first[i, s], i, s, a)
-        emptied = [(0, 0), (1, 0), (2, 0), (0, 1), (1, 1), (2, 1), (3, 0), (3, 1)]
+        emptied = [(0, 0), (1, 0), (0, 1), (1, 1), (2, 0), (2, 1), (3, 0), (3, 1)]
         for i, s in emptied:
             empty(first[i, s], i, s)
+        undo_t = at(61, "undo_t", [P, TILES], F32)
+        nc.vector.reciprocal(undo_t[:], keep_all[:])
 
         def second_group(i):
             for s in range(HALVES):
@@ -256,9 +253,10 @@ def tile_list_ring_leak_blend_kernel(
         for i in (4, 5):
             second_group(i)
             gather_up(i)
+            if i == PACK:
+                gather_own(at(80, "own_first", [P, E], F32)[:])
             sigmoid(2 * (i - PACK))
             sigmoid(2 * (i - PACK) + 1)
-        gather_own(at(80, "own_first", [P, E], F32)[:])
         second_group(6)
         gather_up(6)
         own_pair = at(82, "own_pair", [P, 2, E], F32)
@@ -281,20 +279,22 @@ def tile_list_ring_leak_blend_kernel(
         x_sc = [held(f"x_sc{b}", [P, E], U8) for b in range(GROUPS)]
         x_w = [held("x_w0", [P, E], U32)]
 
-        def quantise_w2(kb, b, c):
-            words = at(kb, f"w2_w{b}{c}", [P, KP], U32)
-            scales = held(f"w2_sc{b}{c}", [P, KP], U8)
-            nc.vector.quantize_mx(out=words[:].bitcast(FP8X4), scales=scales[:], in_=w2_bf[b, c][:])
-            for t in range(PACK):
-                w2_w[b, c, t] = words[:, P * t : P * (t + 1)]
-                w2_sc[b, c, t] = scales[:, P * t : P * (t + 1)]
+        def quantise_w2(kb, b, c, tiles=range(PACK)):
+            words = at(kb, f"w2_w{b}{c}{tiles.start}", [P, P * len(tiles)], U32)
+            scales = held(f"w2_sc{b}{c}{tiles.start}", [P, P * len(tiles)], U8)
+            nc.vector.quantize_mx(out=words[:].bitcast(FP8X4), scales=scales[:], in_=w2_bf[b, c][:, KP * tiles.start : KP * tiles.stop])
+            for k, t in enumerate(tiles):
+                w2_w[b, c, t] = words[:, P * k : P * (k + 1)]
+                w2_sc[b, c, t] = scales[:, P * k : P * (k + 1)]
 
         rows_of = [x_rows[b][:].rearrange("p (t m) -> p m t", t=PACK) for b in range(GROUPS)]
         x_bf0 = at(44, "x_bf0", [P, E * PACK], BF16)
         nc.gpsimd.tensor_scalar(x_bf0[:].rearrange("p (m t) -> p m t", t=PACK), rows_of[0], 1.0, 0.0, MULT, ADD)
-        quantise_w2(91, 0, 0)
+        quantise_w2(91, 0, 0, range(1))
         nc.vector.quantize_mx(out=x_w[0][:].bitcast(FP8X4), scales=x_sc[0][:], in_=x_bf0[:])
+        quantise_w2(91.5, 0, 0, range(1, PACK))
         quantise_w2(93, 1, 0)
+        quantise_w2(0, 0, 1)
 
         x_bf1 = [at(164 + 2 * k, f"x_bf1{k}", [P, E // 2 * PACK], BF16) for k in range(2)]
         parts = (slice(0, E // 2), slice(E // 2, E))
@@ -303,11 +303,11 @@ def tile_list_ring_leak_blend_kernel(
             nc.scalar.copy(x_bf1[k][:].rearrange("p (m t) -> p m t", t=PACK), rows_of[1][:, parts[k]])
         for k in range(2):
             nc.vector.quantize_mx(out=x_w[1][:, parts[k]].bitcast(FP8X4), scales=x_sc[1][:, parts[k]], in_=x_bf1[k][:])
-        quantise_w2(164, 0, 1)
-        quantise_w2(166, 1, 1)
+        quantise_w2(164, 1, 1)
 
         banks = [bank_tile(k) for k in range(TILES)]
-        order = [(i, b, b == 0) for b in range(GROUPS) for i in range(AHEAD)] + [(i, b, b == 1) for i in (3, 5, 4, 6, 7) for b in (1, 0)]
+        turn = (0, 1, 2, 3, 5, 4, 6, 7)
+        order = [(i, b, b == 0) for b in range(GROUPS) for i in turn[:AHEAD]] + [(i, b, b == 1) for i in turn[AHEAD:] for b in (1, 0)]
         for i, b, opens in order:
             c, t = divmod(i, PACK)
             nc.tensor.matmul_mx(

from contextlib import ExitStack

import concourse.mybir as mybir

K, T, S, E, H = 1536, 4096, 1024, 512, 1024
FLOPS = 2 * K * H * S + 2 * H * H * E

F32 = mybir.dt.float32
BF16 = mybir.dt.bfloat16
I32 = mybir.dt.int32
U32 = mybir.dt.uint32
U16 = mybir.dt.uint16
U8 = mybir.dt.uint8
FP8X4 = mybir.dt.float8_e4m3fn_x4
FP4X4 = mybir.dt.float4_e2m1fn_x4
MULT = mybir.AluOpType.mult
ADD = mybir.AluOpType.add
COPY = mybir.ActivationFunctionType.Copy
SIGMOID = mybir.ActivationFunctionType.Sigmoid

P = 128
PACK = 4
KP = P * PACK
PASSES1 = K // KP
GROUPS = H // KP
TILES = GROUPS * PACK
BANK = 512
HALVES = S // BANK
QUADS = 4
RUN = 2 * PACK
PAIRS = P // 2
KB = 1024
PLAIN = 5
AHEAD = 5
SUMMED = 1
SLOT = S + KP
FIRST_PIECE = 5 * T // 16


def tile_list_ring_leak_blend_kernel(
    tc, tab_words, tab_scales, w4_words, w4_scales, w2, gain, blend, offs, pos1, pos2, out
):
    nc = tc.nc
    with ExitStack() as ctx:
        lists = ctx.enter_context(tc.tile_pool(name="lists", bufs=1))
        keep = ctx.enter_context(tc.tile_pool(name="keep", bufs=1))
        laid = ctx.enter_context(tc.tile_pool(name="laid", bufs=1))
        psum = ctx.enter_context(tc.psum_pool(name="psum", bufs=1))

        def held(name, shape, dtype):
            return keep.tile(shape, dtype, name=name, align_bytes=64)

        def at(kb, name, shape, dtype):
            return laid.tile(shape, dtype, name=name, offset=int(kb * KB), align_bytes=64)

        def bank_tile(k):
            return psum.tile([P, BANK], F32, name=f"bank{k}")

        offs_t = lists.tile([P, S // 16], U16, name="offs_t")
        pos1_t = lists.tile([P, E // 16], U16, name="pos1_t")
        pos2_t = lists.tile([P, E // 16], U16, name="pos2_t")

        tab_sc = [held("tab_sc0", [P, T // 4], I32), at(56, "tab_sc1", [P, T // 4], I32)]
        early_sc = held("early_sc", [P, 2 * KP // 4], I32)
        late_sc = at(60, "late_sc", [P, 4 * KP // 4], I32)
        early_planes = held("early_planes", [P, 2 * SLOT // 4], I32)
        late_planes = held("late_planes", [P, 2 * SLOT // 4], I32)
        for tile in (early_sc, tab_sc[0]):
            nc.vector.memset(tile[:, 0:1], 0)
            nc.vector.memset(tile[:, 1:], 0)
        nc.gpsimd.memset(tab_sc[1][:], 0)
        for tile in (late_sc, early_planes, late_planes):
            nc.vector.memset(tile[:], 0)
        warm_in = held("warm_in", [P, 1], F32)
        warm_out = held("warm_out", [P, 1], F32)
        nc.vector.memset(warm_in[:], 0.0)
        nc.scalar.activation(warm_out[:], warm_in[:], SIGMOID)

        tab_w = [at(16 * a, f"tab_w{a}", [P, T], I32) for a in range(PASSES1 - 1)]

        def load_w4(kb, b, passes):
            raw = at(kb, f"w4_raw{b}{passes.start}", [P, (passes.stop - passes.start) * KP // 2], I32)
            nc.sync.dma_start(
                raw[:].rearrange("p (a c) -> p a c", c=KP // 2),
                w4_words.bitcast(I32)[passes, :, b * KP // 2 : (b + 1) * KP // 2].rearrange("a p c -> p a c"),
            )
            return raw

        def load_factors(tile, factors):
            runs = factors.rearrange("(b v k) -> v b k", b=GROUPS, k=RUN)
            for e in range(2):
                nc.sync.dma_start(tile[e:P:2, :, 0 : RUN - 1], runs[:, :, e : e + RUN - 1])

        def load_table(a, cols):
            nc.sync.dma_start(tab_w[a][:, cols], tab_words[a].rearrange("p t i -> p (t i)").bitcast(I32)[:, cols])

        def move_rows(planes, rows, first_row):
            for r in range(QUADS):
                nc.sync.dma_start(planes[r:P:32, :], rows[first_row + 8 * r : P : 32, :])

        def order_scales(dst, src):
            nc.vector.tensor_copy(
                dst.bitcast(U16).rearrange("p g (t v) -> p g t v", t=PACK),
                src[:].bitcast(U16).rearrange("p (g v t) -> p g t v", t=PACK, v=PAIRS),
            )

        nc.sync.dma_start(offs_t[:], offs)
        nc.sync.dma_start(pos1_t[:], pos1)
        load_table(0, slice(0, FIRST_PIECE))
        nc.sync.dma_start(pos2_t[:], pos2)
        w4_sc_rows = w4_scales.bitcast(I32).rearrange("a j c -> j a c")
        nc.sync.dma_start(early_sc[5:P:8].rearrange("j (a c) -> j a c", a=2), w4_sc_rows[:, 0:2, 0 : KP // 4])
        for a, tile, first_row in ((0, tab_sc[0], 5), (2, tab_sc[0], 6), (1, tab_sc[1], 5)):
            nc.sync.dma_start(tile[first_row:P:8, :], tab_scales.bitcast(I32)[a])
        load_table(0, slice(FIRST_PIECE, T))
        nc.sync.dma_start(late_sc[6:P:8, 0 : H // 4], w4_sc_rows[:, 2])
        nc.sync.dma_start(late_sc[6:P:8, H // 4 :].rearrange("j (a c) -> j a c", a=2), w4_sc_rows[:, 0:2, KP // 4 :])
        w4_first = load_w4(64, 0, slice(0, 1))
        load_table(1, slice(0, T))

        early_rows = held("early_rows", [P, 2 * SLOT // 4], I32)
        early_slots = early_rows[:].rearrange("p (a c) -> p a c", a=2)
        order_scales(early_slots[:, :, S // 4 :], early_sc)
        picked = [held("picked0", [P, S // 4], I32), at(35.25, "picked1", [P, S // 4], I32)]
        for a in range(2):
            nc.vector.tensor_copy(picked[a][:].bitcast(U8), tab_sc[a][:].bitcast(U8).indirect(offs_t[:]))
            nc.vector.tensor_copy(early_slots[:, a, 0 : S // 4], picked[a][:])
        move_rows(early_planes, early_rows, 5)
        w4_rest = load_w4(56, 0, slice(1, PASSES1))
        tab_w.append(at(36, "tab_w2", [P, T], I32))
        load_table(2, slice(0, T))
        blend_t = at(35.5, "blend_t", [P, GROUPS, RUN], F32)
        load_factors(blend_t, blend)

        v_w = [[at(55 + 2 * s if a == 2 else 68 + 2 * (HALVES * a + s), f"v_w{a}{s}", [P, BANK], U32) for s in range(HALVES)] for a in range(PASSES1)]

        def gather_words(a):
            for s in range(HALVES):
                cols = slice(s * BANK // 16, (s + 1) * BANK // 16)
                nc.vector.tensor_copy(v_w[a][s][:], tab_w[a][:].bitcast(U32).indirect(offs_t[:, cols]))

        w4_w = {}

        def order_words(dst, src, b, passes, tiles=range(PACK)):
            nc.vector.tensor_copy(
                dst[:].rearrange("p (t c i) -> p c t i", t=len(tiles), i=4),
                src[:].rearrange("p (c i t) -> p c t i", t=PACK, i=4)[:, :, tiles.start : tiles.stop],
            )
            for t in tiles:
                for k, a in enumerate(passes):
                    first_word = PAIRS * (len(passes) * (t - tiles.start) + k)
                    w4_w[PACK * b + t, a] = dst[:, first_word : first_word + PAIRS].bitcast(U8)

        order_words(held("w4_w0", [P, PACK * PAIRS], I32), w4_first, 0, range(1))
        gather_words(0)
        late_rows = at(64, "late_rows", [P, 2 * SLOT // 4], I32)
        nc.vector.tensor_copy(late_rows[:, 0 : S // 4], picked[0][:])
        order_scales(late_rows[:, S // 4 :].rearrange("p (g c) -> p g c", g=4), late_sc)
        move_rows(late_planes, late_rows, 6)
        early_bytes, late_bytes = early_planes[:].bitcast(U8), late_planes[:].bitcast(U8)
        v_planes = [early_bytes[:, 0:S], early_bytes[:, SLOT : SLOT + S], late_bytes[:, 0:S]]
        late_w4 = [late_bytes[:, S + KP * g : S + KP * (g + 1)] for g in range(4)]
        w4_planes = [[early_bytes[:, S:SLOT], early_bytes[:, SLOT + S :], late_w4[0]], [late_w4[2], late_w4[3], late_w4[1]]]
        w4_second = load_w4(60, 1, slice(0, PASSES1))
        order_words(held("w4_w1", [P, 2 * PACK * PAIRS], I32), w4_rest, 0, range(1, PASSES1))

        keep_all = held("keep_all", [P, TILES], F32)
        nc.scalar.activation(keep_all[:].rearrange("p (b t) -> p b t", b=GROUPS), blend_t[:, :, 0 : RUN - 1 : 2], COPY, scale=-1.0, bias=1.0)
        gate = {}
        for (i, s), kb in (((0, 1), 104), ((1, 1), 108), ((4, 1), 80), ((6, 1), 82), ((7, 1), 86)):
            gate[i, s] = at(kb, f"keep_gate{i}", [P, 1], F32)
            nc.scalar.activation(gate[i, s][:, 0:1], blend_t[:, i // PACK, 2 * (i % PACK) : 2 * (i % PACK) + 1], COPY, scale=-1.0, bias=1.0)

        for a in range(1, PASSES1):
            gather_words(a)
        order_words(at(52 - 1 / 16, "w4_w2", [P, PASSES1 * PACK * PAIRS], I32), w4_second, 1, range(PASSES1))

        pieces = [(b, c, slice(0, PAIRS)) for c in range(GROUPS) for b in range(GROUPS)]
        w2_raw = []
        gain_t = at(24, "gain_t", [P, GROUPS, RUN], F32)
        for k, (b, c, vs) in enumerate(pieces):
            cols = slice(c * KP + RUN * vs.start, c * KP + RUN * vs.stop)
            w2_raw.append(at((16, 24 + 1 / 16, 35.625, 43.625)[k], f"w2_raw{k}", [P, PACK, cols.stop - cols.start], F32))
            block = w2[b * KP : (b + 1) * KP, cols].rearrange("(v j e) n -> e v j n", j=PACK, e=2)
            for e in range(2):
                nc.sync.dma_start(w2_raw[k][e:P:2], block[e])
            if k == 0:
                load_factors(gain_t, gain)

        def pass1(bank, i, s, a):
            nc.tensor.matmul_mx(
                out=bank[:],
                lhsT=w4_w[i, a].bitcast(FP4X4),
                lhsT_scale=w4_planes[i // PACK][a][:, P * (i % PACK) : P * (i % PACK + 1)],
                rhs=v_w[a][s][:].bitcast(FP8X4),
                rhs_scale=v_planes[a][:, s * BANK : (s + 1) * BANK],
                start=(a == 0),
                stop=(a == PASSES1 - 1),
            )

        h = [at(96 + 4 * i, f"h{i}", [P, S], F32) for i in range(TILES)]

        def empty(bank, i, s):
            factor = gate[i, s][:, 0:1] if (i, s) in gate else keep_all[:, i : i + 1]
            nc.scalar.activation(h[i][:, s * BANK : (s + 1) * BANK], bank[:], COPY, scale=factor)

        first = {(i, s): bank_tile(PACK * s + i) for s in range(HALVES) for i in range(PACK)}
        for a in range(PASSES1):
            for s in range(HALVES):
                for i in range(PACK):
                    pass1(first[i, s], i, s, a)
        emptied = [(0, 0), (1, 0), (0, 1), (1, 1), (2, 0), (2, 1), (3, 0), (3, 1)]
        for i, s in emptied:
            empty(first[i, s], i, s)
        undo_t = at(61, "undo_t", [P, TILES], F32)
        nc.vector.reciprocal(undo_t[:], keep_all[:])

        def second_group(i):
            for s in range(HALVES):
                was_i, was_s = emptied[HALVES * (i - PACK) + s]
                bank = bank_tile(PACK * was_s + was_i)
                for a in range(PASSES1):
                    pass1(bank, i, s, a)
                empty(bank, i, s)

        w2_bf = {(b, c): at(4 * (GROUPS * c + b), f"w2_bf{b}{c}", [P, PACK * KP], BF16) for c in range(GROUPS) for b in range(GROUPS)}
        for k, (b, c, vs) in enumerate(pieces):
            rounded = w2_bf[b, c][:].rearrange("p (t v e j) -> p v t e j", v=PAIRS, e=2, j=PACK)
            raw = w2_raw[k][:].rearrange("p j (v t e) -> p v t e j", t=PACK, e=2)
            nc.gpsimd.tensor_scalar(rounded[:, vs], raw, 1.0, 0.0, MULT, ADD)

        up = [at(128 + 2 * i, f"up{i}", [P, E], F32) for i in range(TILES)]
        sig = [at(144 + 2 * i, f"sig{i}", [P, E], F32) for i in range(TILES)]
        x_rows = [at((91, 160)[b], f"x_rows{b}", [P, PACK * E], BF16) for b in range(GROUPS)]
        own = []

        def gather_up(i):
            nc.vector.tensor_copy(up[i][:], h[i][:].indirect(pos1_t[:]))

        def gather_own(dst):
            nc.vector.tensor_copy(dst, h[len(own)][:].indirect(pos2_t[:]))
            own.append(dst)

        def sigmoid(i):
            nc.scalar.activation(sig[i][:], up[i][:], SIGMOID, scale=undo_t[:, i : i + 1])

        def apply_gain(i):
            b, t = divmod(i, PACK)
            nc.scalar.activation(x_rows[b][:, t * E : (t + 1) * E], sig[i][:], COPY, scale=gain_t[:, b, 2 * t : 2 * t + 1])

        for i in range(PACK):
            gather_up(i)
        for i in (4, 5):
            second_group(i)
            gather_up(i)
            if i == PACK:
                gather_own(at(80, "own_first", [P, E], F32)[:])
            sigmoid(2 * (i - PACK))
            sigmoid(2 * (i - PACK) + 1)
        second_group(6)
        gather_up(6)
        own_pair = at(82, "own_pair", [P, 2, E], F32)
        for k in range(2):
            gather_own(own_pair[:, k, :])
        for i in range(PACK):
            apply_gain(i)
        second_group(7)
        gather_up(7)
        own_next = at(86, "own_next", [P, 2, E], F32)
        for k in range(2):
            gather_own(own_next[:, k, :])
        for pair in ((4, 5), (6, 7)):
            for i in pair:
                sigmoid(i)
            for i in pair:
                apply_gain(i)

        w2_sc, w2_w = {}, {}
        x_sc = [held(f"x_sc{b}", [P, E], U8) for b in range(GROUPS)]
        x_w = [held("x_w0", [P, E], U32)]

        def quantise_w2(kb, b, c, tiles=range(PACK)):
            words = at(kb, f"w2_w{b}{c}{tiles.start}", [P, P * len(tiles)], U32)
            scales = held(f"w2_sc{b}{c}{tiles.start}", [P, P * len(tiles)], U8)
            nc.vector.quantize_mx(out=words[:].bitcast(FP8X4), scales=scales[:], in_=w2_bf[b, c][:, KP * tiles.start : KP * tiles.stop])
            for k, t in enumerate(tiles):
                w2_w[b, c, t] = words[:, P * k : P * (k + 1)]
                w2_sc[b, c, t] = scales[:, P * k : P * (k + 1)]

        rows_of = [x_rows[b][:].rearrange("p (t m) -> p m t", t=PACK) for b in range(GROUPS)]
        x_bf0 = at(44, "x_bf0", [P, E * PACK], BF16)
        nc.gpsimd.tensor_scalar(x_bf0[:].rearrange("p (m t) -> p m t", t=PACK), rows_of[0], 1.0, 0.0, MULT, ADD)
        quantise_w2(91, 0, 0, range(1))
        nc.vector.quantize_mx(out=x_w[0][:].bitcast(FP8X4), scales=x_sc[0][:], in_=x_bf0[:])
        quantise_w2(91.5, 0, 0, range(1, PACK))
        quantise_w2(93, 1, 0)
        quantise_w2(0, 0, 1)

        x_bf1 = [at(164 + 2 * k, f"x_bf1{k}", [P, E // 2 * PACK], BF16) for k in range(2)]
        parts = (slice(0, E // 2), slice(E // 2, E))
        x_w.append(at(44, "x_w1", [P, E], U32))
        for k in range(2):
            nc.scalar.copy(x_bf1[k][:].rearrange("p (m t) -> p m t", t=PACK), rows_of[1][:, parts[k]])
        for k in range(2):
            nc.vector.quantize_mx(out=x_w[1][:, parts[k]].bitcast(FP8X4), scales=x_sc[1][:, parts[k]], in_=x_bf1[k][:])
        quantise_w2(164, 1, 1)

        banks = [bank_tile(k) for k in range(TILES)]
        turn = (0, 1, 2, 3, 5, 4, 6, 7)
        order = [(i, b, b == 0) for b in range(GROUPS) for i in turn[:AHEAD]] + [(i, b, b == 1) for i in turn[AHEAD:] for b in (1, 0)]
        for i, b, opens in order:
            c, t = divmod(i, PACK)
            nc.tensor.matmul_mx(
                out=banks[i][:],
                lhsT=w2_w[b, c, t].bitcast(FP8X4),
                lhsT_scale=w2_sc[b, c, t],
                rhs=x_w[b][:].bitcast(FP8X4),
                rhs_scale=x_sc[b][:],
                start=opens,
                stop=not opens,
            )

        rows = out.rearrange("(c v t e) m -> c t v e m", v=PAIRS, t=PACK, e=2)
        for i in range(TILES):
            c, t = divmod(i, PACK)
            factor = blend_t[:, c, 2 * t : 2 * t + 1]
            if i < PLAIN and i != SUMMED:
                res = at(172 + 2 * i, f"res{i}", [P, E], F32)
                nc.vector.scalar_tensor_tensor(res[:], banks[i][:], factor, own[i], MULT, ADD)
                nc.sync.dma_start(rows[c, t], res[:])
                continue
            share = at(188 + 2 * max(0, i - PLAIN + 1), f"share{i}", [P, E], F32)
            nc.scalar.activation(share[:], banks[i][:], COPY, scale=factor)
            if i == SUMMED:
                res = at(12, "summed", [P, E], F32)
                nc.gpsimd.tensor_tensor(res[:], own[i], share[:], ADD)
                nc.gpsimd.dma_start(rows[c, t], res[:])
                continue
            res = at(172 + 2 * i, f"res{i}", [P, E], F32)
            for cols in (slice(0, E // 2), slice(E // 2, 3 * E // 4), slice(3 * E // 4, E)) if i == TILES - 1 else (slice(0, E),):
                picks = pos2_t[:, cols.start // 16 : cols.stop // 16]
                nc.vector.tensor_tensor(res[:, cols], h[i][:].indirect(picks), share[:, cols], ADD)
                nc.sync.dma_start(rows[c, t][:, :, cols], res[:, cols])
